import numpy as np, ml_dtypes
CORES = [6,15,38,47]
N = 4
BF = ml_dtypes.bfloat16
def gentries(a):
    return np.ascontiguousarray(a.reshape(8, 16, -1).transpose(0, 2, 1)).reshape(8, -1)
def gtable(e):
    e = np.asarray(e); return np.ascontiguousarray(e.reshape(8, -1, 16).transpose(0, 2, 1)).reshape(128, -1).astype(np.int32)
W, L, HS = 3584, 256, 1024
HOP = (1, 0, 2, 0)
HB = W // 12
def above(rng, hub, c, fill=None):
    M = c.shape[2]; s = (N, 8, 16, M); c = c[:, :, None, :]
    k = np.stack([np.stack([np.searchsorted(hub[r, g], c[r, g, 0], side="right") for g in range(8)]) for r in range(N)])[:, :, None, :] + rng.integers(0, 24, s)
    e1 = np.where(k < HB, np.take_along_axis(hub[:, :, None, :], np.minimum(k, HB - 1), 3), 0)
    e2 = np.where(c < W - 1, np.minimum(c + 1 + ((W - 1 - c) * rng.random(s) ** 2).astype(np.int64), W - 1), 0)
    e = np.where(rng.random(s) < 0.6, e1, e2)
    e = np.where(rng.random(s) < 0.03, ((c + 1) * rng.random(s)).astype(np.int64), e)
    if fill is None: fill = rng.choice(np.array([0.0, 0.25, 0.5, 0.75, 1.0]), (N, 8, 1, M))
    return np.where(rng.random(s) < fill, e, 0)
def parts(rng):
    hub = np.sort(np.argsort(rng.random((N, 8, W - 1)), axis=-1)[..., :HB] + 1, axis=-1)
    d = rng.integers(0, 256, (N, 8, 16, W)); v = rng.integers(0, 256, (N, 8, 16, L))
    w = rng.integers(1, 256, (N, 8, 16)); a = rng.integers(30, 91, (N, 8, 16))
    p = above(rng, hub, np.broadcast_to(np.arange(W), (N, 8, W)))
    j = np.where(rng.random((N, 8, L)) < 0.5, (W * rng.random((N, 8, L)) ** 1.5).astype(np.int64), np.take_along_axis(hub, rng.integers(0, HB // 2, (N, 8, L)), 2))
    q = above(rng, hub, j)
    pj = np.take_along_axis(p, j[:, :, None, :], 3)
    q = np.where(rng.random(q.shape) < 0.25, np.roll(pj, 1, axis=2), q)
    return d, p, j, q, v, w, a, hub
def pack(d, p, j, q, v, w, a):
    return {"d0": d.reshape(N, 128, W).astype(np.float32).astype(BF), "p0": np.ascontiguousarray(p.reshape(N, 128, W)).astype(np.int32), "j0": np.stack([gtable(x) for x in j]),
            "q0": np.ascontiguousarray(q.reshape(N, 128, L)).astype(np.int32), "v0": v.reshape(N, 128, L).astype(np.float32).astype(BF), "wa": np.ascontiguousarray(np.stack([w, a], axis=-1).reshape(N, 128, 2)).astype(np.int32)}
def setup_inputs(rng):
    d, p, j, q, v, w, a, hub = parts(rng)
    return pack(d, p, j, q, v, w, a)
def setup_inputs_edge(rng):
    d, p, j, q, v, w, a, hub = parts(rng)
    v = rng.integers(96, 160, (N, 8, 16, 1)); a = rng.integers(1, 91, (N, 8, 16))
    near = (np.argsort(rng.random((N, 8, 16, W)), axis=2) < rng.integers(7, 11, (N, 8, 1, W))).astype(np.int64)
    d = v + (2 * rng.integers(0, 2, (N, 8, 16, W)) - 1) * (a[..., None] - near)
    return pack(d, p, j, q, np.repeat(v, L, axis=3), w, a)
def setup_inputs_herd(rng):
    d, p, j, q, v, w, a, hub = parts(rng); o = rng.permutation(8); s = rng.permutation(N)
    for r in range(N):
        x = np.stack([rng.permutation(W)[:L] for g in range(8)])
        if r == s[0]:
            for g in range(8): j[r, g] = x[g, rng.permutation(np.arange(L) % (4 * g + 1))]
        elif r == s[1]:
            j[r] = x
        else:
            j[r, o[0]] = x[0, 0]; j[r, o[1]] = x[1]; j[r, o[2]] = np.tile(x[2, :L // 2], 2); j[r, o[3]] = x[3, rng.integers(0, 4, L)]
            for i in range(4, 8):
                n = 1 + (r + i) % 4; y = x[i].copy(); y[L - n:] = y[:n]; j[r, o[i]] = y
    return pack(d, p, j, q, v, w, a)
def setup_inputs_alike(rng):
    d, p, j, q, v, w, a, hub = parts(rng); o = rng.permutation(8)
    q[:, o[0]] = np.roll(np.take_along_axis(p, j[:, :, None, :], 3), 5, axis=2)[:, o[0]]
    p[:, o[1]] = p[:, o[1]][:, np.arange(16) // 4 * 4]; q[:, o[1]] = q[:, o[1]][:, np.arange(16) // 8 * 8]
    p[:, o[2]] = 0; q[:, o[3]] = 0; p[:, o[4]] = 0; q[:, o[4]] = 0
    q[:, o[5]] = above(rng, hub, j, 1.0)[:, o[5]]
    p[:, o[6]] = above(rng, hub, np.broadcast_to(np.arange(W), (N, 8, W)), 1.0)[:, o[6]]
    a[:, o[7]] = 0
    for r in range(N):
        x = rng.permutation(L); c = L + rng.permutation(W - L)[np.arange(32 * L) % (W - L)].reshape(L, 32).T
        j[r, o[7]] = x; p[r, o[7]][:, x] = c[:16]; q[r, o[7]] = c[16:]
    e = int(rng.integers(0, N)); p[e] = 0; q[e] = 0; j[e] = np.stack([rng.permutation(W)[:L] for g in range(8)])
    return pack(d, p, j, q, v, w, a)
def setup_inputs_ends(rng):
    d, p, j, q, v, w, a, hub = parts(rng); o = rng.permutation(8); c = np.arange(W); e = np.array([0, 1, W - 2, W - 1])
    p[:, o[0]] = np.where(rng.random((N, 16, W)) < 0.5, np.minimum(c + 1, W - 1), c); j[:, o[0], :4] = e; a[:, o[0]] = 5
    p[:, o[1]] = np.where(rng.random((N, 16, W)) < 0.3, W - 1, 0); a[:, o[1]] = 20
    j[:, o[2]] = rng.choice(e, (N, L)); q[:, o[2]] = rng.choice(e, (N, 16, L)); a[:, o[2]] = 30
    w[:, o[3]] = 0; p[:, o[3], :, ::2] = 0; q[:, o[3], :, ::2] = 0
    w[:, o[4]] = 255; v[:, o[4], :, ::2] = 255; p[:, o[4], :, ::3] = 0; q[:, o[4], :, ::2] = 0
    a[:, o[5]] = 0; a[:, o[6]] = 255
    d[:, o[7]] = 0; v[:, o[7]] = 255
    for r in range(N):
        n = r % 4; y = rng.permutation(W)[:L]; y[L - n:] = y[:n].copy()
        j[r, o[7]] = y; a[r, o[7]] = 253 if n == 3 else 255
    return pack(d, p, j, q, v, w, a)
def setup_inputs_spread(rng):
    d, p, j, q, v, w, a, hub = parts(rng)
    d = (np.exp2(8 * rng.random((N, 8, 1, W))) * rng.random((N, 8, 16, W))).astype(np.int64)
    v = (np.exp2(8 * rng.random((N, 8, 1, L))) * rng.random((N, 8, 16, L))).astype(np.int64)
    s = np.argsort(rng.random((N, 8)), axis=1)[..., None] + 1
    a = (np.exp2(s) * rng.random((N, 8, 16))).astype(np.int64)
    w = rng.integers(0, 256, (N, 8, 16)); p = rng.integers(0, W, p.shape); q = rng.integers(0, W, q.shape); j = rng.integers(0, W, j.shape)
    return pack(d, p, j, q, v, w, a)
def check_inputs(d):
    bad = []
    for k, hi in (("d0", 255), ("p0", W - 1), ("j0", W - 1), ("q0", W - 1), ("v0", 255), ("wa", 255)):
        x = np.asarray(d[k]).astype(np.float64)
        if not (np.all(x >= 0) and np.all(x <= hi) and np.all(x == np.floor(x))): bad.append("range of " + k)
    return bad
def stays(d, e, j, v, th):
    x = np.take_along_axis(d, e.reshape(N, 8, 1, 16 * L), 3).reshape(N, 8, 16, 16, L)
    votes = np.add.reduce((np.abs(x - v[:, :, :, None, :]) < th[:, :, :, None, None]).astype(np.int32), axis=2)
    return (e > j[:, :, None, :]) & (votes < 9)
def reference(d0, p0, j0, q0, v0, wa):
    d = d0.astype(np.float32).astype(np.int32).reshape(N, 8, 16, W); p = p0.astype(np.int64).reshape(N, 8, 16, W)
    j = np.stack([gentries(x) for x in j0]).astype(np.int64); q = q0.astype(np.int64).reshape(N, 8, 16, L)
    v = v0.astype(np.float32).astype(np.int32).reshape(N, 8, 16, L)
    w = wa[:, :, 0].astype(np.int32).reshape(N, 8, 16, 1); a = wa[:, :, 1].astype(np.int32).reshape(N, 8, 16)
    waited = np.zeros((N, 8), np.int32)
    for hop in HOP:
        key = (np.arange(8 * N).reshape(N, 8, 1) * W + j).reshape(-1)
        act = np.zeros(8 * N * L, bool); act[np.unique(key, return_index=True)[1]] = True; act = act.reshape(N, 8, L)
        th = a + (waited & 3)[:, :, None]
        pj = np.take_along_axis(p, j[:, :, None, :], 3)
        sp = stays(d, pj, j, v, th); sq = stays(d, q, j, v, th)
        dup = np.any(q[:, :, :, None, :] == pj[:, :, None, :, :], axis=3)
        u = np.where(sp, pj, np.where(sq & ~dup, q, 0))
        f = np.minimum.reduce(np.where(u > 0, u, W), axis=2)
        f = np.where(f < W, f, np.add.reduce(w * v, axis=2) & (HS - 1))
        nd = np.abs(np.take_along_axis(d, j[:, :, None, :], 3) - v)
        nv = np.abs(v - np.take_along_axis(d, f[:, :, None, :], 3))
        d = d.copy(); p = p.copy()
        for r in range(N):
            for g in range(8):
                m = act[r, g]; c = j[r, g][m]
                d[r, g][:, c] = nd[r, g][:, m]; p[r, g][:, c] = u[r, g][:, m]
        waited = np.add.reduce((~act).astype(np.int32), axis=2)
        j = np.where(act, f, j); q = np.where(act[:, :, None, :], u, q); v = np.where(act[:, :, None, :], nv, v)
        j = np.roll(j, hop, axis=0); q = np.roll(q, hop, axis=0); v = np.roll(v, hop, axis=0)
    return {"yd": d.reshape(N, 128, W).astype(np.float32).astype(BF), "yj": j.astype(np.float32), "yq": q.reshape(N, 128, L).astype(np.float32), "yv": v.reshape(N, 128, L).astype(np.float32).astype(BF)}

@@ -1,0 +1,451 @@
+from concourse.mybir import AluOpType, ActivationFunctionType
+
+A = AluOpType
+AF = ActivationFunctionType
+W = 3584
+WX = 3856
+OFF = 1792.0
+C = 8192.0
+HOP = (1, 0, 2, 0)
+DVE_TILES = (1,)
+NX, NAB, NFL = 8, 6, 8
+G, SCAT, F, FPE, HOPNS, XFER = 1.56, 3.8, 1.04, 0.52, 120.0, 3200.0
+MIX, WIN, ITER, SEED, AMP = 250.0, 100.0, 600, 1, 30.0
+
+
+def _sb(d, **kw):
+    return {k: ("sbuf", [128] + (list(v) if isinstance(v, tuple) else [v]), d) for k, v in kw.items()}
+
+
+SCRATCH = {}
+SCRATCH.update(_sb("bfloat16", D0=WX, D1=WX, D2=WX, D3=WX, D4=WX, V=1280, VO=1024, X=NX * 1024, AB=NAB * 1024, FL=NFL * 1024,
+                   DUF=4096, EA=(8, 128), EB=(8, 128), EC=(8, 128), WR=1024, SG=512, VT=256, DJ=256, ND=256, DV=256, RL=256, Y=128,
+                   ones=2048, E=2048, ID=11 * 128, blk=256, REP=2048, BW=144, R8=128, tri=(8, 16), mk=(8, 16), cst=128, b8=64))
+SCRATCH.update(_sb("float16", QC=1280, QO=1024, JC=8 * 144, JO=8 * 144, PC=1024, LS=16, F8=256, cm=24))
+SCRATCH.update(_sb("int32", PT=WX, q0i=256, j0i=16, wai=2, aci=8, hi=32, mi=16, pi=4))
+SCRATCH.update(_sb("uint16", QU=1024, PU=1024, UU=1024, JU=64, FU=64, SO=64))
+SCRATCH.update(_sb("float32", waf=2, JF=64, sa=16, sb=16, AC=8, TH=4, TQ=256, TP=128, S0=512, SC=256, YQ=256, YJ=256,
+                   pf=8, r144=144, rg=128, rc=(8, 16), m16=16, dum=16))
+SCRATCH.update({k: ("psum", [128, n], "float32") for k, n in (("DF0", 1024), ("DF1", 1024), ("ZP", 512), ("ZQ", 512), ("DU", 512), ("MI", 512))})
+SEMAPHORES = ["pe", "dve", "act", "pool", "sent"] + ["m%d" % k for k in range(50)] + ["a%d" % k for k in range(16)]
+
+
+def program(g, T, dests):
+    ops = []
+    nd = [0, 0]
+    V_, S_, PE = g.vector, g.scalar, g.tensor
+
+    def add(eng, dur, fn, r, w, banks=(), sem=None, lat=0.0, cnt=0):
+        ops.append({"eng": eng, "dur": dur, "fn": fn, "r": list(r), "w": list(w), "banks": banks, "sem": sem, "lat": lat, "cnt": cnt})
+
+    def dve(n, fn, r, w, *banks):
+        add("dve", 55 + max(n, 16) * F, fn, r, w, banks)
+
+    def act(n, fn, r, w, *banks):
+        add("act", 70 + max(n, 16) * F, fn, r, w, banks)
+
+    def mm(lst, r, w, *banks):
+        def fn():
+            ins = None
+            for (o, a, b, s0, s1, n) in lst:
+                ins = PE.matmul(o, a, b, s0, s1)
+            return ins
+        add("pe", 60 + sum(max(64, x[5]) for x in lst) * FPE, fn, r, w, banks)
+
+    def grp(out, terms, n):
+        return [(out, a, b, k == 0, k == len(terms) - 1, n) for k, (a, b) in enumerate(terms)]
+
+    def dma(out, in_, nbytes, r, w):
+        k = nd[0]
+        nd[0] += 1
+        add("sp", 60.0, lambda: g.sync.dma_start(out, in_), r, w, (), "m%d" % k, 1900 + nbytes / 190.0, 16)
+
+    def send(t, out, in_, r, w):
+        k = nd[1]
+        nd[1] += 1
+        rid, pid, mask, ne = dests[t]
+        add("pool", 150.0, lambda: g.remote_dma(out, in_, T.sem["a%d" % k], T.sem.sent, pid, rid, mask), r, w, (), "a%d" % k, XFER, ne)
+
+    def ts(out, in0, s1, op0, s2=None, op1=None):
+        if op1 is None:
+            return lambda: V_.tensor_scalar(out, in0, s1, None, op0)
+        return lambda: V_.tensor_scalar(out, in0, s1, s2, op0, op1)
+
+    def tt(out, a, b, op):
+        return lambda: V_.tensor_tensor(out, a, b, op)
+
+    def cp(out, a):
+        return lambda: V_.tensor_copy(out, a)
+
+    def ac(out, a, f, **kw):
+        return lambda: S_.activation(out, a, f, **kw)
+
+    def iota(out, pat):
+        return lambda: g.iota(out, pat, 0, 0, allow_small_or_imprecise_dtypes=True)
+
+    D = [T.D0, T.D1, T.D2, T.D3, T.D4]
+    dma(T.q0i[:], T.q0[:], 131072, [], ["q0i"])
+    dma(T.D0[:, 0:W], T.d0[:], 917504, [], ["D0"])
+    dma(T.j0i[:], T.j0[:], 8192, [], ["j0i"])
+    dma(T.V[:, 0:256], T.v0[:], 65536, [], ["V00", "V01"])
+    dma(T.wai[:], T.wa[:], 1024, [], ["wai"])
+    dma(T.PT[:, 0:W], T.p0[:], 3 * 917504, [], ["PT"])
+    dma(T.D1[:, 0:W], T.d0[:], 4 * 917504, [], ["D1"])
+    add("pool", 150, lambda: g.iota(T.pi[:, 0:1], [[0, 1]], 0, 1), [], ["pi0"])
+    add("pool", 430, iota(T.r144[:], [[1, 144]]), [], ["r144"])
+    add("pool", 400, iota(T.rg[:], [[1, 8], [0, 16]]), [], ["rg"])
+    add("pool", 400, iota(T.rc[:], [[0, 8], [1, 16]]), [], ["rc"])
+    dve(1024, lambda: V_.memset(T.ones[:], 1.0), [], ["ones"])
+    add("pool", 4500, lambda: g.affine_select(T.E[:], T.ones[:], [[-1, 128], [0, 16]], A.is_equal, 0.0, 0, 1), ["ones"], ["E"])
+    dve(136, lambda: V_.memset(T.D0[:, W:WX], 0.0), [], ["D0x"])
+    dve(136, lambda: V_.memset(T.D1[:, W:WX], 0.0), [], ["D1x"])
+    dve(272, lambda: V_.memset(T.PT[:, W:WX], 0), [], ["PTx"])
+    dve(512, lambda: V_.memset(T.S0[:], 1.0e9), [], ["S00", "S01", "S10", "S11"])
+    dve(64, lambda: V_.memset(T.cst[:], -14.0), [], ["c14"])
+    dve(1, ts(T.pi[:, 1:2], T.pi[:, 0:1], 15, A.bitwise_and), ["pi0"], ["pi1"])
+    dve(1, ts(T.pi[:, 2:3], T.pi[:, 0:1], 4, A.arith_shift_right), ["pi0"], ["pi2"])
+    dve(1, cp(T.pf[:, 0:3], T.pi[:, 0:3]), ["pi0", "pi1", "pi2"], ["pf"])
+    p_, pm, pg = T.pf[:, 0:1], T.pf[:, 1:2], T.pf[:, 2:3]
+    r8 = T.r144[:, 0:8]
+    dve(1, ts(T.pf[:, 4:5], p_, 16.0, A.mult, 15.0, A.add), ["pf"], ["pf4"])
+    dve(1, ts(T.pf[:, 5:6], pg, -8192.0, A.mult, 7 * 8192.0 + OFF + C / 2, A.add), ["pf"], ["pf5"])
+    I0, In, I2C, I16, Iw, IR, InC, Io, Ip, Ih, Inh = [T.ID[:, 128 * k:128 * k + 128] for k in range(11)]
+    dve(128, ts(I0, T.r144[:, 0:128], p_, A.is_equal), ["pf", "r144"], ["I0"])
+    for k, val in ((1, -1.0), (2, 2 * C), (3, -16.0), (4, -2048.0), (6, -C), (7, -OFF), (8, OFF), (9, C / 2), (10, -C / 2)):
+        dve(64, ts(T.ID[:, 128 * k:128 * k + 128], I0, val, A.mult), ["I0"], ["I%d" % k])
+    dve(64, ts(IR, I0, T.pf[:, 5:6], A.mult), ["I0", "pf5"], ["I5"])
+    blkC = T.blk[:, 128:256]
+    dve(128, ts(T.blk[:, 0:128], T.rg[:], pg, A.is_equal), ["pf", "rg"], ["blk"])
+    dve(64, ts(blkC, T.blk[:, 0:128], C, A.mult), ["blk"], ["blkC"])
+    dve(16, ts(T.m16[:], T.r144[:, 0:16], pm, A.is_equal), ["pf", "r144"], ["m16"])
+    rep = [T.REP[:, 128 * i:128 * i + 128] for i in range(16)]
+    REPS = ["REP%d" % i for i in range(16)]
+    for i in range(16):
+        dve(64, ts(rep[i], T.blk[:, 0:128], T.m16[:, i:i + 1], A.mult), ["blk", "m16"], [REPS[i]])
+    dve(144, ts(T.BW[:], T.r144[:], T.pf[:, 4:5], A.is_equal), ["pf4", "r144"], ["BW"])
+    dve(128, ts(T.R8[:], T.rg[:], p_, A.is_equal), ["pf", "rg"], ["R8"])
+    dve(128, ts(T.tri[:], T.rc[:], pm, A.is_gt), ["pf", "rc"], ["tri"])
+    dve(128, ts(T.mk[:], T.rc[:], pm, A.is_equal), ["pf", "rc"], ["mk"])
+    dve(16, ts(T.dum[:], T.r144[:, 0:16], 16.0, A.mult, pm, A.add), ["pf", "r144"], ["dum0"])
+    dve(16, ts(T.dum[:], T.dum[:], W + 1 - OFF, A.add), ["dum0"], ["dum"])
+    for k, val in ((0, C / 16), (1, -C / 16), (2, W / 16.0), (3, 1 / 16.0), (5, 1.0), (6, 16.0), (7, C)):
+        dve(8, ts(T.b8[:, 8 * k:8 * k + 8], r8, pg, A.is_equal, val, A.mult), ["pf", "r144"], ["b8%d" % k])
+    dve(2, cp(T.waf[:], T.wai[:]), ["wai"], ["waf"])
+    dve(8, ts(T.b8[:, 32:40], r8, pg, A.is_equal, T.waf[:, 0:1], A.mult), ["pf", "r144", "waf"], ["b84"])
+    for k, (m_, a_) in enumerate(((-64.0, 480.0), (-64.0, 558.0), (0.0, -14.0))):
+        dve(8, ts(T.cm[:, 8 * k:8 * k + 8], r8, m_, A.mult, a_, A.add), ["r144"], ["cm%d" % k])
+    ones128 = T.ones[:, 0:128]
+    zP, scA, RR = T.ZP[:, 0:128], T.ZP[:, 128:256], T.ZP[:, 384:512]
+    zQ, vTp, zT = T.ZQ[:, 0:128], T.ZQ[:, 128:256], T.ZQ[:, 256:384]
+    cw, penP, penQ = T.MI[:, 0:128], T.MI[:, 256:384], T.MI[:, 384:512]
+    for h in range(2):
+        n = "0%d" % h
+        jw = T.JC[:, 144 * h + 128:144 * h + 136]
+        dve(128, cp(T.QU[:, 128 * h:128 * h + 128], T.q0i[:, 128 * h:128 * h + 128]), ["q0i"], ["QU" + n])
+        dve(128, ts(T.QC[:, 128 * h:128 * h + 128], T.q0i[:, 128 * h:128 * h + 128], -OFF, A.add), ["q0i"], ["QC" + n])
+        dve(8, ts(jw, T.j0i[:, 8 * h:8 * h + 8], -OFF, A.add), ["j0i"], ["JW" + n])
+        mm([(T.ZP[:, 384 + c:512:16], rep[c], jw, True, True, 8) for c in range(16)], REPS + ["JW" + n], ["RR"], "ZP")
+        dve(128, cp(T.JC[:, 144 * h:144 * h + 128], RR), ["RR"], ["JR" + n], "ZP")
+
+    tile = 0
+    UUS = {}
+    for t in range(4):
+        last = t == 3
+        Dn = ["D%d" % t] + (["D%dx" % t] if t < 2 else [])
+        Dw = D[t][:, 0:WX]
+        if t == 0:
+            th, thn = T.waf[:, 1:2], "waf"
+        else:
+            th, thn = T.TH[:, t:t + 1], "TH%d" % t
+            k = 2 * (t - 1)
+            dve(1, tt(T.aci[:, k:k + 1], T.AC[:, k:k + 1], T.AC[:, k + 1:k + 2], A.add), ["AC%d0" % (t - 1), "AC%d1" % (t - 1)], ["aci%d" % k])
+            dve(1, ts(T.aci[:, k + 1:k + 2], T.aci[:, k:k + 1], 3, A.bitwise_and), ["aci%d" % k], ["aci%d" % (k + 1)])
+            dve(1, tt(th, T.aci[:, k + 1:k + 2], T.waf[:, 1:2], A.add), ["aci%d" % (k + 1), "waf"], [thn])
+            dma(D[t + 1][:], D[t][:], 987136, Dn, ["D%d" % (t + 1)])
+        for h in range(2):
+            n, H, s, c0 = "%d%d" % (t, h), str(h), 2 * t + h, 256 * t + 128 * h
+            hs, h8 = slice(128 * h, 128 * h + 128), slice(8 * h, 8 * h + 8)
+            qc, v, pu, wr = [b[:, c0:c0 + 128] for b in (T.QC, T.V, T.PU, T.WR)]
+            jr, jw = T.JC[:, 144 * s:144 * s + 128], T.JC[:, 144 * s + 128:144 * s + 136]
+            ju, jf, fu, so = [b[:, 8 * s:8 * s + 8] for b in (T.JU, T.JF, T.FU, T.SO)]
+            pc = T.PC[:, 512 * h:512 * h + 128]
+            duf = [T.DUF[:, 2048 * h + 128 * i:2048 * h + 128 * i + 128] for i in range(16)]
+            dve(8, ts(ju, jw, OFF, A.add), ["JW" + n], ["JU" + n])
+            dve(8, cp(jf, jw), ["JW" + n], ["JF" + n])
+            mm(grp(vTp, [(v, In)], 128), ["V" + n, "I1"], ["vTp"], "ZQ")
+            act(128, ac(T.VT[:, hs], vTp, AF.Copy), ["vTp"], ["VT" + H], "ZQ")
+            dve(128 * G, cp(pu, T.PT[:, 0:W].indirect(ju)), ["PT", "JU" + n], ["PU" + n])
+            dve(64, ts(pc, pu, -OFF, A.add), ["PU" + n], ["PC" + H])
+            for k in range(1, 4):
+                dma(T.PC[:, 512 * h + 128 * k:512 * h + 128 * k + 128], pc, 32768, ["PC" + H], ["P4%s%d" % (H, k)])
+            EO, en = (T.EA, "EA") if h == 0 else (T.EB, "EB")
+            terms, rd = [], ["blkC"]
+            if h == 1:
+                for b in range(8):
+                    dve(64, ts(T.EC[:, b, :], jr, T.JF[:, 16 * t + b:16 * t + b + 1], A.is_equal), ["JR" + n, "JF%d0" % t], ["EC%d" % b])
+                    terms.append((cw, blkC, T.EC[:, b, :], b == 0, False, 128))
+                    rd.append("EC%d" % b)
+            for b in range(8):
+                m = 128 - 16 * b
+                dve(m / 2, ts(EO[:, b, 0:m], T.JC[:, 144 * s + 16 * b:144 * s + 128], T.JF[:, 8 * s + b:8 * s + b + 1], A.is_equal),
+                    ["JR" + n, "JF" + n], [en + str(b)])
+                terms.append((T.MI[:, 16 * b:128], blkC, EO[:, b, 0:m], b == 0 and h == 0, b == 7, m))
+            ens = [en + str(b) for b in range(8)]
+            dve(256, tt(EO[:, :, 0:16], EO[:, :, 0:16], T.tri[:], A.mult), ens + ["tri"], ens)
+            mm(terms, rd + ens, ["cw"], "MI")
+            act(128, ac(wr, cw, AF.Sign, accum_out=T.AC[:, s:s + 1]), ["cw"], ["WR" + n, "AC" + n], "MI")
+            wW = T.MI[:, 128 + 8 * h:136 + 8 * h]
+            mm(grp(vTp, [(wr, I0)], 128), ["WR" + n, "I0"], ["vTp"], "ZQ")
+            dve(128, tt(T.Y[:], vTp, T.mk[:], A.mult), ["vTp", "mk"], ["Y"], "ZQ")
+            mm(grp(wW, [(T.cst[:], T.ones[:, 0:8]), (T.Y[:], T.b8[:, 56:64])], 8), ["c14", "ones", "b87", "Y"], ["wW" + H], "MI")
+            dve(8, tt(T.sa[:, h8], wW, T.dum[:, h8], A.min), ["wW" + H, "dum"], ["sa" + H], "MI")
+            dve(8, tt(T.sb[:, h8], T.sa[:, h8], jf, A.max), ["sa" + H, "JF" + n], ["sb" + H])
+            dve(8, ts(so, T.sb[:, h8], OFF, A.add), ["sb" + H], ["SO" + n])
+            y0 = 160 + 32 * h
+            mm([(T.MI[:, y0:y0 + 24], wr, T.b8[:, 0:24], True, False, 24), (T.MI[:, y0 + 8:y0 + 16], jr, T.b8[:, 24:32], False, False, 8),
+                (T.MI[:, y0:y0 + 24], ones128, T.cm[:], False, True, 24), (T.MI[:, y0 + 24:y0 + 32], v, T.b8[:, 32:40], True, True, 8)],
+               ["WR" + n, "JR" + n, "V" + n, "ones", "b80", "b81", "b82", "b83", "b84", "cm0", "cm1", "cm2"], ["y" + H], "MI")
+            h1, h2 = T.hi[:, 16 * h:16 * h + 8], T.hi[:, 16 * h + 8:16 * h + 16]
+            dve(8, cp(h1, T.MI[:, y0 + 24:y0 + 32]), ["y" + H], ["hi" + H], "MI")
+            dve(8, ts(h2, h1, 1023, A.bitwise_and), ["hi" + H], ["hj" + H])
+            dve(8, tt(T.S0[:, 256 * h:256 * h + 256:32], T.MI[:, y0:y0 + 8], h2, A.add), ["y" + H, "hj" + H], ["S0" + H], "MI")
+            dve(8, cp(T.S0[:, 256 * h + 1:256 * h + 256:32], T.MI[:, y0 + 8:y0 + 16]), ["y" + H], ["S1" + H], "MI")
+            mm(grp(penP, [(I0, pc), (In, jr), (InC, wr)], 128) + grp(penQ, [(I0, qc), (In, jr)], 128),
+               ["I0", "I1", "I6", "WR" + n, "PC" + H, "QC" + n, "JR" + n], ["pen"], "MI")
+            act(256, ac(T.SG[:, 256 * h:256 * h + 256], T.MI[:, 256:512], AF.Sign, bias=-0.5), ["pen"], ["SG" + H], "MI")
+            for u in range(4):
+                mm([(T.DU[:, 128 * a:128 * a + 128], rep[4 * u + a], qc, True, True, 128) for a in range(4)], REPS + ["QC" + n], ["DU"], "DU")
+                f0 = 2048 * h + 512 * u
+                dve(512, tt(T.DUF[:, f0:f0 + 512], T.DU[:], T.PC[:, 512 * h:512 * h + 512], A.is_equal),
+                    ["DU", "PC" + H] + ["P4%s%d" % (H, x) for x in (1, 2, 3)], ["DUF%s%d" % (H, u)], "DU")
+            if h == 1:
+                dve(256 * G, tt(T.DJ[:], Dw.indirect(T.JU[:, 16 * t:16 * t + 16]), T.V[:, 256 * t:256 * t + 256], A.subtract),
+                    Dn + ["JU%d0" % t, "JU" + n, "V%d0" % t, "V" + n], ["DJ"])
+                act(256, ac(T.ND[:], T.DJ[:], AF.Abs), ["DJ"], ["ND"])
+                dve(256 * SCAT, cp(D[t + 1][:, 0:WX].indirect(T.SO[:, 16 * t:16 * t + 16]), T.ND[:]), ["ND", "SO%d0" % t, "SO" + n],
+                    ["D%d" % (t + 1)] + (["D1x"] if t == 0 else []))
+                if last:
+                    dma(T.yd[:], T.D4[:, 0:W], 917504, ["D4"], ["yd"])
+            for kind in range(2):
+                offs, on = (T.QU, "QU" + n) if kind == 0 else (T.PU, "PU" + n)
+                for u in range(2):
+                    k = tile
+                    tile += 1
+                    x0, xn = 1024 * (k % NX), "X%d" % (k % NX)
+                    src = Dw.indirect(offs[:, c0 + 64 * u:c0 + 64 * u + 64])
+                    if k in DVE_TILES:
+                        dve(1024 * G, cp(T.X[:, x0:x0 + 1024], src), Dn + [on], [xn])
+                    else:
+                        act(1024 * G, ac(T.X[:, x0:x0 + 1024], src, AF.Copy), Dn + [on], [xn])
+                    DF, dn = (T.DF0, "DF0") if u == 0 else (T.DF1, "DF1")
+                    lst = []
+                    for b in range(2):
+                        e0 = 1024 * u + 512 * b
+                        lst += grp(DF[:, 512 * b:512 * b + 512], [(T.VT[:, hs], T.E[:, e0:e0 + 512]), (I0, T.X[:, x0 + 512 * b:x0 + 512 * b + 512])], 512)
+                    mm(lst, [xn, "I0", "VT" + H, "E"], [dn], dn)
+                    ab, an = T.AB[:, 1024 * (k % NAB):1024 * (k % NAB) + 1024], "AB%d" % (k % NAB)
+                    act(1024, ac(ab, DF[:], AF.Abs), [dn], [an], dn)
+                    f0 = 1024 * (k % NFL)
+                    dve(512, ts(T.FL[:, f0:f0 + 1024], ab, th, A.is_lt, 15.0 / 32, A.add), [an, thn], ["FL%d" % (k % NFL)])
+                f0, g0 = f0 - 1024, 256 * h + 128 * (1 - kind)
+                lst = [(zT, T.SG[:, g0:g0 + 128], I16, True, False, 128)]
+                rd = ["b85", "I3", "SG" + H, "FL%d" % ((k - 1) % NFL), "FL%d" % (k % NFL)]
+                if kind == 0:
+                    lst += [(zT, wr, Iw, False, False, 128)]
+                    lst += [(T.ZQ[:, 256 + i:384:16], duf[i], T.b8[:, 48:56], False, False, 8) for i in range(16)]
+                    rd += ["b86", "I4", "WR" + n] + ["DUF%s%d" % (H, x) for x in range(4)]
+                lst += [(T.ZQ[:, 256 + i:384:16], T.FL[:, f0 + i:f0 + 2048:16], T.b8[:, 40:48], False, i == 15, 8) for i in range(16)]
+                mm(lst, rd, ["zT"], "ZQ")
+                rl = T.RL[:, 128 * kind:128 * kind + 128]
+                act(128, ac(rl, zT, AF.Sign), ["zT"], ["RL%d" % kind], "ZQ")
+                if kind == 0:
+                    mm(grp(zQ, [(rl, Io)], 128), ["I7", "RL0"], ["zQ"], "ZQ")
+                    dve(128, tt(T.TQ[:, hs], zQ, qc, A.min), ["zQ", "QC" + n], ["TQ" + H], "ZQ")
+                else:
+                    mm(grp(zP, [(rl, Io)], 128) + grp(scA, [(rl, Ip)], 128), ["I7", "I8", "RL1"], ["zP", "scA"], "ZP")
+            mv = HOP[t] != 0
+            n1, s1, c1 = "%d%d" % (t + 1, h), s + 2, c0 + 256
+            if mv:
+                qo, qn, vo, vn = T.QO[:, c0:c0 + 128], "QO" + n, T.VO[:, c0:c0 + 128], "VO" + n
+                JB, j0, jrn, jwn = T.JO, 144 * s, "JOR" + n, "JOW" + n
+            else:
+                qo, qn, vo, vn = T.QC[:, c1:c1 + 128], "QC" + n1, T.V[:, c1:c1 + 128], "V" + n1
+                JB, j0, jrn, jwn = T.JC, 144 * s1, "JR" + n1, "JW" + n1
+            dve(128, tt(T.TP[:], zP, pc, A.min), ["zP", "PC" + H], ["TP"], "ZP")
+            dve(128, tt(scA, scA, T.TQ[:, hs], A.min), ["scA", "TQ" + H], ["scA"], "ZP")
+            dve(128, tt(qo, scA, T.TP[:], A.max), ["scA", "TP"], [qn], "ZP")
+            if not last:
+                uu, un = (T.UU[:, c0:c0 + 128], "UU" + n) if mv else (T.QU[:, c1:c1 + 128], "QU" + n1)
+                UUS[h] = (uu, un)
+                dve(64, ts(uu, qo, OFF, A.add), [qn], [un])
+            if mv:
+                send(t, T.QU[:, c1:c1 + 128], uu, [un], ["QU" + n1])
+                send(t, T.QC[:, c1:c1 + 128], qo, [qn], ["QC" + n1])
+            sq, sp = T.RL[:, 0:128], T.RL[:, 128:256]
+            mm(grp(T.ZP[:, 257:512:2], [(ones128, IR), (ones128, Ih), (qc, I0), (wr, I2C), (Ih, sq), (Inh, sp)], 128)
+               + grp(T.ZP[:, 256:512:2], [(ones128, IR), (pc, I0), (Ih, sp)], 128),
+               ["ones", "I5", "I2", "I0", "I9", "I10", "WR" + n, "QC" + n, "PC" + H, "RL0", "RL1"], ["KT", "RR"], "ZP")
+            dve(256, lambda h=h: V_.tensor_tensor_scan(T.SC[:], T.S0[:, 256 * h:256 * h + 256], T.ZP[:, 256:512], 1.0e9, A.min, A.min),
+                ["KT", "RR", "S0" + H, "S1" + H], ["SC"], "ZP")
+            dve(8, cp(T.mi[:, 0:8], T.SC[:, 31:256:32]), ["SC"], ["mi0"])
+            dve(8, ts(T.mi[:, 8:16], T.mi[:, 0:8], 4095, A.bitwise_and), ["mi0"], ["mi1"])
+            dve(8, ts(T.LS[:, 0:8], T.mi[:, 8:16], -OFF, A.add), ["mi1"], ["LS0"])
+            dve(8, tt(T.LS[:, 8:16], T.MI[:, y0 + 16:y0 + 24], T.LS[:, 0:8], A.max), ["LS0", "y" + H], ["LS1"], "MI")
+            mm([(T.ZP[0:8, 256:384], T.LS[:, 0:8], I0, True, True, 128), (T.ZP[0:8, 384:512], T.LS[:, 8:16], I0, True, True, 128)],
+               ["LS0", "LS1", "I0"], ["KT", "RR"], "ZP")
+            dve(256, cp(T.F8[0:8, :], T.ZP[0:8, 256:512]), ["KT", "RR"], ["F8"], "ZP")
+            mm(grp(T.ZQ[:, 384:400], [(T.BW[0:8, 15 - c:143 - c], T.F8[0:8, c:256:16]) for c in range(16)], 16), ["F8", "BW"], ["Wr"], "ZQ")
+            dve(8, ts(fu, T.ZQ[:, 392:400], OFF, A.add), ["Wr"], ["FU" + n], "ZQ")
+            dve(128 * G, tt(T.DV[:, hs], Dw.indirect(fu), v, A.subtract), Dn + ["FU" + n, "V" + n], ["DV" + H])
+            act(128, ac(vo, T.DV[:, hs], AF.Abs), ["DV" + H], [vn])
+            if not last:
+                dve(8, cp(JB[:, j0 + 128:j0 + 136], T.ZQ[:, 384:392]), ["Wr"], [jwn], "ZQ")
+                mm(grp(RR, [(T.R8[0:8, :], T.F8[0:8, 0:128])], 128), ["F8", "R8"], ["RR"], "ZP")
+                dve(128, cp(JB[:, j0:j0 + 128], RR), ["RR"], [jrn], "ZP")
+                if mv:
+                    send(t, T.JC[:, 144 * s1:144 * s1 + 136], T.JO[:, j0:j0 + 136], [jrn, jwn], ["JR" + n1, "JW" + n1])
+                    send(t, T.V[:, c1:c1 + 128], vo, [vn], ["V" + n1])
+                if h == 1:
+                    for x in range(2):
+                        dve(128 * SCAT, cp(T.PT[:, 0:WX].indirect(T.SO[:, 16 * t + 8 * x:16 * t + 8 * x + 8]), UUS[x][0]),
+                            [UUS[x][1], "SO%d%d" % (t, x), "PTx"], ["PT"])
+            else:
+                dve(128, ts(T.YQ[:, hs], qo, OFF, A.add), [qn], ["YQ" + H])
+                dma(T.yq[:, hs], T.YQ[:, hs], 65536, ["YQ" + H], ["yq" + H])
+                dve(128, ts(T.YJ[0:8, hs], T.F8[0:8, 0:128], OFF, A.add), ["F8"], ["YJ" + H])
+                dma(T.yj[:, hs], T.YJ[0:8, hs], 4096, ["YJ" + H], ["yj" + H])
+                dma(T.yv[:, hs], vo, 32768, [vn], ["yv" + H])
+    return ops
+
+
+def schedule(ops, deps0, succ, pr):
+    n = len(ops)
+    deps = [set(d) for d in deps0]
+    left = [len(d) for d in deps]
+    ready = {k: 0.0 for k in range(n) if left[k] == 0}
+    free, done, bank, order, t0 = {}, [0.0] * n, {}, [], [0.0] * n
+    while ready:
+        st = {}
+        for k, s in ready.items():
+            o = ops[k]
+            s = max(s, free.get(o["eng"], 0.0))
+            for b in o["banks"]:
+                for e, d in bank.get(b, {}).items():
+                    if e != o["eng"]:
+                        s = max(s, done[d] + HOPNS)
+            st[k] = s
+        k0 = min(ready, key=lambda k: (st[k], -pr[k]))
+        e0 = ops[k0]["eng"]
+        k = max([x for x in ready if ops[x]["eng"] == e0 and st[x] <= st[k0] + WIN], key=lambda x: (pr[x], -x))
+        o = ops[k]
+        for b in o["banks"]:
+            for e, d in bank.setdefault(b, {}).items():
+                if e != o["eng"]:
+                    deps[k].add(d)
+            bank[b][o["eng"]] = k
+        free[e0] = st[k] + o["dur"]
+        done[k] = st[k] + o["dur"] + o["lat"]
+        t0[k] = st[k]
+        order.append(k)
+        del ready[k]
+        for x in succ[k]:
+            left[x] -= 1
+            if left[x] == 0:
+                ready[x] = max(done[d] for d in deps0[x]) + HOPNS
+    return order, deps, max(done), t0
+
+
+PLANS = {}
+
+
+def plan(ops):
+    n = len(ops)
+    if n not in PLANS:
+        wr, rd, deps = {}, {}, []
+        for k, o in enumerate(ops):
+            d = set(wr[x] for x in o["r"] + o["w"] if x in wr)
+            for x in o["w"]:
+                d.update(rd.get(x, ()))
+            for x in o["r"]:
+                rd.setdefault(x, []).append(k)
+            for x in o["w"]:
+                wr[x] = k
+                rd[x] = []
+            deps.append(d)
+        succ = [[] for _ in range(n)]
+        for k in range(n):
+            for d in deps[k]:
+                succ[d].append(k)
+        pr = [0.0] * n
+        for k in range(n - 1, -1, -1):
+            pr[k] = ops[k]["dur"] + ops[k]["lat"] + max([pr[x] + HOPNS for x in succ[k]] + [0.0])
+        pr = [pr[k] - k * MIX for k in range(n)]
+        best = schedule(ops, deps, succ, pr)
+        kinds = sorted(set(o["eng"] + o["w"][0].rstrip("0123456789") for o in ops))
+        kind = [kinds.index(o["eng"] + o["w"][0].rstrip("0123456789")) for o in ops]
+        x = SEED
+        for it in range(ITER):
+            q = list(pr)
+            for _ in range(2 if it < ITER * 0.7 else 30):
+                x = (x * 1103515245 + 12345) % 2147483648
+                c = x >> 8
+                x = (x * 1103515245 + 12345) % 2147483648
+                a = ((x >> 8) % 2001 - 1000) * AMP
+                if it < ITER * 0.7:
+                    for k in range(n):
+                        if kind[k] == c % len(kinds):
+                            q[k] += a
+                else:
+                    q[c % n] += a / 3
+            r = schedule(ops, deps, succ, q)
+            if r[2] <= best[2]:
+                best, pr = r, q
+        PLANS[n] = best
+    best = PLANS[n]
+    for k in range(n):
+        ops[k]["t0"] = best[3][k]
+    return best[:3]
+
+
+def rank_program(g, core, T, topo):
+    rank = T.rank_of(core)
+    if rank is None:
+        return
+    dests = {}
+    for t, hop in enumerate(HOP):
+        if hop:
+            dst = T.cores[(rank + hop) % len(T.cores)]
+            rid, pid, _ = topo.addr(dst)
+            dests[t] = (rid, pid, topo.mask(core, dst), len(topo.engines(core, dst)))
+    ops = program(g, T, dests)
+    order, deps, _ = plan(ops)
+    queue = {"pe": g.tensor, "dve": g.vector, "act": g.scalar, "pool": g, "sp": g.sync}
+    count, mark, known, sent = {}, {}, {}, 0
+    seen = {e: {} for e in queue}
+    for k in order:
+        o = ops[k]
+        e = o["eng"]
+        for d in sorted(deps[k], key=lambda d: -ops[d]["t0"]):
+            sem, val = mark[d]
+            if not (sem == "pe" and e == "pe") and seen[e].get(sem, 0) < val:
+                queue[e].wait_ge(T.sem[sem], val)
+                seen[e][sem] = val
+                for s_, v_ in known[d].items():
+                    if seen[e].get(s_, 0) < v_:
+                        seen[e][s_] = v_
+        known[k] = dict(seen[e]) if o["sem"] is None or o["sem"][0] == "m" else {}
+        ins = o["fn"]()
+        if o["sem"] is None:
+            count[e] = count.get(e, 0) + 1
+            ins.then_inc(T.sem[e], 1)
+            mark[k] = (e, count[e])
+        else:
+            if o["sem"][0] == "m":
+                ins.then_inc(T.sem[o["sem"]], 16)
+            else:
+                sent += o["cnt"]
+            count[o["sem"]] = o["cnt"]
+            mark[k] = (o["sem"], o["cnt"])
+    g.wait_ge(T.sem.sent, sent)
+    for sem, val in count.items():
+        g.wait_ge(T.sem[sem], val)

@@ -3,14 +3,15 @@ from concourse.mybir import AluOpType, ActivationFunctionType
 A = AluOpType
 AF = ActivationFunctionType
 W = 3584
-WX = 3856
+WX = 4112
 OFF = 1792.0
 C = 8192.0
 HOP = (1, 0, 2, 0)
-DVE_TILES = (1,)
-NX, NAB, NFL = 8, 6, 8
-G, SCAT, F, FPE, HOPNS, XFER = 1.56, 3.8, 1.04, 0.52, 120.0, 3200.0
-MIX, WIN, ITER, SEED, AMP = 250.0, 100.0, 600, 1, 30.0
+DVE_TILES = (1, 5, 11, 19, 27, 30)
+P4V = (0,)
+NX, NAB, NFL = 8, 8, 8
+PARS = [(1.0, 1.56, 3.8, 140.0, 3300.0), (0.85, 1.2, 2.5, 200.0, 4000.0), (1.2, 1.95, 5.0, 100.0, 2800.0), (1.15, 1.2, 4.5, 140.0, 3300.0)]
+HOPNS, MIX, WIN, ITER, SEED, AMP, MOVES, TEMP = 140.0, 250.0, 100.0, 1200, 1, 10.0, 14000, 60.0
 
 
 def _sb(d, **kw):
@@ -19,19 +20,21 @@ def _sb(d, **kw):
 
 SCRATCH = {}
 SCRATCH.update(_sb("bfloat16", D0=WX, D1=WX, D2=WX, D3=WX, D4=WX, V=1280, VO=1024, X=NX * 1024, AB=NAB * 1024, FL=NFL * 1024,
-                   DUF=4096, EA=(8, 128), EB=(8, 128), EC=(8, 128), WR=1024, SG=512, VT=256, DJ=256, ND=256, DV=256, RL=256, Y=128,
+                   DUF=4096, EA=(8, 128), EB=(8, 128), EC=(8, 128), WR=1024, SG=512, VT=256, DJ=256, ND=256, DV=256, RL=256,
                    ones=2048, E=2048, ID=11 * 128, blk=256, REP=2048, BW=144, R8=128, tri=(8, 16), mk=(8, 16), cst=128, b8=64))
-SCRATCH.update(_sb("float16", QC=1280, QO=1024, JC=8 * 144, JO=8 * 144, PC=1024, LS=16, F8=256, cm=24))
+SCRATCH.update(_sb("float16", QC=1280, QO=1024, JC=8 * 144, JO=8 * 144, PC=1024, LS=16, Y=128, Gd=(16, 16), F8=256, cm=24))
 SCRATCH.update(_sb("int32", PT=WX, q0i=256, j0i=16, wai=2, aci=8, hi=32, mi=16, pi=4))
 SCRATCH.update(_sb("uint16", QU=1024, PU=1024, UU=1024, JU=64, FU=64, SO=64))
-SCRATCH.update(_sb("float32", waf=2, JF=64, sa=16, sb=16, AC=8, TH=4, TQ=256, TP=128, S0=512, SC=256, YQ=256, YJ=256,
-                   pf=8, r144=144, rg=128, rc=(8, 16), m16=16, dum=16))
+SCRATCH.update(_sb("float32", waf=2, JF=64, sb=16, AC=8, TH=4, TQ=256, TP=128, S0=512, SC=256, YQ=256, YJ=256,
+                   pf=8, r144=144, rg=128, rc=(8, 16), m16=16))
 SCRATCH.update({k: ("psum", [128, n], "float32") for k, n in (("DF0", 1024), ("DF1", 1024), ("ZP", 512), ("ZQ", 512), ("DU", 512), ("MI", 512))})
 SEMAPHORES = ["pe", "dve", "act", "pool", "sent"] + ["m%d" % k for k in range(50)] + ["a%d" % k for k in range(16)]
 
 
-def program(g, T, dests):
+def program(g, T, dests, par=None):
     ops = []
+    F, G, SCAT, _, XFER = par or PARS[0]
+    FPE = F / 2
     nd = [0, 0]
     V_, S_, PE = g.vector, g.scalar, g.tensor
 
@@ -90,16 +93,16 @@ def program(g, T, dests):
     dma(T.V[:, 0:256], T.v0[:], 65536, [], ["V00", "V01"])
     dma(T.wai[:], T.wa[:], 1024, [], ["wai"])
     dma(T.PT[:, 0:W], T.p0[:], 3 * 917504, [], ["PT"])
-    dma(T.D1[:, 0:W], T.d0[:], 4 * 917504, [], ["D1"])
+    dma(T.D1[:, 0:W], T.d0[:], 917504, ["PT"], ["D1"])
     add("pool", 150, lambda: g.iota(T.pi[:, 0:1], [[0, 1]], 0, 1), [], ["pi0"])
     add("pool", 430, iota(T.r144[:], [[1, 144]]), [], ["r144"])
     add("pool", 400, iota(T.rg[:], [[1, 8], [0, 16]]), [], ["rg"])
     add("pool", 400, iota(T.rc[:], [[0, 8], [1, 16]]), [], ["rc"])
     dve(1024, lambda: V_.memset(T.ones[:], 1.0), [], ["ones"])
     add("pool", 4500, lambda: g.affine_select(T.E[:], T.ones[:], [[-1, 128], [0, 16]], A.is_equal, 0.0, 0, 1), ["ones"], ["E"])
-    dve(136, lambda: V_.memset(T.D0[:, W:WX], 0.0), [], ["D0x"])
-    dve(136, lambda: V_.memset(T.D1[:, W:WX], 0.0), [], ["D1x"])
-    dve(272, lambda: V_.memset(T.PT[:, W:WX], 0), [], ["PTx"])
+    dve(264, lambda: V_.memset(T.D0[:, W:WX], 0.0), [], ["D0x"])
+    dve(264, lambda: V_.memset(T.D1[:, W:WX], 0.0), [], ["D1x"])
+    dve(528, lambda: V_.memset(T.PT[:, W:WX], 0), [], ["PTx"])
     dve(512, lambda: V_.memset(T.S0[:], 1.0e9), [], ["S00", "S01", "S10", "S11"])
     dve(64, lambda: V_.memset(T.cst[:], -14.0), [], ["c14"])
     dve(1, ts(T.pi[:, 1:2], T.pi[:, 0:1], 15, A.bitwise_and), ["pi0"], ["pi1"])
@@ -126,9 +129,10 @@ def program(g, T, dests):
     dve(128, ts(T.R8[:], T.rg[:], p_, A.is_equal), ["pf", "rg"], ["R8"])
     dve(128, ts(T.tri[:], T.rc[:], pm, A.is_gt), ["pf", "rc"], ["tri"])
     dve(128, ts(T.mk[:], T.rc[:], pm, A.is_equal), ["pf", "rc"], ["mk"])
-    dve(16, ts(T.dum[:], T.r144[:, 0:16], 16.0, A.mult, pm, A.add), ["pf", "r144"], ["dum0"])
-    dve(16, ts(T.dum[:], T.dum[:], W + 1 - OFF, A.add), ["dum0"], ["dum"])
-    for k, val in ((0, C / 16), (1, -C / 16), (2, W / 16.0), (3, 1 / 16.0), (5, 1.0), (6, 16.0), (7, C)):
+    for h in range(2):
+        dve(1, ts(T.pf[:, 6 + h:7 + h], p_, 2.0, A.mult, W + 2.0 + 256 * h, A.add), ["pf"], ["pf%d" % (6 + h)])
+        dve(64, ts(T.Gd[:, 8 * h:8 * h + 8, :], T.mk[:], T.pf[:, 6 + h:7 + h], A.mult), ["mk", "pf%d" % (6 + h)], ["Gd%d" % h])
+    for k, val in ((0, C / 16), (1, -C / 16), (2, W / 16.0), (3, 1 / 16.0), (5, 1.0), (6, 16.0)):
         dve(8, ts(T.b8[:, 8 * k:8 * k + 8], r8, pg, A.is_equal, val, A.mult), ["pf", "r144"], ["b8%d" % k])
     dve(2, cp(T.waf[:], T.wai[:]), ["wai"], ["waf"])
     dve(8, ts(T.b8[:, 32:40], r8, pg, A.is_equal, T.waf[:, 0:1], A.mult), ["pf", "r144", "waf"], ["b84"])
@@ -148,6 +152,7 @@ def program(g, T, dests):
         dve(128, cp(T.JC[:, 144 * h:144 * h + 128], RR), ["RR"], ["JR" + n], "ZP")
 
     tile = 0
+    DFS = [T.DF0, T.DF1]
     UUS = {}
     for t in range(4):
         last = t == 3
@@ -161,7 +166,7 @@ def program(g, T, dests):
             dve(1, tt(T.aci[:, k:k + 1], T.AC[:, k:k + 1], T.AC[:, k + 1:k + 2], A.add), ["AC%d0" % (t - 1), "AC%d1" % (t - 1)], ["aci%d" % k])
             dve(1, ts(T.aci[:, k + 1:k + 2], T.aci[:, k:k + 1], 3, A.bitwise_and), ["aci%d" % k], ["aci%d" % (k + 1)])
             dve(1, tt(th, T.aci[:, k + 1:k + 2], T.waf[:, 1:2], A.add), ["aci%d" % (k + 1), "waf"], [thn])
-            dma(D[t + 1][:], D[t][:], 987136, Dn, ["D%d" % (t + 1)])
+            dma(D[t + 1][:], D[t][:], 1052672, Dn + ["V%d0" % t], ["D%d" % (t + 1)])
         for h in range(2):
             n, H, s, c0 = "%d%d" % (t, h), str(h), 2 * t + h, 256 * t + 128 * h
             hs, h8 = slice(128 * h, 128 * h + 128), slice(8 * h, 8 * h + 8)
@@ -177,7 +182,11 @@ def program(g, T, dests):
             dve(128 * G, cp(pu, T.PT[:, 0:W].indirect(ju)), ["PT", "JU" + n], ["PU" + n])
             dve(64, ts(pc, pu, -OFF, A.add), ["PU" + n], ["PC" + H])
             for k in range(1, 4):
-                dma(T.PC[:, 512 * h + 128 * k:512 * h + 128 * k + 128], pc, 32768, ["PC" + H], ["P4%s%d" % (H, k)])
+                pk = T.PC[:, 512 * h + 128 * k:512 * h + 128 * k + 128]
+                if s in P4V:
+                    dve(64, ts(pk, pu, -OFF, A.add), ["PU" + n], ["P4%s%d" % (H, k)])
+                else:
+                    dma(pk, pc, 32768, ["PC" + H], ["P4%s%d" % (H, k)])
             EO, en = (T.EA, "EA") if h == 0 else (T.EB, "EB")
             terms, rd = [], ["blkC"]
             if h == 1:
@@ -195,11 +204,10 @@ def program(g, T, dests):
             mm(terms, rd + ens, ["cw"], "MI")
             act(128, ac(wr, cw, AF.Sign, accum_out=T.AC[:, s:s + 1]), ["cw"], ["WR" + n, "AC" + n], "MI")
             wW = T.MI[:, 128 + 8 * h:136 + 8 * h]
-            mm(grp(vTp, [(wr, I0)], 128), ["WR" + n, "I0"], ["vTp"], "ZQ")
-            dve(128, tt(T.Y[:], vTp, T.mk[:], A.mult), ["vTp", "mk"], ["Y"], "ZQ")
-            mm(grp(wW, [(T.cst[:], T.ones[:, 0:8]), (T.Y[:], T.b8[:, 56:64])], 8), ["c14", "ones", "b87", "Y"], ["wW" + H], "MI")
-            dve(8, tt(T.sa[:, h8], wW, T.dum[:, h8], A.min), ["wW" + H, "dum"], ["sa" + H], "MI")
-            dve(8, tt(T.sb[:, h8], T.sa[:, h8], jf, A.max), ["sa" + H, "JF" + n], ["sb" + H])
+            mm(grp(vTp, [(wr, I2C)], 128), ["WR" + n, "I2"], ["vTp"], "ZQ")
+            dve(128, tt(T.Y[:], vTp, T.Gd[:, 8 * h:8 * h + 8, :], A.min), ["vTp", "Gd" + H], ["Y"], "ZQ")
+            mm(grp(wW, [(T.cst[:], T.ones[:, 0:8]), (T.Y[:], T.b8[:, 40:48])], 8), ["c14", "ones", "b85", "Y"], ["wW" + H], "MI")
+            dve(8, tt(T.sb[:, h8], wW, jf, A.max), ["wW" + H, "JF" + n], ["sb" + H], "MI")
             dve(8, ts(so, T.sb[:, h8], OFF, A.add), ["sb" + H], ["SO" + n])
             y0 = 160 + 32 * h
             mm([(T.MI[:, y0:y0 + 24], wr, T.b8[:, 0:24], True, False, 24), (T.MI[:, y0 + 8:y0 + 16], jr, T.b8[:, 24:32], False, False, 8),
@@ -237,14 +245,19 @@ def program(g, T, dests):
                         dve(1024 * G, cp(T.X[:, x0:x0 + 1024], src), Dn + [on], [xn])
                     else:
                         act(1024 * G, ac(T.X[:, x0:x0 + 1024], src, AF.Copy), Dn + [on], [xn])
-                    DF, dn = (T.DF0, "DF0") if u == 0 else (T.DF1, "DF1")
-                    lst = []
-                    for b in range(2):
-                        e0 = 1024 * u + 512 * b
-                        lst += grp(DF[:, 512 * b:512 * b + 512], [(T.VT[:, hs], T.E[:, e0:e0 + 512]), (I0, T.X[:, x0 + 512 * b:x0 + 512 * b + 512])], 512)
-                    mm(lst, [xn, "I0", "VT" + H, "E"], [dn], dn)
+                    slot = [0]
+
+                    def diff(slot=slot, x0=x0, u=u, hs=hs):
+                        DF, ins = DFS[slot[0]], None
+                        for b in range(2):
+                            PE.matmul(DF[:, 512 * b:512 * b + 512], T.VT[:, hs], T.E[:, 1024 * u + 512 * b:1024 * u + 512 * b + 512], True, False)
+                            ins = PE.matmul(DF[:, 512 * b:512 * b + 512], I0, T.X[:, x0 + 512 * b:x0 + 512 * b + 512], False, True)
+                        return ins
+                    add("pe", 60 + 2048 * FPE, diff, [xn, "I0", "VT" + H, "E"], ["df%d" % k])
+                    ops[-1]["take"] = slot
                     ab, an = T.AB[:, 1024 * (k % NAB):1024 * (k % NAB) + 1024], "AB%d" % (k % NAB)
-                    act(1024, ac(ab, DF[:], AF.Abs), [dn], [an], dn)
+                    act(1024, lambda slot=slot, ab=ab: S_.activation(ab, DFS[slot[0]][:], AF.Abs), ["df%d" % k], [an])
+                    ops[-1]["give"] = len(ops) - 2
                     f0 = 1024 * (k % NFL)
                     dve(512, ts(T.FL[:, f0:f0 + 1024], ab, th, A.is_lt, 15.0 / 32, A.add), [an, thn], ["FL%d" % (k % NFL)])
                 f0, g0 = f0 - 1024, 256 * h + 128 * (1 - kind)
@@ -320,45 +333,128 @@ def program(g, T, dests):
 
 def schedule(ops, deps0, succ, pr):
     n = len(ops)
-    deps = [set(d) for d in deps0]
-    left = [len(d) for d in deps]
+    left = [len(d) for d in deps0]
     ready = {k: 0.0 for k in range(n) if left[k] == 0}
-    free, done, bank, order, t0 = {}, [0.0] * n, {}, [], [0.0] * n
+    free, done, bank, order = {}, [0.0] * n, {}, []
+    held, slot = [None, None], {}
     while ready:
         st = {}
         for k, s in ready.items():
             o = ops[k]
+            if "take" in o:
+                c = [done[d] + HOPNS if d is not None else 0.0 for d in held if d != -1]
+                if not c:
+                    continue
+                s = max(s, min(c))
             s = max(s, free.get(o["eng"], 0.0))
             for b in o["banks"]:
                 for e, d in bank.get(b, {}).items():
                     if e != o["eng"]:
                         s = max(s, done[d] + HOPNS)
             st[k] = s
-        k0 = min(ready, key=lambda k: (st[k], -pr[k]))
+        k0 = min(st, key=lambda k: (st[k], -pr[k]))
         e0 = ops[k0]["eng"]
-        k = max([x for x in ready if ops[x]["eng"] == e0 and st[x] <= st[k0] + WIN], key=lambda x: (pr[x], -x))
+        k = max([x for x in st if ops[x]["eng"] == e0 and st[x] <= st[k0] + WIN], key=lambda x: (pr[x], -x))
         o = ops[k]
         for b in o["banks"]:
-            for e, d in bank.setdefault(b, {}).items():
-                if e != o["eng"]:
-                    deps[k].add(d)
-            bank[b][o["eng"]] = k
+            bank.setdefault(b, {})[e0] = k
+        if "take" in o:
+            i = min([i for i in range(2) if held[i] != -1], key=lambda i: done[held[i]] if held[i] is not None else 0.0)
+            held[i], slot[k] = -1, i
+        if "give" in o:
+            held[slot[o["give"]]] = k
         free[e0] = st[k] + o["dur"]
         done[k] = st[k] + o["dur"] + o["lat"]
-        t0[k] = st[k]
         order.append(k)
         del ready[k]
         for x in succ[k]:
             left[x] -= 1
             if left[x] == 0:
                 ready[x] = max(done[d] for d in deps0[x]) + HOPNS
-    return order, deps, max(done), t0
+    return order
+
+
+def replay(r, alt):
+    tot = 0.0
+    for (o2, hop, scale) in alt:
+        free, done = {}, {}
+        for k in r[0]:
+            eng, dur, lat = o2[k]
+            s = free.get(eng, 0.0)
+            for d in r[1][k]:
+                if done[d] + hop > s:
+                    s = done[d] + hop
+            free[eng] = s + dur
+            done[k] = s + dur + lat
+        tot += max(done.values()) / scale
+    return tot
+
+
+def decode(ops, deps0, order):
+    deps, bank, held, slot, used = {}, {}, [None, None], {}, [0, 0]
+    for j, k in enumerate(order):
+        o = ops[k]
+        d = deps0[k]
+        if o["banks"] or "take" in o:
+            d = list(d)
+            for b in o["banks"]:
+                m = bank.setdefault(b, {})
+                d += [x for e, x in m.items() if e != o["eng"]]
+                m[o["eng"]] = k
+            if "take" in o:
+                c = [i for i in (0, 1) if held[i] != -1]
+                if not c:
+                    return None
+                i = min(c, key=lambda i: used[i])
+                if held[i] is not None:
+                    d.append(held[i])
+                held[i], slot[k] = -1, i
+        if "give" in o:
+            held[slot[o["give"]]] = k
+            used[slot[o["give"]]] = j
+        deps[k] = d
+    return order, deps, slot
+
+
+def refine(ops, deps0, cur, alt):
+    n = len(ops)
+    val = replay(cur, alt)
+    best, bval, x = cur, val, SEED
+    for it in range(MOVES):
+        order = cur[0]
+        x = (x * 1103515245 + 12345) % 2147483648
+        j = (x >> 8) % n
+        k = order[j]
+        e = ops[k]["eng"]
+        x = (x * 1103515245 + 12345) % 2147483648
+        hops, i = 1 + (x >> 10) % 3, j
+        while hops and i > 0:
+            i -= 1
+            if ops[order[i]]["eng"] == e:
+                hops -= 1
+        if hops:
+            continue
+        need, seg = {k}, order[i:j + 1]
+        for y in reversed(seg):
+            if y in need:
+                need.update(deps0[y])
+        if order[i] in need:
+            continue
+        r = decode(ops, deps0, order[:i] + [y for y in seg if y in need] + [y for y in seg if y not in need] + order[j + 1:])
+        if r is None:
+            continue
+        v_ = replay(r, alt)
+        if v_ <= val + TEMP * (1 - it / MOVES) * ((x >> 14) % 100) / 100.0:
+            cur, val = r, v_
+            if v_ < bval:
+                best, bval = r, v_
+    return best
 
 
 PLANS = {}
 
 
-def plan(ops):
+def plan(ops, others=()):
     n = len(ops)
     if n not in PLANS:
         wr, rd, deps = {}, {}, []
@@ -371,7 +467,7 @@ def plan(ops):
             for x in o["w"]:
                 wr[x] = k
                 rd[x] = []
-            deps.append(d)
+            deps.append(sorted(d))
         succ = [[] for _ in range(n)]
         for k in range(n):
             for d in deps[k]:
@@ -380,31 +476,33 @@ def plan(ops):
         for k in range(n - 1, -1, -1):
             pr[k] = ops[k]["dur"] + ops[k]["lat"] + max([pr[x] + HOPNS for x in succ[k]] + [0.0])
         pr = [pr[k] - k * MIX for k in range(n)]
-        best = schedule(ops, deps, succ, pr)
+        best = decode(ops, deps, schedule(ops, deps, succ, pr))
+        alt = [([(o["eng"], o["dur"], o["lat"]) for o in o2], p[3], p[0] * (1 + p[1] / 4)) for o2, p in zip([ops] + list(others), PARS)]
+        val = replay(best, alt)
         kinds = sorted(set(o["eng"] + o["w"][0].rstrip("0123456789") for o in ops))
         kind = [kinds.index(o["eng"] + o["w"][0].rstrip("0123456789")) for o in ops]
         x = SEED
         for it in range(ITER):
             q = list(pr)
-            for _ in range(2 if it < ITER * 0.7 else 30):
+            for _ in range(2):
                 x = (x * 1103515245 + 12345) % 2147483648
-                c = x >> 8
+                c = (x >> 8) % len(kinds)
                 x = (x * 1103515245 + 12345) % 2147483648
                 a = ((x >> 8) % 2001 - 1000) * AMP
-                if it < ITER * 0.7:
-                    for k in range(n):
-                        if kind[k] == c % len(kinds):
-                            q[k] += a
-                else:
-                    q[c % n] += a / 3
-            r = schedule(ops, deps, succ, q)
-            if r[2] <= best[2]:
-                best, pr = r, q
-        PLANS[n] = best
-    best = PLANS[n]
-    for k in range(n):
-        ops[k]["t0"] = best[3][k]
-    return best[:3]
+                for k in range(n):
+                    if kind[k] == c:
+                        q[k] += a
+            r = decode(ops, deps, schedule(ops, deps, succ, q))
+            v_ = replay(r, alt)
+            if v_ <= val:
+                best, pr, val = r, q, v_
+        PLANS[n] = refine(ops, deps, best, alt)
+    order, deps, slot = PLANS[n]
+    for j, k in enumerate(order):
+        ops[k]["t0"] = j
+    for k, i in slot.items():
+        ops[k]["take"][0] = i
+    return order, deps, 0.0
 
 
 def rank_program(g, core, T, topo):
@@ -418,18 +516,19 @@ def rank_program(g, core, T, topo):
             rid, pid, _ = topo.addr(dst)
             dests[t] = (rid, pid, topo.mask(core, dst), len(topo.engines(core, dst)))
     ops = program(g, T, dests)
-    order, deps, _ = plan(ops)
+    order, deps, _ = plan(ops, [program(g, T, dests, p) for p in PARS[1:]])
     queue = {"pe": g.tensor, "dve": g.vector, "act": g.scalar, "pool": g, "sp": g.sync}
-    count, mark, known, sent = {}, {}, {}, 0
+    count, mark, known, place, waited, sent = {}, {}, {}, {}, {}, 0
     seen = {e: {} for e in queue}
     for k in order:
         o = ops[k]
         e = o["eng"]
-        for d in sorted(deps[k], key=lambda d: -ops[d]["t0"]):
+        for d in sorted(set(deps[k]), key=lambda d: -ops[d]["t0"]):
             sem, val = mark[d]
             if not (sem == "pe" and e == "pe") and seen[e].get(sem, 0) < val:
                 queue[e].wait_ge(T.sem[sem], val)
                 seen[e][sem] = val
+                waited[sem] = max(waited.get(sem, 0), val)
                 for s_, v_ in known[d].items():
                     if seen[e].get(s_, 0) < v_:
                         seen[e][s_] = v_
@@ -446,6 +545,8 @@ def rank_program(g, core, T, topo):
                 sent += o["cnt"]
             count[o["sem"]] = o["cnt"]
             mark[k] = (o["sem"], o["cnt"])
+        place[mark[k][0]] = o["t0"]
     g.wait_ge(T.sem.sent, sent)
-    for sem, val in count.items():
-        g.wait_ge(T.sem[sem], val)
+    for sem in sorted(count, key=lambda s_: place[s_]):
+        if waited.get(sem, 0) < count[sem]:
+            g.wait_ge(T.sem[sem], count[sem])

@@ -1,17 +1,30 @@
-from concourse.mybir import AluOpType, ActivationFunctionType
+from concourse.mybir import AluOpType, ActivationFunctionType, AxisListType
 
 A = AluOpType
 AF = ActivationFunctionType
 W = 3584
 WX = 4112
+ZONE = 260
 OFF = 1792.0
-C = 8192.0
+B = 4096.0
+BIG = 1.5 * 2.0 ** 23
 HOP = (1, 0, 2, 0)
-DVE_TILES = (1, 5, 11, 19, 27, 30)
-P4V = (0,)
-NX, NAB, NFL = 8, 8, 8
-PARS = [(1.0, 1.56, 3.8, 140.0, 3300.0), (0.85, 1.2, 2.5, 200.0, 4000.0), (1.2, 1.95, 5.0, 100.0, 2800.0), (1.15, 1.2, 4.5, 140.0, 3300.0)]
-HOPNS, MIX, WIN, ITER, SEED, AMP, MOVES, TEMP = 140.0, 250.0, 100.0, 1200, 1, 10.0, 14000, 60.0
+DVE_TILES = (2,)
+X_FIRST, V_FIRST = (8, 16, 24), ()
+HALF_PAIRS = ()
+Q_LAST = ()
+HALF_TILES = range(3, 32, 4)
+ACT_FLAGS = (0, 4, 22)
+EARLY = (0, 2, 4)
+SPLIT_SG = (0, 1)
+ON_ACT = ("FS", "JR", "TO", "QC", "YJ", "DS")
+MERGE = 2
+LW = 528
+PU_ACT = (0, 1, 3, 5, 7)
+NX, NAB, NFL = 8, 4, 8
+PARS = [(0.85, 1.56, 3.8, 90.0, 3300.0), (0.9, 1.15, 2.2, 150.0, 4000.0), (1.2, 1.9, 5.0, 100.0, 2800.0)]
+MEAN, FREE = 1.0, 3
+HOPNS, MIX, WIN, ITER, SEED, AMP, MOVES, TEMP = 100.0, 50.0, 100.0, 100, 5, 10.0, 50000, 500.0
 
 
 def _sb(d, **kw):
@@ -19,16 +32,18 @@ def _sb(d, **kw):
 
 
 SCRATCH = {}
-SCRATCH.update(_sb("bfloat16", D0=WX, D1=WX, D2=WX, D3=WX, D4=WX, V=1280, VO=1024, X=NX * 1024, AB=NAB * 1024, FL=NFL * 1024,
-                   DUF=4096, EA=(8, 128), EB=(8, 128), EC=(8, 128), WR=1024, SG=512, VT=256, DJ=256, ND=256, DV=256, RL=256,
-                   ones=2048, E=2048, ID=11 * 128, blk=256, REP=2048, BW=144, R8=128, tri=(8, 16), mk=(8, 16), cst=128, b8=64))
-SCRATCH.update(_sb("float16", QC=1280, QO=1024, JC=8 * 144, JO=8 * 144, PC=1024, LS=16, Y=128, Gd=(16, 16), F8=256, cm=24))
-SCRATCH.update(_sb("int32", PT=WX, q0i=256, j0i=16, wai=2, aci=8, hi=32, mi=16, pi=4))
-SCRATCH.update(_sb("uint16", QU=1024, PU=1024, UU=1024, JU=64, FU=64, SO=64))
-SCRATCH.update(_sb("float32", waf=2, JF=64, sb=16, AC=8, TH=4, TQ=256, TP=128, S0=512, SC=256, YQ=256, YJ=256,
-                   pf=8, r144=144, rg=128, rc=(8, 16), m16=16))
-SCRATCH.update({k: ("psum", [128, n], "float32") for k, n in (("DF0", 1024), ("DF1", 1024), ("ZP", 512), ("ZQ", 512), ("DU", 512), ("MI", 512))})
-SEMAPHORES = ["pe", "dve", "act", "pool", "sent"] + ["m%d" % k for k in range(50)] + ["a%d" % k for k in range(16)]
+SCRATCH.update(_sb("bfloat16", D0=WX, D1=WX, D2=WX, D3=WX, D4=WX, V=1280, X=NX * 1024, AB=NAB * 1024, FL=NFL * 1024,
+                   AN=2048, EA=(8, 128), EB=(8, 128), EC=(8, 128), WR=1024, SG=512, DJ=256, ND=256, RL=512,
+                   ones=528, E=2048, ID=10 * 128, blk=384, C3=(8, 32), M=16 * 128, MN=9 * 128, Bs=256, BW2=144, BW4=144, R4=512,
+                   mk2=128, b8=8, bv=24, bw=24, bj=24))
+SCRATCH.update(_sb("float16", LN=10 * LW, LO=6 * LW, NF=2048, TB=512, LS=112, FS=64, Y0=256, VT=256, DS=512,
+                   cm=24, SP=32, d16=64))
+SCRATCH.update(_sb("int32", PT=WX, q0i=256, j0i=16, wai=2, aci=8, pi=4))
+SCRATCH.update(_sb("uint16", QU=1280, PU=1024, UL=1024, JU=64, FU=64, SO=64))
+SCRATCH.update(_sb("float32", waf=2, JF=64, sb=64, AC=8, U2=4, RS=4, S2=4, S0=512, SC=512, UF=256, TO=256, YJ=256, kk=32, rr=16,
+                   pf=12, r144=144, rg=128, rc=128, r4=512, m16=16, pw=48))
+SCRATCH.update({k: ("psum", [128, n], "float32") for k, n in (("DF0", 1024), ("DF1", 1024), ("ZP", 512), ("ZQ", 512), ("KT", 512), ("MI", 512))})
+SEMAPHORES = ["pe", "dve", "act", "pool", "sent"] + ["m%d" % k for k in range(30)] + ["a%d" % k for k in range(16)]
 
 
 def program(g, T, dests, par=None):
@@ -37,9 +52,15 @@ def program(g, T, dests, par=None):
     FPE = F / 2
     nd = [0, 0]
     V_, S_, PE = g.vector, g.scalar, g.tensor
+    tag = [""]
 
     def add(eng, dur, fn, r, w, banks=(), sem=None, lat=0.0, cnt=0):
-        ops.append({"eng": eng, "dur": dur, "fn": fn, "r": list(r), "w": list(w), "banks": banks, "sem": sem, "lat": lat, "cnt": cnt})
+        ops.append({"eng": eng, "dur": dur, "fn": fn, "r": list(r), "w": list(w), "banks": banks, "sem": sem, "lat": lat, "cnt": cnt,
+                    "tag": tag[0]})
+
+    def lend(what, slot=None):
+        ops[-2]["take"] = (what, slot or [0])
+        ops[-1]["give"] = len(ops) - 2
 
     def dve(n, fn, r, w, *banks):
         add("dve", 55 + max(n, 16) * F, fn, r, w, banks)
@@ -47,13 +68,16 @@ def program(g, T, dests, par=None):
     def act(n, fn, r, w, *banks):
         add("act", 70 + max(n, 16) * F, fn, r, w, banks)
 
+    def pool(base, n, fn, r, w):
+        add("pool", base + 2 * n * F, fn, r, w)
+
     def mm(lst, r, w, *banks):
         def fn():
             ins = None
             for (o, a, b, s0, s1, n) in lst:
                 ins = PE.matmul(o, a, b, s0, s1)
             return ins
-        add("pe", 60 + sum(max(64, x[5]) for x in lst) * FPE, fn, r, w, banks)
+        add("pe", 60 + sum(x[5] for x in lst) * FPE, fn, r, w, banks)
 
     def grp(out, terms, n):
         return [(out, a, b, k == 0, k == len(terms) - 1, n) for k, (a, b) in enumerate(terms)]
@@ -80,11 +104,20 @@ def program(g, T, dests, par=None):
     def cp(out, a):
         return lambda: V_.tensor_copy(out, a)
 
+    def ms(out, c):
+        return lambda: V_.memset(out, c)
+
     def ac(out, a, f, **kw):
         return lambda: S_.activation(out, a, f, **kw)
 
     def iota(out, pat):
         return lambda: g.iota(out, pat, 0, 0, allow_small_or_imprecise_dtypes=True)
+
+    def affine(what, n, out, a, scale, bias, r, w, *banks):
+        if what in ON_ACT:
+            act(n, ac(out, a, AF.Identity, bias=bias, scale=scale) if bias else ac(out, a, AF.Copy, scale=scale), r, w, *banks)
+        else:
+            dve(n, ts(out, a, scale, A.mult, bias, A.add), r, w, *banks)
 
     D = [T.D0, T.D1, T.D2, T.D3, T.D4]
     dma(T.q0i[:], T.q0[:], 131072, [], ["q0i"])
@@ -93,242 +126,363 @@ def program(g, T, dests, par=None):
     dma(T.V[:, 0:256], T.v0[:], 65536, [], ["V00", "V01"])
     dma(T.wai[:], T.wa[:], 1024, [], ["wai"])
     dma(T.PT[:, 0:W], T.p0[:], 3 * 917504, [], ["PT"])
-    dma(T.D1[:, 0:W], T.d0[:], 917504, ["PT"], ["D1"])
+    dve(W / 2, cp(T.D1[:, 0:W], T.D0[:, 0:W]), ["D0"], ["D1"])
     add("pool", 150, lambda: g.iota(T.pi[:, 0:1], [[0, 1]], 0, 1), [], ["pi0"])
-    add("pool", 430, iota(T.r144[:], [[1, 144]]), [], ["r144"])
-    add("pool", 400, iota(T.rg[:], [[1, 8], [0, 16]]), [], ["rg"])
-    add("pool", 400, iota(T.rc[:], [[0, 8], [1, 16]]), [], ["rc"])
-    dve(1024, lambda: V_.memset(T.ones[:], 1.0), [], ["ones"])
-    add("pool", 4500, lambda: g.affine_select(T.E[:], T.ones[:], [[-1, 128], [0, 16]], A.is_equal, 0.0, 0, 1), ["ones"], ["E"])
-    dve(264, lambda: V_.memset(T.D0[:, W:WX], 0.0), [], ["D0x"])
-    dve(264, lambda: V_.memset(T.D1[:, W:WX], 0.0), [], ["D1x"])
-    dve(528, lambda: V_.memset(T.PT[:, W:WX], 0), [], ["PTx"])
-    dve(512, lambda: V_.memset(T.S0[:], 1.0e9), [], ["S00", "S01", "S10", "S11"])
-    dve(64, lambda: V_.memset(T.cst[:], -14.0), [], ["c14"])
+    pool(130, 144, iota(T.r144[:], [[1, 144]]), [], ["r144"])
+    pool(130, 128, iota(T.rg[:], [[1, 8], [0, 16]]), [], ["rg"])
+    pool(130, 128, iota(T.rc[:], [[0, 8], [1, 16]]), [], ["rc"])
+    dve(264, ms(T.ones[:], 1.0), [], ["ones"])
+    dve(128, ms(T.Bs[:], B), [], ["Bs"])
+    dve(1024, ms(T.AN[:], 0.0), [], ["AN0", "AN1"])
+    pool(170, 2048, lambda: g.affine_select(T.E[:], T.AN[:], [[-1, 128], [0, 16]], A.not_equal, -1.0, 0, 1), ["AN0", "AN1"], ["E"])
+    pool(170, 256, lambda: g.affine_select(T.C3[:], T.Bs[:], [[-16, 8], [0, 2], [-1, 16]], A.is_equal, 0.0, 0, 1), ["Bs"], ["C3"])
+    M = [T.M[:, 128 * k:128 * k + 128] for k in range(16)]
+    MN = [T.MN[:, 128 * k:128 * k + 128] for k in range(9)]
+    for k in range(1, 16):
+        pool(170, 128, lambda k=k: g.affine_select(M[k], T.C3[:, :, k:k + 16], [[-1, 128]], A.not_equal, B, 0, 1), ["C3"], ["M%d" % k])
+        if k <= 8:
+            act(128, ac(MN[k], M[k], AF.Copy, scale=-1.0), ["M%d" % k], ["MN%d" % k])
+    pool(130, 512, iota(T.r4[:], [[1, 32], [0, 16]]), [], ["r4"])
+    pool(130, WX - W, lambda: g.iota(T.PT[:, W:WX], [[0, WX - W]], 0, 0), [], ["PTx"])
+    for t in range(5):
+        act(WX - W, ac(D[t][:, W:WX], T.ones[:, 0:WX - W], AF.Copy, scale=0.0), ["ones"], ["D%dx" % t])
+    dve(512, ms(T.S0[:], 1.0e9), [], ["S00", "S01"])
+    dve(32, ms(T.kk[:], 0.0), [], ["kk0", "kk1"])
+    dve(56, ts(T.LS[:], T.ones[:, 0:112], 0.0, A.mult), ["ones"], ["LS0", "LS1"])
     dve(1, ts(T.pi[:, 1:2], T.pi[:, 0:1], 15, A.bitwise_and), ["pi0"], ["pi1"])
     dve(1, ts(T.pi[:, 2:3], T.pi[:, 0:1], 4, A.arith_shift_right), ["pi0"], ["pi2"])
     dve(1, cp(T.pf[:, 0:3], T.pi[:, 0:3]), ["pi0", "pi1", "pi2"], ["pf"])
     p_, pm, pg = T.pf[:, 0:1], T.pf[:, 1:2], T.pf[:, 2:3]
     r8 = T.r144[:, 0:8]
-    dve(1, ts(T.pf[:, 4:5], p_, 16.0, A.mult, 15.0, A.add), ["pf"], ["pf4"])
-    dve(1, ts(T.pf[:, 5:6], pg, -8192.0, A.mult, 7 * 8192.0 + OFF + C / 2, A.add), ["pf"], ["pf5"])
-    I0, In, I2C, I16, Iw, IR, InC, Io, Ip, Ih, Inh = [T.ID[:, 128 * k:128 * k + 128] for k in range(11)]
+    I0, In, I16, Iwp, Iwn, Io, Ip, Ih, Inh, Ib = [T.ID[:, 128 * k:128 * k + 128] for k in range(10)]
     dve(128, ts(I0, T.r144[:, 0:128], p_, A.is_equal), ["pf", "r144"], ["I0"])
-    for k, val in ((1, -1.0), (2, 2 * C), (3, -16.0), (4, -2048.0), (6, -C), (7, -OFF), (8, OFF), (9, C / 2), (10, -C / 2)):
-        dve(64, ts(T.ID[:, 128 * k:128 * k + 128], I0, val, A.mult), ["I0"], ["I%d" % k])
-    dve(64, ts(IR, I0, T.pf[:, 5:6], A.mult), ["I0", "pf5"], ["I5"])
-    blkC = T.blk[:, 128:256]
-    dve(128, ts(T.blk[:, 0:128], T.rg[:], pg, A.is_equal), ["pf", "rg"], ["blk"])
-    dve(64, ts(blkC, T.blk[:, 0:128], C, A.mult), ["blk"], ["blkC"])
+    for k, val in ((1, -1.0), (2, -16.0), (3, 1024.0), (4, -1024.0), (5, -OFF), (6, OFF), (7, B), (8, -B), (9, -B / 2)):
+        act(128, ac(T.ID[:, 128 * k:128 * k + 128], I0, AF.Copy, scale=val), ["I0"], ["I%d" % k])
+    IRp, IRq = M[0], MN[0]
+    for k, (dst, c) in enumerate(((IRp, B), (IRq, 2 * B))):
+        dve(1, ts(T.pf[:, 4 + k:5 + k], pg, -4 * B, A.mult, 28 * B + c, A.add), ["pf"], ["pf%d" % (4 + k)])
+        act(128, ac(dst, I0, AF.Copy, scale=T.pf[:, 4 + k:5 + k]), ["I0", "pf%d" % (4 + k)], ["IR%d" % k])
+    blk, blkC, blkW = T.blk[:, 0:128], T.blk[:, 128:256], T.blk[:, 256:384]
+    dve(128, ts(blk, T.rg[:], pg, A.is_equal), ["pf", "rg"], ["blk"])
+    act(128, ac(blkC, blk, AF.Copy, scale=131072.0), ["blk"], ["blkC"])
     dve(16, ts(T.m16[:], T.r144[:, 0:16], pm, A.is_equal), ["pf", "r144"], ["m16"])
-    rep = [T.REP[:, 128 * i:128 * i + 128] for i in range(16)]
-    REPS = ["REP%d" % i for i in range(16)]
-    for i in range(16):
-        dve(64, ts(rep[i], T.blk[:, 0:128], T.m16[:, i:i + 1], A.mult), ["blk", "m16"], [REPS[i]])
-    dve(144, ts(T.BW[:], T.r144[:], T.pf[:, 4:5], A.is_equal), ["pf4", "r144"], ["BW"])
-    dve(128, ts(T.R8[:], T.rg[:], p_, A.is_equal), ["pf", "rg"], ["R8"])
-    dve(128, ts(T.tri[:], T.rc[:], pm, A.is_gt), ["pf", "rc"], ["tri"])
-    dve(128, ts(T.mk[:], T.rc[:], pm, A.is_equal), ["pf", "rc"], ["mk"])
-    for h in range(2):
-        dve(1, ts(T.pf[:, 6 + h:7 + h], p_, 2.0, A.mult, W + 2.0 + 256 * h, A.add), ["pf"], ["pf%d" % (6 + h)])
-        dve(64, ts(T.Gd[:, 8 * h:8 * h + 8, :], T.mk[:], T.pf[:, 6 + h:7 + h], A.mult), ["mk", "pf%d" % (6 + h)], ["Gd%d" % h])
-    for k, val in ((0, C / 16), (1, -C / 16), (2, W / 16.0), (3, 1 / 16.0), (5, 1.0), (6, 16.0)):
-        dve(8, ts(T.b8[:, 8 * k:8 * k + 8], r8, pg, A.is_equal, val, A.mult), ["pf", "r144"], ["b8%d" % k])
+    dve(16, ms(T.pw[:, 0:16], 0.5), [], ["pw0"])
+    dve(16, lambda: V_.tensor_tensor_scan(T.pw[:, 16:32], T.pw[:, 0:16], T.ones[:, 0:16], 65536.0, A.mult, A.mult), ["pw0", "ones"], ["pw1"])
+    dve(32, tt(T.pw[:, 32:48], T.pw[:, 16:32], T.m16[:], A.mult), ["pw1", "m16"], ["pw2"])
+    dve(16, lambda: V_.tensor_reduce(T.pf[:, 6:7], T.pw[:, 32:48], AxisListType.X, A.add), ["pw2"], ["pf6"])
+    act(128, ac(blkW, blk, AF.Copy, scale=T.pf[:, 6:7]), ["blk", "pf6"], ["blkW"])
+    dve(128, ts(T.mk2[:], T.rc[:], pm, A.is_equal, -2.0, A.mult), ["pf", "rc"], ["mk2"])
+    dve(1, ts(T.pf[:, 7:8], pm, 0.0, A.is_equal, p_, A.mult), ["pf"], ["pf7"])
+    dve(1, ts(T.pf[:, 8:9], pm, -200.0, A.mult, T.pf[:, 7:8], A.add), ["pf", "pf7"], ["pf8"])
+    dve(144, ts(T.BW2[:, 15:144], T.r144[:, 0:129], T.pf[:, 8:9], A.is_equal, 2304.0, A.mult), ["pf8", "r144"], ["BW2"])
+    dve(8, ms(T.BW2[:, 0:15], 0.0), [], ["BW2a"])
+    dve(1, ts(T.pi[:, 3:4], T.pi[:, 0:1], 3, A.arith_shift_right), ["pi0"], ["pi3"])
+    dve(1, ts(T.pf[:, 9:10], T.pi[:, 3:4], -127.0, A.mult, 12.0, A.add), ["pi3"], ["pf9"])
+    dve(1, ts(T.pf[:, 10:11], p_, 16.0, A.mult, T.pf[:, 9:10], A.add), ["pf", "pf9"], ["pf10"])
+    dve(144, ts(T.BW4[:], T.r144[:], T.pf[:, 10:11], A.is_equal), ["pf10", "r144"], ["BW4"])
+    dve(512, ts(T.R4[:], T.r4[:], p_, A.is_equal), ["pf", "r4"], ["R4"])
+    for z in range(2):
+        dve(1, ts(T.pf[:, 11:12], pm, W + ZONE * z + 2.0 - OFF - 2304.0, A.add), ["pf"], ["pf11"])
+        dve(16, ts(T.SP[:, 16 * z:16 * z + 16], T.r144[:, 0:16], 16.0, A.mult, T.pf[:, 11:12], A.add), ["r144", "pf11"], ["SP%d" % z])
+    dve(8, ts(T.b8[:], r8, pg, A.is_equal), ["pf", "r144"], ["b8"])
     dve(2, cp(T.waf[:], T.wai[:]), ["wai"], ["waf"])
-    dve(8, ts(T.b8[:, 32:40], r8, pg, A.is_equal, T.waf[:, 0:1], A.mult), ["pf", "r144", "waf"], ["b84"])
-    for k, (m_, a_) in enumerate(((-64.0, 480.0), (-64.0, 558.0), (0.0, -14.0))):
-        dve(8, ts(T.cm[:, 8 * k:8 * k + 8], r8, m_, A.mult, a_, A.add), ["r144"], ["cm%d" % k])
+    for buf, nm in ((T.bv, "bv"), (T.bw, "bw"), (T.bj, "bj")):
+        dve(12, ms(buf[:], 0.0), [], [nm])
+    dve(8, ts(T.bv[:, 0:16:2], T.b8[:], T.waf[:, 0:1], A.mult), ["b8", "waf"], ["bv"])
+    dve(8, ts(T.bv[:, 16:24], T.b8[:], T.waf[:, 0:1], A.mult), ["b8", "waf"], ["bv"])
+    dve(8, ts(T.bw[:, 1:16:2], T.b8[:], -384.0, A.mult), ["b8"], ["bw"])
+    dve(8, ts(T.bj[:, 1:16:2], T.b8[:], 1 / 16.0, A.mult), ["b8"], ["bj"])
+    for k, (dst, m_, a_) in enumerate(((T.cm[:, 0:16:2], -128.0, 914.0), (T.cm[:, 1:16:2], -128.0, 912.0), (T.cm[:, 16:24], 0.0, -511.5 / 128))):
+        dve(8, ts(dst, r8, m_, A.mult, a_, A.add), ["r144"], ["cm%d" % k])
+    dve(1, ts(T.pf[:, 3:4], T.waf[:, 1:2], 2.0, A.mult, -1.0, A.add), ["waf"], ["a2"])
     ones128 = T.ones[:, 0:128]
-    zP, scA, RR = T.ZP[:, 0:128], T.ZP[:, 128:256], T.ZP[:, 384:512]
-    zQ, vTp, zT = T.ZQ[:, 0:128], T.ZQ[:, 128:256], T.ZQ[:, 256:384]
+    zPA, US, RR = T.ZP[:, 0:256], T.ZP[:, 256:384], T.ZP[:, 384:512]
+    vTp, xW = T.ZQ[:, 128:256], T.ZQ[:, 336:352]
+    XU = T.KT[:, 256:384]
     cw, penP, penQ = T.MI[:, 0:128], T.MI[:, 256:384], T.MI[:, 384:512]
     for h in range(2):
         n = "0%d" % h
-        jw = T.JC[:, 144 * h + 128:144 * h + 136]
         dve(128, cp(T.QU[:, 128 * h:128 * h + 128], T.q0i[:, 128 * h:128 * h + 128]), ["q0i"], ["QU" + n])
-        dve(128, ts(T.QC[:, 128 * h:128 * h + 128], T.q0i[:, 128 * h:128 * h + 128], -OFF, A.add), ["q0i"], ["QC" + n])
-        dve(8, ts(jw, T.j0i[:, 8 * h:8 * h + 8], -OFF, A.add), ["j0i"], ["JW" + n])
-        mm([(T.ZP[:, 384 + c:512:16], rep[c], jw, True, True, 8) for c in range(16)], REPS + ["JW" + n], ["RR"], "ZP")
-        dve(128, cp(T.JC[:, 144 * h:144 * h + 128], RR), ["RR"], ["JR" + n], "ZP")
+        dve(128, ts(T.LN[:, LW * h + 128:LW * h + 256], T.q0i[:, 128 * h:128 * h + 128], -OFF, A.add), ["q0i"], ["QC" + n])
 
-    tile = 0
     DFS = [T.DF0, T.DF1]
-    UUS = {}
     for t in range(4):
         last = t == 3
-        Dn = ["D%d" % t] + (["D%dx" % t] if t < 2 else [])
-        Dw = D[t][:, 0:WX]
+        Dn, Dw = "D%d" % t, D[t][:, 0:W]
+        tag[0] = "s%d" % t
+        u2, rs, s2, ds = T.U2[:, t:t + 1], T.RS[:, t:t + 1], T.S2[:, t:t + 1], T.DS[:, 128 * t:128 * t + 128]
         if t == 0:
-            th, thn = T.waf[:, 1:2], "waf"
+            u2, un_ = T.pf[:, 3:4], "a2"
         else:
-            th, thn = T.TH[:, t:t + 1], "TH%d" % t
-            k = 2 * (t - 1)
+            un_, k = "U2%d" % t, 2 * (t - 1)
             dve(1, tt(T.aci[:, k:k + 1], T.AC[:, k:k + 1], T.AC[:, k + 1:k + 2], A.add), ["AC%d0" % (t - 1), "AC%d1" % (t - 1)], ["aci%d" % k])
-            dve(1, ts(T.aci[:, k + 1:k + 2], T.aci[:, k:k + 1], 3, A.bitwise_and), ["aci%d" % k], ["aci%d" % (k + 1)])
-            dve(1, tt(th, T.aci[:, k + 1:k + 2], T.waf[:, 1:2], A.add), ["aci%d" % (k + 1), "waf"], [thn])
-            dma(D[t + 1][:], D[t][:], 1052672, Dn + ["V%d0" % t], ["D%d" % (t + 1)])
+            dve(1, ts(T.aci[:, k + 1:k + 2], T.aci[:, k:k + 1], 1, A.arith_shift_right, 3, A.bitwise_and), ["aci%d" % k], ["aci%d" % (k + 1)])
+            dve(1, ts(u2, T.aci[:, k + 1:k + 2], 2.0, A.mult, T.pf[:, 3:4], A.add), ["aci%d" % (k + 1), "a2"], [un_])
+            dma(D[t + 1][:, 0:W], D[t][:, 0:W], 917504, [Dn] + (["DV%d0" % t] if HOP[t - 1] else []), ["D%d" % (t + 1)])
+        dve(190, lambda rs=rs, u2=u2: V_.reciprocal(rs, u2), [un_], ["RS%d" % t])
+        if "DS" in ON_ACT:
+            act(128, ac(ds, I0, AF.Copy, scale=rs), ["I0", "RS%d" % t], ["DS%d" % t])
+        else:
+            dve(64, ts(ds, I0, rs, A.mult), ["I0", "RS%d" % t], ["DS%d" % t])
+        dve(1, ts(s2, u2, 0.0, A.is_gt, BIG, A.mult), [un_], ["S2%d" % t])
         for h in range(2):
             n, H, s, c0 = "%d%d" % (t, h), str(h), 2 * t + h, 256 * t + 128 * h
-            hs, h8 = slice(128 * h, 128 * h + 128), slice(8 * h, 8 * h + 8)
-            qc, v, pu, wr = [b[:, c0:c0 + 128] for b in (T.QC, T.V, T.PU, T.WR)]
-            jr, jw = T.JC[:, 144 * s:144 * s + 128], T.JC[:, 144 * s + 128:144 * s + 136]
-            ju, jf, fu, so = [b[:, 8 * s:8 * s + 8] for b in (T.JU, T.JF, T.FU, T.SO)]
-            pc = T.PC[:, 512 * h:512 * h + 128]
-            duf = [T.DUF[:, 2048 * h + 128 * i:2048 * h + 128 * i + 128] for i in range(16)]
-            dve(8, ts(ju, jw, OFF, A.add), ["JW" + n], ["JU" + n])
-            dve(8, cp(jf, jw), ["JW" + n], ["JF" + n])
-            mm(grp(vTp, [(v, In)], 128), ["V" + n, "I1"], ["vTp"], "ZQ")
-            act(128, ac(T.VT[:, hs], vTp, AF.Copy), ["vTp"], ["VT" + H], "ZQ")
-            dve(128 * G, cp(pu, T.PT[:, 0:W].indirect(ju)), ["PT", "JU" + n], ["PU" + n])
-            dve(64, ts(pc, pu, -OFF, A.add), ["PU" + n], ["PC" + H])
-            for k in range(1, 4):
-                pk = T.PC[:, 512 * h + 128 * k:512 * h + 128 * k + 128]
-                if s in P4V:
-                    dve(64, ts(pk, pu, -OFF, A.add), ["PU" + n], ["P4%s%d" % (H, k)])
-                else:
-                    dma(pk, pc, 32768, ["PC" + H], ["P4%s%d" % (H, k)])
+            hs = slice(128 * h, 128 * h + 128)
+            v, pu, wr = [b[:, c0:c0 + 128] for b in (T.V, T.PU, T.WR)]
+            pc, qc = T.LN[:, LW * s:LW * s + 128], T.LN[:, LW * s + 128:LW * s + 256]
+            jr, jw = T.LN[:, LW * s + 384:LW * s + 512], T.LN[:, LW * s + 512:LW * s + 520]
+            ju, jf = [b[:, 8 * s:8 * s + 8] for b in (T.JU, T.JF)]
+            tag[0] = "e" + n
+            if t == 0:
+                dve(8, cp(ju, T.j0i[:, 8 * h:8 * h + 8]), ["j0i"], ["JU" + n])
+                dve(8, ts(jf, T.j0i[:, 8 * h:8 * h + 8], -OFF, A.add), ["j0i"], ["JF" + n])
+            elif HOP[t - 1]:
+                dve(8, ts(ju, jw, OFF, A.add), ["JW" + n], ["JU" + n])
+                affine("JF", 8, jf, jw, 1.0, 0.0, ["JW" + n], ["JF" + n])
+            else:
+                dve(8, ts(ju, jf, OFF, A.add), ["JF" + n], ["JU" + n])
+            if t == 0:
+                for b in range(8):
+                    dve(8, ts(T.Y0[:, 128 * h + 16 * b:128 * h + 16 * b + 16], T.m16[:], T.JF[:, 8 * h + b:8 * h + b + 1], A.mult),
+                        ["m16", "JF" + n], ["Y0%s%d" % (H, b)])
+                mm(grp(RR, [(blk, T.Y0[:, hs])], 128), ["blk"] + ["Y0%s%d" % (H, b) for b in range(8)], ["RR9" + H], "ZP")
+                affine("JR", 128, jr, RR, 1.0, 0.0, ["RR9" + H], ["JR" + n], "ZP")
+                lend("RR")
+            dv, dvn = (v, "V" + n) if t == 0 else (T.LN[:, LW * s + 256:LW * s + 384], "DV" + n)
+            if t:
+                act(128, ac(v, dv, AF.Abs), [dvn], ["V" + n])
+            mm(grp(vTp, [(dv, ds)], 128), [dvn, "DS%d" % t], ["vTp" + n], "ZQ")
+            act(128, ac(T.VT[:, hs], vTp, AF.Abs), ["vTp" + n], ["VT" + H], "ZQ")
+            lend("vT")
+            tag[0] = "p" + n
+            if s in PU_ACT:
+                act(128 * G, ac(pc, T.PT[:, 0:W].indirect(ju), AF.Identity, bias=-OFF), ["PT", "JU" + n], ["PC" + n])
+                dve(64, ts(pu, pc, OFF, A.add), ["PC" + n], ["PU" + n])
+            else:
+                dve(128 * G, cp(pu, T.PT[:, 0:W].indirect(ju)), ["PT", "JU" + n], ["PU" + n])
+                dve(64, ts(pc, pu, -OFF, A.add), ["PU" + n], ["PC" + n])
+            if s in SPLIT_SG:
+                for kind, (pen, e_, en_) in enumerate(((penQ, qc, "QC"), (penP, pc, "PC"))):
+                    g0 = 256 * h + 128 * (1 - kind)
+                    mm(grp(pen, [(I0, e_), (In, jr)], 128), ["I0", "I1", en_ + n, "JR" + n], ["pen%s%d" % (n, kind)], "MI")
+                    act(128, ac(T.SG[:, g0:g0 + 128], pen, AF.Sign, bias=-0.5), ["pen%s%d" % (n, kind)], ["SG%s%d" % (H, kind)], "MI")
+                    lend("pen")
+            else:
+                mm(grp(penP, [(I0, pc), (In, jr)], 128) + grp(penQ, [(I0, qc), (In, jr)], 128),
+                   ["I0", "I1", "PC" + n, "QC" + n, "JR" + n], ["pen" + n], "MI")
+                act(256, ac(T.SG[:, 256 * h:256 * h + 256], T.MI[:, 256:512], AF.Sign, bias=-0.5), ["pen" + n], ["SG%s0" % H, "SG%s1" % H], "MI")
+                lend("pen")
+            tag[0] = "w" + n
             EO, en = (T.EA, "EA") if h == 0 else (T.EB, "EB")
-            terms, rd = [], ["blkC"]
+            terms, rd = [(cw, blkW, T.mk2[:], True, False, 128)], ["blkC", "blkW", "mk2"]
             if h == 1:
                 for b in range(8):
                     dve(64, ts(T.EC[:, b, :], jr, T.JF[:, 16 * t + b:16 * t + b + 1], A.is_equal), ["JR" + n, "JF%d0" % t], ["EC%d" % b])
-                    terms.append((cw, blkC, T.EC[:, b, :], b == 0, False, 128))
+                    terms.append((cw, blkC, T.EC[:, b, :], False, False, 128))
                     rd.append("EC%d" % b)
             for b in range(8):
                 m = 128 - 16 * b
-                dve(m / 2, ts(EO[:, b, 0:m], T.JC[:, 144 * s + 16 * b:144 * s + 128], T.JF[:, 8 * s + b:8 * s + b + 1], A.is_equal),
+                dve(m / 2, ts(EO[:, b, 0:m], T.LN[:, LW * s + 384 + 16 * b:LW * s + 512], T.JF[:, 8 * s + b:8 * s + b + 1], A.is_equal),
                     ["JR" + n, "JF" + n], [en + str(b)])
-                terms.append((T.MI[:, 16 * b:128], blkC, EO[:, b, 0:m], b == 0 and h == 0, b == 7, m))
-            ens = [en + str(b) for b in range(8)]
-            dve(256, tt(EO[:, :, 0:16], EO[:, :, 0:16], T.tri[:], A.mult), ens + ["tri"], ens)
-            mm(terms, rd + ens, ["cw"], "MI")
-            act(128, ac(wr, cw, AF.Sign, accum_out=T.AC[:, s:s + 1]), ["cw"], ["WR" + n, "AC" + n], "MI")
-            wW = T.MI[:, 128 + 8 * h:136 + 8 * h]
-            mm(grp(vTp, [(wr, I2C)], 128), ["WR" + n, "I2"], ["vTp"], "ZQ")
-            dve(128, tt(T.Y[:], vTp, T.Gd[:, 8 * h:8 * h + 8, :], A.min), ["vTp", "Gd" + H], ["Y"], "ZQ")
-            mm(grp(wW, [(T.cst[:], T.ones[:, 0:8]), (T.Y[:], T.b8[:, 40:48])], 8), ["c14", "ones", "b85", "Y"], ["wW" + H], "MI")
-            dve(8, tt(T.sb[:, h8], wW, jf, A.max), ["wW" + H, "JF" + n], ["sb" + H], "MI")
-            dve(8, ts(so, T.sb[:, h8], OFF, A.add), ["sb" + H], ["SO" + n])
-            y0 = 160 + 32 * h
-            mm([(T.MI[:, y0:y0 + 24], wr, T.b8[:, 0:24], True, False, 24), (T.MI[:, y0 + 8:y0 + 16], jr, T.b8[:, 24:32], False, False, 8),
-                (T.MI[:, y0:y0 + 24], ones128, T.cm[:], False, True, 24), (T.MI[:, y0 + 24:y0 + 32], v, T.b8[:, 32:40], True, True, 8)],
-               ["WR" + n, "JR" + n, "V" + n, "ones", "b80", "b81", "b82", "b83", "b84", "cm0", "cm1", "cm2"], ["y" + H], "MI")
-            h1, h2 = T.hi[:, 16 * h:16 * h + 8], T.hi[:, 16 * h + 8:16 * h + 16]
-            dve(8, cp(h1, T.MI[:, y0 + 24:y0 + 32]), ["y" + H], ["hi" + H], "MI")
-            dve(8, ts(h2, h1, 1023, A.bitwise_and), ["hi" + H], ["hj" + H])
-            dve(8, tt(T.S0[:, 256 * h:256 * h + 256:32], T.MI[:, y0:y0 + 8], h2, A.add), ["y" + H, "hj" + H], ["S0" + H], "MI")
-            dve(8, cp(T.S0[:, 256 * h + 1:256 * h + 256:32], T.MI[:, y0 + 8:y0 + 16]), ["y" + H], ["S1" + H], "MI")
-            mm(grp(penP, [(I0, pc), (In, jr), (InC, wr)], 128) + grp(penQ, [(I0, qc), (In, jr)], 128),
-               ["I0", "I1", "I6", "WR" + n, "PC" + H, "QC" + n, "JR" + n], ["pen"], "MI")
-            act(256, ac(T.SG[:, 256 * h:256 * h + 256], T.MI[:, 256:512], AF.Sign, bias=-0.5), ["pen"], ["SG" + H], "MI")
-            for u in range(4):
-                mm([(T.DU[:, 128 * a:128 * a + 128], rep[4 * u + a], qc, True, True, 128) for a in range(4)], REPS + ["QC" + n], ["DU"], "DU")
-                f0 = 2048 * h + 512 * u
-                dve(512, tt(T.DUF[:, f0:f0 + 512], T.DU[:], T.PC[:, 512 * h:512 * h + 512], A.is_equal),
-                    ["DU", "PC" + H] + ["P4%s%d" % (H, x) for x in (1, 2, 3)], ["DUF%s%d" % (H, u)], "DU")
+                if b < 7:
+                    terms.append((T.MI[:, 16 * b + 16:128], blkC, EO[:, b, 16:m], False, False, max(64, m - 16)))
+            terms.append((cw, blkW, EO[:, :, 0:16], False, True, 128))
+            mm(terms, rd + [en + str(b) for b in range(8)], ["cw" + n], "MI")
+            act(128, ac(wr, cw, AF.Sign, bias=0.5, accum_out=T.AC[:, s:s + 1]), ["cw" + n], ["WR" + n, "AC" + n], "MI")
+            lend("cw")
+            tag[0] = "y" + n
+            y0 = 128 + 24 * h
+            mm(grp(T.MI[:, y0:y0 + 24], [(ones128, T.cm[:]), (v, T.bv[:]), (jr, T.bj[:]), (wr, T.bw[:])], 64),
+               ["WR" + n, "JR" + n, "V" + n, "ones", "bv", "bw", "bj", "cm0", "cm1", "cm2"], ["y" + H], "MI")
+            dve(8, ts(T.kk[:, 16 * h:16 * h + 16:2], T.MI[:, y0 + 16:y0 + 24], 1024 * BIG, A.add, 1024 * BIG, A.subtract), ["y" + H], ["kk" + H], "MI")
+            dve(16, tt(T.S0[:, 256 * h:256 * h + 256:16], T.MI[:, y0:y0 + 16], T.kk[:, 16 * h:16 * h + 16], A.subtract), ["y" + H, "kk" + H], ["S0" + H], "MI")
             if h == 1:
-                dve(256 * G, tt(T.DJ[:], Dw.indirect(T.JU[:, 16 * t:16 * t + 16]), T.V[:, 256 * t:256 * t + 256], A.subtract),
-                    Dn + ["JU%d0" % t, "JU" + n, "V%d0" % t, "V" + n], ["DJ"])
+                tag[0] = "d%d" % t
+                t16, tn = slice(16 * t, 16 * t + 16), str(t)
+                mm(grp(xW, [(I0, T.SP[:, 16 * (t % 2):16 * (t % 2) + 16])]
+                       + [(T.BW2[:, 15 - a:143 - a], T.WR[:, 256 * t + a:256 * t + 256:16]) for a in range(16)], 64),
+                   ["I0", "SP0", "SP1", "BW2", "BW2a", "WR%d0" % t, "WR" + n], ["xW"], "ZQ")
+                dve(16, tt(T.sb[:, t16], xW, T.JF[:, t16], A.max), ["xW", "JF%d0" % t, "JF" + n], ["sb" + tn], "ZQ")
+                dve(16, ts(T.SO[:, t16], T.sb[:, t16], OFF, A.add), ["sb" + tn], ["SO" + tn])
+                dve(32, tt(T.d16[:, t16], T.sb[:, t16], T.JF[:, t16], A.subtract), ["sb" + tn, "JF%d0" % t, "JF" + n], ["d16" + tn])
+                dve(256 * G, tt(T.DJ[:], Dw.indirect(T.JU[:, t16]), T.V[:, 256 * t:256 * t + 256], A.subtract),
+                    [Dn, "JU%d0" % t, "JU" + n, "V%d0" % t, "V" + n], ["DJ"])
                 act(256, ac(T.ND[:], T.DJ[:], AF.Abs), ["DJ"], ["ND"])
-                dve(256 * SCAT, cp(D[t + 1][:, 0:WX].indirect(T.SO[:, 16 * t:16 * t + 16]), T.ND[:]), ["ND", "SO%d0" % t, "SO" + n],
-                    ["D%d" % (t + 1)] + (["D1x"] if t == 0 else []))
+                dve(256 * SCAT, cp(D[t + 1][:, 0:WX].indirect(T.SO[:, t16]), T.ND[:]), ["ND", "SO" + tn],
+                    ["D%d" % (t + 1), "D%dx" % (t + 1)])
                 if last:
                     dma(T.yd[:], T.D4[:, 0:W], 917504, ["D4"], ["yd"])
-            for kind in range(2):
+        for h in range(2):
+            n, H, s, c0 = "%d%d" % (t, h), str(h), 2 * t + h, 256 * t + 128 * h
+            hs = slice(128 * h, 128 * h + 128)
+            v, pu, wr = [b[:, c0:c0 + 128] for b in (T.V, T.PU, T.WR)]
+            pc, qc = T.LN[:, LW * s:LW * s + 128], T.LN[:, LW * s + 128:LW * s + 256]
+            fu, d16 = [b[:, 8 * s:8 * s + 8] for b in (T.FU, T.d16)]
+            kinds = (1, 0) if 4 * s in Q_LAST or 4 * s + 1 in Q_LAST else (0, 1)
+            for kind in kinds:
+                tag[0] = "g%s%d" % (n, kind)
                 offs, on = (T.QU, "QU" + n) if kind == 0 else (T.PU, "PU" + n)
                 for u in range(2):
-                    k = tile
-                    tile += 1
-                    x0, xn = 1024 * (k % NX), "X%d" % (k % NX)
-                    src = Dw.indirect(offs[:, c0 + 64 * u:c0 + 64 * u + 64])
-                    if k in DVE_TILES:
-                        dve(1024 * G, cp(T.X[:, x0:x0 + 1024], src), Dn + [on], [xn])
-                    else:
-                        act(1024 * G, ac(T.X[:, x0:x0 + 1024], src, AF.Copy), Dn + [on], [xn])
+                    k = 4 * s + 2 * kind + u
+                    x0, xn = 1024 * (k % NX), ["Xa%d" % (k % NX), "Xb%d" % (k % NX)]
+                    parts = 2 if k in HALF_TILES else 1
+                    for b in range(parts):
+                        m = 64 // parts
+                        src = Dw.indirect(offs[:, c0 + 64 * u + m * b:c0 + 64 * u + m * b + m])
+                        dst, dn = T.X[:, x0 + 16 * m * b:x0 + 16 * m * (b + 1)], xn[b::parts]
+                        rd, wt = [Dn, on], dn
+                        if kind == 0 and k in Q_LAST:
+                            rd = rd + ["go" + n]
+                        if kind == 1 and kinds[0]:
+                            wt = wt + ["go" + n]
+                        if k in DVE_TILES:
+                            dve(16 * m * G, cp(dst, src), rd, wt)
+                        else:
+                            act(16 * m * G, ac(dst, src, AF.Copy), rd, wt)
                     slot = [0]
 
-                    def diff(slot=slot, x0=x0, u=u, hs=hs):
-                        DF, ins = DFS[slot[0]], None
-                        for b in range(2):
-                            PE.matmul(DF[:, 512 * b:512 * b + 512], T.VT[:, hs], T.E[:, 1024 * u + 512 * b:1024 * u + 512 * b + 512], True, False)
-                            ins = PE.matmul(DF[:, 512 * b:512 * b + 512], I0, T.X[:, x0 + 512 * b:x0 + 512 * b + 512], False, True)
-                        return ins
-                    add("pe", 60 + 2048 * FPE, diff, [xn, "I0", "VT" + H, "E"], ["df%d" % k])
-                    ops[-1]["take"] = slot
-                    ab, an = T.AB[:, 1024 * (k % NAB):1024 * (k % NAB) + 1024], "AB%d" % (k % NAB)
-                    act(1024, lambda slot=slot, ab=ab: S_.activation(ab, DFS[slot[0]][:], AF.Abs), ["df%d" % k], [an])
-                    ops[-1]["give"] = len(ops) - 2
-                    f0 = 1024 * (k % NFL)
-                    dve(512, ts(T.FL[:, f0:f0 + 1024], ab, th, A.is_lt, 15.0 / 32, A.add), [an, thn], ["FL%d" % (k % NFL)])
-                f0, g0 = f0 - 1024, 256 * h + 128 * (1 - kind)
-                lst = [(zT, T.SG[:, g0:g0 + 128], I16, True, False, 128)]
-                rd = ["b85", "I3", "SG" + H, "FL%d" % ((k - 1) % NFL), "FL%d" % (k % NFL)]
-                if kind == 0:
-                    lst += [(zT, wr, Iw, False, False, 128)]
-                    lst += [(T.ZQ[:, 256 + i:384:16], duf[i], T.b8[:, 48:56], False, False, 8) for i in range(16)]
-                    rd += ["b86", "I4", "WR" + n] + ["DUF%s%d" % (H, x) for x in range(4)]
-                lst += [(T.ZQ[:, 256 + i:384:16], T.FL[:, f0 + i:f0 + 2048:16], T.b8[:, 40:48], False, i == 15, 8) for i in range(16)]
-                mm(lst, rd, ["zT"], "ZQ")
-                rl = T.RL[:, 128 * kind:128 * kind + 128]
-                act(128, ac(rl, zT, AF.Sign), ["zT"], ["RL%d" % kind], "ZQ")
-                if kind == 0:
-                    mm(grp(zQ, [(rl, Io)], 128), ["I7", "RL0"], ["zQ"], "ZQ")
-                    dve(128, tt(T.TQ[:, hs], zQ, qc, A.min), ["zQ", "QC" + n], ["TQ" + H], "ZQ")
-                else:
-                    mm(grp(zP, [(rl, Io)], 128) + grp(scA, [(rl, Ip)], 128), ["I7", "I8", "RL1"], ["zP", "scA"], "ZP")
+                    def diff(terms, slot=slot, x0=x0, u=u, hs=hs, ds=ds):
+                        def fn():
+                            for b, side, s0 in terms:
+                                a_, b_ = (T.VT[:, hs], T.E[:, 1024 * u + 512 * b:1024 * u + 512 * b + 512]) if side == "v" else \
+                                    (ds, T.X[:, x0 + 512 * b:x0 + 512 * b + 512])
+                                ins = PE.matmul(DFS[slot[0]][:, 512 * b:512 * b + 512], a_, b_, s0, not s0)
+                            return ins
+                        rd = [xn[b] for b, side, _ in terms if side == "x"] + ["DS%d" % t] + ["dfa%d" % k] * terms[0][0]
+                        rd += ["VT" + H, "E"] if any(side == "v" for _, side, _ in terms) else []
+                        add("pe", 60 + 512 * len(terms) * FPE, fn, rd, ["df%s%d" % ("ab"[b], k) for b in sorted(set(x[0] for x in terms))])
+                    first = len(ops)
+                    s1_, s2_ = "xv" if k in X_FIRST else "vx"
+                    if k in X_FIRST or k in V_FIRST:
+                        diff([(0, s1_, True), (1, s1_, True)])
+                        rest = [[(b, s2_, False)] for b in range(2)]
+                    else:
+                        rest = [[(b, s1_, True), (b, s2_, False)] for b in range(2)]
+                    for terms in (rest if parts == 2 else [rest[0] + rest[1]]):
+                        diff(terms)
+                    ops[first]["take"] = ("DF", slot)
+                    f0, fn_, dn = 1024 * (k % NFL), ["FLa%d" % (k % NFL), "FLb%d" % (k % NFL)], ["dfa%d" % k, "dfb%d" % k]
+                    m = 1024 // parts
+                    if k in ACT_FLAGS:
+                        ab, an = T.AB[:, 1024 * (k % NAB):1024 * (k % NAB) + 1024], "AB%d" % (k % NAB)
+                        act(1024, lambda slot=slot, ab=ab: S_.activation(ab, DFS[slot[0]][:], AF.Identity, bias=192.0), dn, [an])
+                        ops[-1]["give"] = first
+                        dve(512, ts(T.FL[:, f0:f0 + 1024], ab, BIG - 192.0, A.add, s2, A.is_equal), [an, "S2%d" % t], fn_)
+                    else:
+                        for b in range(parts):
+                            dve(m, lambda slot=slot, fl=T.FL[:, f0 + m * b:f0 + m * b + m], s2=s2, a=m * b, m=m:
+                                V_.tensor_scalar(fl, DFS[slot[0]][:, a:a + m], BIG, s2, A.add, A.is_equal),
+                                dn[b::parts] + ["S2%d" % t] + fn_[:b], fn_[b::parts])
+                        ops[-1]["give"] = first
+            for kind in range(2):
+                tag[0] = "g%s%d" % (n, kind)
+                k = 4 * s + 1 + 2 * kind
+                f0, g0, z0 = 1024 * ((k - 1) % NFL), 256 * h + 128 * (1 - kind), 384 * kind
+                zT, zn = T.ZQ[:, z0:z0 + 128], "zT%s%d" % (n, kind)
+                lst = [(zT, T.SG[:, g0:g0 + 128], I16, True, False, 128), (zT, wr, Iwp if kind else Iwn, False, False, 128)]
+                lst += [(T.ZQ[:, z0 + i:z0 + 128:16], T.FL[:, f0 + i:f0 + 2048:16], T.b8[:], False, i == 15, 64) for i in range(16)]
+                mm(lst, ["b8", "I2", "I3", "I4", "WR" + n, "SG%s%d" % (H, kind)] + ["FL%s%d" % (a, b % NFL) for a in "ab" for b in (k - 1, k)], [zn], "ZQ")
+                rl = T.RL[:, 256 * h + 128 * kind:256 * h + 128 * kind + 128]
+                act(128, ac(rl, zT, AF.Sign, bias=7.5 + (1024.0 if kind else -1024.0)), [zn], ["RL%s%d" % (H, kind)], "ZQ")
+                lend("zT%d" % kind)
+            tag[0] = "u" + n
             mv = HOP[t] != 0
             n1, s1, c1 = "%d%d" % (t + 1, h), s + 2, c0 + 256
-            if mv:
-                qo, qn, vo, vn = T.QO[:, c0:c0 + 128], "QO" + n, T.VO[:, c0:c0 + 128], "VO" + n
-                JB, j0, jrn, jwn = T.JO, 144 * s, "JOR" + n, "JOW" + n
-            else:
-                qo, qn, vo, vn = T.QC[:, c1:c1 + 128], "QC" + n1, T.V[:, c1:c1 + 128], "V" + n1
-                JB, j0, jrn, jwn = T.JC, 144 * s1, "JR" + n1, "JW" + n1
-            dve(128, tt(T.TP[:], zP, pc, A.min), ["zP", "PC" + H], ["TP"], "ZP")
-            dve(128, tt(scA, scA, T.TQ[:, hs], A.min), ["scA", "TQ" + H], ["scA"], "ZP")
-            dve(128, tt(qo, scA, T.TP[:], A.max), ["scA", "TP"], [qn], "ZP")
-            if not last:
-                uu, un = (T.UU[:, c0:c0 + 128], "UU" + n) if mv else (T.QU[:, c1:c1 + 128], "QU" + n1)
-                UUS[h] = (uu, un)
-                dve(64, ts(uu, qo, OFF, A.add), [qn], [un])
-            if mv:
-                send(t, T.QU[:, c1:c1 + 128], uu, [un], ["QU" + n1])
-                send(t, T.QC[:, c1:c1 + 128], qo, [qn], ["QC" + n1])
-            sq, sp = T.RL[:, 0:128], T.RL[:, 128:256]
-            mm(grp(T.ZP[:, 257:512:2], [(ones128, IR), (ones128, Ih), (qc, I0), (wr, I2C), (Ih, sq), (Inh, sp)], 128)
-               + grp(T.ZP[:, 256:512:2], [(ones128, IR), (pc, I0), (Ih, sp)], 128),
-               ["ones", "I5", "I2", "I0", "I9", "I10", "WR" + n, "QC" + n, "PC" + H, "RL0", "RL1"], ["KT", "RR"], "ZP")
-            dve(256, lambda h=h: V_.tensor_tensor_scan(T.SC[:], T.S0[:, 256 * h:256 * h + 256], T.ZP[:, 256:512], 1.0e9, A.min, A.min),
-                ["KT", "RR", "S0" + H, "S1" + H], ["SC"], "ZP")
-            dve(8, cp(T.mi[:, 0:8], T.SC[:, 31:256:32]), ["SC"], ["mi0"])
-            dve(8, ts(T.mi[:, 8:16], T.mi[:, 0:8], 4095, A.bitwise_and), ["mi0"], ["mi1"])
-            dve(8, ts(T.LS[:, 0:8], T.mi[:, 8:16], -OFF, A.add), ["mi1"], ["LS0"])
-            dve(8, tt(T.LS[:, 8:16], T.MI[:, y0 + 16:y0 + 24], T.LS[:, 0:8], A.max), ["LS0", "y" + H], ["LS1"], "MI")
-            mm([(T.ZP[0:8, 256:384], T.LS[:, 0:8], I0, True, True, 128), (T.ZP[0:8, 384:512], T.LS[:, 8:16], I0, True, True, 128)],
-               ["LS0", "LS1", "I0"], ["KT", "RR"], "ZP")
-            dve(256, cp(T.F8[0:8, :], T.ZP[0:8, 256:512]), ["KT", "RR"], ["F8"], "ZP")
-            mm(grp(T.ZQ[:, 384:400], [(T.BW[0:8, 15 - c:143 - c], T.F8[0:8, c:256:16]) for c in range(16)], 16), ["F8", "BW"], ["Wr"], "ZQ")
-            dve(8, ts(fu, T.ZQ[:, 392:400], OFF, A.add), ["Wr"], ["FU" + n], "ZQ")
-            dve(128 * G, tt(T.DV[:, hs], Dw.indirect(fu), v, A.subtract), Dn + ["FU" + n, "V" + n], ["DV" + H])
-            act(128, ac(vo, T.DV[:, hs], AF.Abs), ["DV" + H], [vn])
-            if not last:
-                dve(8, cp(JB[:, j0 + 128:j0 + 136], T.ZQ[:, 384:392]), ["Wr"], [jwn], "ZQ")
-                mm(grp(RR, [(T.R8[0:8, :], T.F8[0:8, 0:128])], 128), ["F8", "R8"], ["RR"], "ZP")
-                dve(128, cp(JB[:, j0:j0 + 128], RR), ["RR"], [jrn], "ZP")
+            l1 = LW * s1
+            LB, o1, on1 = (T.LO, LW * s, "o" + n) if mv else (T.LN, l1, n1)
+            vo, vn = LB[:, o1 + 256:o1 + 384], "DV" + on1
+            ul, uln = (T.UL[:, c0:c0 + 128], "UL" + n) if mv else (T.QU[:, c1:c1 + 128], "QU" + n1)
+            rq, rp, rqn, rpn = T.RL[:, 256 * h:256 * h + 128], T.RL[:, 256 * h + 128:256 * h + 256], "RL%s0" % H, "RL%s1" % H
+            tp, tb = T.TB[:, 256 * h:256 * h + 128], T.TB[:, 256 * h + 128:256 * h + 256]
+            mm(grp(T.ZP[:, 0:128], [(rp, Io)], 128) + grp(T.ZP[:, 128:256], [(rp, Ip)], 128), ["I5", "I6", rpn], ["zPA" + n], "ZP")
+            dve(256, tt(T.TB[:, 256 * h:256 * h + 256], zPA, T.LN[:, LW * s:LW * s + 256], A.min), ["zPA" + n, "PC" + n, "QC" + n], ["TB" + H], "ZP")
+            lend("zP")
+            affine("TO", 128, T.TO[:, hs], tp, 1.0, OFF, ["TB" + H], ["TO" + H])
+            early = s in EARLY and not last
+            if early:
+                mm(grp(US, [(I0, tp), (I0, tb)], 128), ["I0", "TB" + H], ["US" + n], "ZP")
+                dve(128, ts(ul, US, 2 * OFF, A.add), ["US" + n], [uln], "ZP")
+                lend("US")
                 if mv:
-                    send(t, T.JC[:, 144 * s1:144 * s1 + 136], T.JO[:, j0:j0 + 136], [jrn, jwn], ["JR" + n1, "JW" + n1])
-                    send(t, T.V[:, c1:c1 + 128], vo, [vn], ["V" + n1])
-                if h == 1:
-                    for x in range(2):
-                        dve(128 * SCAT, cp(T.PT[:, 0:WX].indirect(T.SO[:, 16 * t + 8 * x:16 * t + 8 * x + 8]), UUS[x][0]),
-                            [UUS[x][1], "SO%d%d" % (t, x), "PTx"], ["PT"])
+                    send(t, T.QU[:, c1:c1 + 128], ul, [uln], ["QU" + n1])
+            tag[0] = "r" + n
+            slot = [0]
+
+            parts, first = 2 if s in HALF_PAIRS else 1, len(ops)
+            m = 8 // parts
+            for b in range(parts):
+                def pairs(slot=slot, tp=tp, tb=tb, ks=range(1 + m * b, 1 + m * b + m)):
+                    for k in ks:
+                        PE.matmul(DFS[slot[0]][:, 128 * k - 128:128 * k], M[k], tp, True, False)
+                        ins = PE.matmul(DFS[slot[0]][:, 128 * k - 128:128 * k], MN[k], tb, False, True)
+                    return ins
+                add("pe", 60 + 256 * m * FPE, pairs, ["TB" + H] + ["dp0" + n] * b + [x + str(k) for x in ("M", "MN") for k in range(1, 9)], ["dp%d%s" % (b, n)])
+            ops[first]["take"] = ("DF", slot)
+            for b in range(parts):
+                a = 128 * m * b
+                dve(128 * m, lambda slot=slot, nf=T.NF[:, 1024 * h + a:1024 * h + a + 128 * m], a=a, m=m:
+                    V_.tensor_scalar(nf, DFS[slot[0]][:, a:a + 128 * m], 0.0, 257.0 / 256, A.not_equal, A.subtract),
+                    ["dp%d%s" % (b, n)] + ["NF0" + H] * b, ["NF0" + H, "NF1" + H][b::parts])
+            ops[-1]["give"] = first
+            mm(grp(XU, [(M[16 - k], T.NF[:, 1024 * h + 128 * k - 128:1024 * h + 128 * k]) for k in range(1, 9)] + [(I0, tb), (rq, Ib)], 128),
+               ["NF0" + H, "NF1" + H, "TB" + H, rqn, "I0", "I9"] + ["M%d" % k for k in range(8, 16)], ["XU" + n], "KT")
+            uf = T.UF[:, hs]
+            dve(128, tt(uf, XU, T.TO[:, hs], A.max), ["XU" + n, "TO" + H], ["UF" + H], "KT")
+            lend("XU")
+            if not last:
+                dve(128 * SCAT, cp(T.PT[:, 0:WX].indirect(T.SO[:, 8 * s:8 * s + 8]), uf), ["UF" + H, "SO%d" % t, "PTx"], ["PT"])
+                if not early:
+                    dve(128, cp(ul, uf), ["UF" + H], [uln])
+                    if mv:
+                        send(t, T.QU[:, c1:c1 + 128], ul, [uln], ["QU" + n1])
+                affine("QC", 128, LB[:, o1 + 128:o1 + 256], uf, 1.0, -OFF, ["UF" + H], ["QC" + on1])
+                if mv and MERGE < 2:
+                    send(t, T.LN[:, l1 + 128:l1 + 256], LB[:, o1 + 128:o1 + 256], ["QC" + on1], ["QC" + n1])
             else:
-                dve(128, ts(T.YQ[:, hs], qo, OFF, A.add), [qn], ["YQ" + H])
-                dma(T.yq[:, hs], T.YQ[:, hs], 65536, ["YQ" + H], ["yq" + H])
-                dve(128, ts(T.YJ[0:8, hs], T.F8[0:8, 0:128], OFF, A.add), ["F8"], ["YJ" + H])
+                dma(T.yq[:, hs], uf, 65536, ["UF" + H], ["yq" + H])
+            tag[0] = "f" + n
+            mm(grp(T.KT[:, 1:256:2], [(ones128, IRq), (qc, I0), (Ih, rq), (Inh, rp)], 128)
+               + grp(T.KT[:, 0:256:2], [(ones128, IRp), (pc, I0), (Ih, rp)], 128),
+               ["ones", "IR0", "IR1", "I0", "I7", "I8", "QC" + n, "PC" + n, rqn, rpn], ["KT" + n], "KT")
+            dve(256, lambda h=h: V_.tensor_tensor_scan(T.SC[:, 256 * h:256 * h + 256], T.S0[:, 256 * h:256 * h + 256], T.KT[:, 0:256], 1.0e9, A.min, A.min),
+                ["KT" + n, "S0" + H], ["SC" + H], "KT")
+            lend("KT")
+            sc, l0 = T.SC[:, 256 * h + 31:256 * h + 256:32], 56 * h
+            dve(8, ts(T.rr[:, 8 * h:8 * h + 8], sc, B * BIG, A.add, B * BIG, A.subtract), ["SC" + H], ["rr" + H])
+            dve(16, tt(T.LS[:, l0 + 24:l0 + 32], sc, T.rr[:, 8 * h:8 * h + 8], A.subtract), ["SC" + H, "rr" + H], ["LS" + H])
+            fs = T.FS[0:32, 32 * h:32 * h + 32]
+            f32, Wr = T.ZQ[0:32, 256 + 32 * h:288 + 32 * h], T.ZQ[:, 320 + 8 * h:328 + 8 * h]
+            mm(grp(f32, [(T.LS[:, l0 + 24 - 8 * a:l0 + 56 - 8 * a], T.ID[:, a:128:4]) for a in range(4)], 32), ["LS" + H, "I0"], ["F32" + H], "ZQ")
+            affine("FS", 32, fs, f32, 1.0, 0.0, ["F32" + H], ["FS" + H], "ZQ")
+            mm(grp(Wr, [(I0, d16)] + [(T.BW4[0:32, 12 - 4 * a:140 - 4 * a], T.FS[0:32, 32 * h + a:32 * h + 32:4]) for a in range(4)], 64),
+               ["FS" + H, "BW4", "I0", "d16%d" % t], ["Wr" + H], "ZQ")
+            dve(8, ts(fu, Wr, OFF, A.add), ["Wr" + H], ["FU" + n], "ZQ")
+            dve(128 * G, tt(vo, D[t][:, 0:WX].indirect(fu), v, A.subtract), [Dn, Dn + "x", "FU" + n, "V" + n], [vn])
+            if not last:
+                if mv:
+                    dve(8, tt(LB[:, o1 + 512:o1 + 520], Wr, d16, A.subtract), ["Wr" + H, "d16%d" % t], ["JW" + on1], "ZQ")
+                else:
+                    dve(8, tt(T.JF[:, 8 * s1:8 * s1 + 8], Wr, d16, A.subtract), ["Wr" + H, "d16%d" % t], ["JF" + n1], "ZQ")
+                mm([(T.ZP[:, 384 + a:512:4], T.R4[0:32, 128 * a:128 * a + 128], fs, True, True, 64) for a in range(4)], ["FS" + H, "R4"], ["RR" + n], "ZP")
+                affine("JR", 128, LB[:, o1 + 384:o1 + 512], RR, 1.0, 0.0, ["RR" + n], ["JR" + on1], "ZP")
+                lend("RR")
+                if mv:
+                    parts = ((256, 384, ["DV"]), (384, 520, ["JR", "JW"])) if MERGE == 0 else \
+                        ((384 - 128 * MERGE, 520, ["QC", "DV", "JR", "JW"][2 - MERGE:]),)
+                    for a, b, names in parts:
+                        send(t, T.LN[:, l1 + a:l1 + b], LB[:, o1 + a:o1 + b], [x + on1 for x in names], [x + n1 for x in names])
+            else:
+                mm([(T.ZP[0:8, 384 + a:512:4], T.ID[0:32, 8 * a:8 * a + 8], fs, True, True, 32) for a in range(4)], ["FS" + H, "I0"], ["RR" + n], "ZP")
+                affine("YJ", 128, T.YJ[0:8, hs], T.ZP[0:8, 384:512], 1.0, OFF, ["RR" + n], ["YJ" + H], "ZP")
+                lend("RR")
                 dma(T.yj[:, hs], T.YJ[0:8, hs], 4096, ["YJ" + H], ["yj" + H])
-                dma(T.yv[:, hs], vo, 32768, [vn], ["yv" + H])
+                act(128, ac(T.V[:, c1:c1 + 128], vo, AF.Abs), [vn], ["V" + n1])
+                dma(T.yv[:, hs], T.V[:, c1:c1 + 128], 32768, ["V" + n1], ["yv" + H])
     return ops
+
+
+def slots(what):
+    return 2 if what == "DF" else 1
 
 
 def schedule(ops, deps0, succ, pr):
@@ -336,13 +490,13 @@ def schedule(ops, deps0, succ, pr):
     left = [len(d) for d in deps0]
     ready = {k: 0.0 for k in range(n) if left[k] == 0}
     free, done, bank, order = {}, [0.0] * n, {}, []
-    held, slot = [None, None], {}
+    held, slot = {}, {}
     while ready:
         st = {}
         for k, s in ready.items():
             o = ops[k]
             if "take" in o:
-                c = [done[d] + HOPNS if d is not None else 0.0 for d in held if d != -1]
+                c = [x for x in held.setdefault(o["take"][0], [0.0] * slots(o["take"][0])) if x is not None]
                 if not c:
                     continue
                 s = max(s, min(c))
@@ -352,19 +506,22 @@ def schedule(ops, deps0, succ, pr):
                     if e != o["eng"]:
                         s = max(s, done[d] + HOPNS)
             st[k] = s
+        if not st:
+            return None
         k0 = min(st, key=lambda k: (st[k], -pr[k]))
         e0 = ops[k0]["eng"]
         k = max([x for x in st if ops[x]["eng"] == e0 and st[x] <= st[k0] + WIN], key=lambda x: (pr[x], -x))
         o = ops[k]
         for b in o["banks"]:
             bank.setdefault(b, {})[e0] = k
-        if "take" in o:
-            i = min([i for i in range(2) if held[i] != -1], key=lambda i: done[held[i]] if held[i] is not None else 0.0)
-            held[i], slot[k] = -1, i
-        if "give" in o:
-            held[slot[o["give"]]] = k
         free[e0] = st[k] + o["dur"]
         done[k] = st[k] + o["dur"] + o["lat"]
+        if "take" in o:
+            c = held[o["take"][0]]
+            slot[k] = min([i for i, x in enumerate(c) if x is not None], key=lambda i: c[i])
+            c[slot[k]] = None
+        if "give" in o:
+            held[ops[o["give"]]["take"][0]][slot[o["give"]]] = done[k] + HOPNS
         order.append(k)
         del ready[k]
         for x in succ[k]:
@@ -375,80 +532,141 @@ def schedule(ops, deps0, succ, pr):
 
 
 def replay(r, alt):
-    tot = 0.0
-    for (o2, hop, scale) in alt:
-        free, done = {}, {}
-        for k in r[0]:
-            eng, dur, lat = o2[k]
-            s = free.get(eng, 0.0)
-            for d in r[1][k]:
-                if done[d] + hop > s:
-                    s = done[d] + hop
-            free[eng] = s + dur
-            done[k] = s + dur + lat
-        tot += max(done.values()) / scale
-    return tot
+    return sum(max(ends(r, a, [0.0] * len(a[0]), 0, 1e18)) / a[2] for a in alt)
 
 
 def decode(ops, deps0, order):
-    deps, bank, held, slot, used = {}, {}, [None, None], {}, [0, 0]
-    for j, k in enumerate(order):
-        o = ops[k]
-        d = deps0[k]
-        if o["banks"] or "take" in o:
-            d = list(d)
-            for b in o["banks"]:
-                m = bank.setdefault(b, {})
-                d += [x for e, x in m.items() if e != o["eng"]]
-                m[o["eng"]] = k
-            if "take" in o:
-                c = [i for i in (0, 1) if held[i] != -1]
-                if not c:
-                    return None
-                i = min(c, key=lambda i: used[i])
-                if held[i] is not None:
-                    d.append(held[i])
-                held[i], slot[k] = -1, i
-        if "give" in o:
-            held[slot[o["give"]]] = k
-            used[slot[o["give"]]] = j
-        deps[k] = d
+    if order is None:
+        return None
+    deps, bank, free, slot = list(deps0), {}, {}, {}
+    for k in order:
+        u = ops[k]
+        if u is None:
+            continue
+        eng, b, take, give, cls = u
+        if b:
+            e1, k1, k2 = bank.get(b, (eng, None, None))
+            if e1 != eng:
+                k2 = k1
+            bank[b] = (eng, k, k2)
+            if k2 is not None:
+                deps[k] = deps[k] + [k2]
+        if take:
+            c = free.get(take)
+            if c is None:
+                c = free[take] = [(i, None) for i in range(slots(take))]
+            if not c:
+                return None
+            slot[k], d = c.pop(0)
+            if d is not None:
+                deps[k] = deps[k] + [d]
+        if give is not None:
+            free[cls].append((slot[give], k))
     return order, deps, slot
 
 
+def queued(r, a, done, deps0):
+    o2, hop = a[:2]
+    last, prev = {}, {}
+    for k in r[0]:
+        e = o2[k][0]
+        prev[k], last[e] = last.get(e), k
+    k, out = done.index(max(done)), []
+    while k is not None:
+        s, w = done[k] - o2[k][1] - o2[k][2] - hop - 0.01, prev[k]
+        for d in r[1][k]:
+            if done[d] > s:
+                w = d
+        if w is not None and w not in deps0[k]:
+            out.append((w, k))
+        k = w
+    return out, prev
+
+
 def refine(ops, deps0, cur, alt):
-    n = len(ops)
-    val = replay(cur, alt)
-    best, bval, x = cur, val, SEED
+    n, eng = len(ops), [o[0] for o in alt[0][0]]
+    dones = [ends(cur, a, [0.0] * n, 0, 1e18) for a in alt]
+    vals = [max(d) / a[2] for d, a in zip(dones, alt)]
+    val = sum(vals) + MEAN * sum(dones[0]) / n
+    best, bval, x, edges = cur, sum(vals), SEED, None
     for it in range(MOVES):
         order = cur[0]
+        if edges is None:
+            edges, prev = queued(cur, alt[it % len(alt)], dones[it % len(alt)], deps0)
+            pos = {k: j for j, k in enumerate(order)}
         x = (x * 1103515245 + 12345) % 2147483648
-        j = (x >> 8) % n
-        k = order[j]
-        e = ops[k]["eng"]
+        if (x >> 24) % 8 < FREE:
+            k = (x >> 8) % n
+            p = prev[k]
+            if p is None:
+                continue
+        else:
+            p, k = edges[(x >> 8) % len(edges)]
         x = (x * 1103515245 + 12345) % 2147483648
-        hops, i = 1 + (x >> 10) % 3, j
-        while hops and i > 0:
-            i -= 1
-            if ops[order[i]]["eng"] == e:
-                hops -= 1
-        if hops:
-            continue
-        need, seg = {k}, order[i:j + 1]
-        for y in reversed(seg):
-            if y in need:
-                need.update(deps0[y])
-        if order[i] in need:
-            continue
-        r = decode(ops, deps0, order[:i] + [y for y in seg if y in need] + [y for y in seg if y not in need] + order[j + 1:])
+        i, j, e = pos[p], pos[k], eng[k]
+        hops = (x >> 10) % 4 - 1
+        if (x >> 20) % 2:
+            while hops > 0 and i > 0:
+                i -= 1
+                hops -= eng[order[i]] == e
+            need, seg = {k}, order[i:j + 1]
+            for y in reversed(seg):
+                if y in need:
+                    need.update(deps0[y])
+            if order[i] in need:
+                continue
+            seg = [y for y in seg if y in need] + [y for y in seg if y not in need]
+        else:
+            while hops > 0 and j < len(order) - 1:
+                j += 1
+                hops -= eng[order[j]] == e
+            late, seg = {p}, order[i:j + 1]
+            for y in seg:
+                if not late.isdisjoint(deps0[y]):
+                    late.add(y)
+            if order[j] in late:
+                continue
+            seg = [y for y in seg if y not in late] + [y for y in seg if y in late]
+        r = decode(ops, deps0, order[:i] + seg + order[j + 1:])
         if r is None:
             continue
-        v_ = replay(r, alt)
-        if v_ <= val + TEMP * (1 - it / MOVES) * ((x >> 14) % 100) / 100.0:
-            cur, val = r, v_
-            if v_ < bval:
-                best, bval = r, v_
+        room, new = TEMP * (1 - it / MOVES) * ((x >> 14) % 64) / 64.0, []
+        for a, d, v_ in zip(alt, dones, vals):
+            d = ends(r, a, d, i, (v_ + room + 400.0) * a[2])
+            if d is None:
+                break
+            new.append(d)
+        else:
+            nv = [max(d) / a[2] for d, a in zip(new, alt)]
+            v_ = sum(nv) + MEAN * sum(new[0]) / n
+            if v_ <= val + room:
+                cur, dones, vals, val, edges = r, new, nv, v_, None
+                if sum(nv) < bval:
+                    best, bval = r, sum(nv)
     return best
+
+
+def ends(r, a, done, i, limit):
+    order, deps = r[0], r[1]
+    o2, hop, _, tail = a
+    done, free = list(done), {}
+    for j in range(i - 1, max(-1, i - 120), -1):
+        k = order[j]
+        if o2[k][0] not in free:
+            free[o2[k][0]] = done[k] - o2[k][2]
+    for j in range(i, len(order)):
+        k = order[j]
+        eng, dur, lat = o2[k]
+        s = free.get(eng, 0.0) - hop
+        for d in deps[k]:
+            if done[d] > s:
+                s = done[d]
+        s += hop + dur
+        free[eng] = s
+        done[k] = s + lat
+        if s + tail[k] > limit:
+            return None
+    return done
 
 
 PLANS = {}
@@ -468,6 +686,15 @@ def plan(ops, others=()):
                 wr[x] = k
                 rd[x] = []
             deps.append(sorted(d))
+        anc = [0] * n
+        for k in range(n):
+            via = 0
+            for d in deps[k]:
+                via |= anc[d]
+            anc[k] = via | sum(1 << d for d in deps[k])
+            deps[k] = [d for d in deps[k] if not via >> d & 1]
+        use = [(o["eng"], o["banks"] and o["banks"][0], o.get("take", [None])[0], o.get("give"), ops[o.get("give", k)].get("take", [None])[0])
+               if o["banks"] or "take" in o or "give" in o else None for k, o in enumerate(ops)]
         succ = [[] for _ in range(n)]
         for k in range(n):
             for d in deps[k]:
@@ -476,32 +703,41 @@ def plan(ops, others=()):
         for k in range(n - 1, -1, -1):
             pr[k] = ops[k]["dur"] + ops[k]["lat"] + max([pr[x] + HOPNS for x in succ[k]] + [0.0])
         pr = [pr[k] - k * MIX for k in range(n)]
-        best = decode(ops, deps, schedule(ops, deps, succ, pr))
-        alt = [([(o["eng"], o["dur"], o["lat"]) for o in o2], p[3], p[0] * (1 + p[1] / 4)) for o2, p in zip([ops] + list(others), PARS)]
+        best = decode(use, deps, schedule(ops, deps, succ, pr))
+        alt = []
+        for o2, p in zip([ops] + list(others), PARS):
+            tail = [0.0] * n
+            for k in range(n - 1, -1, -1):
+                tail[k] = o2[k]["lat"] + max([tail[x] + o2[x]["dur"] + p[3] for x in succ[k]] + [0.0])
+            alt.append(([(o["eng"], o["dur"], o["lat"]) for o in o2], p[3], p[0] * (1 + p[1] / 4), tail))
         val = replay(best, alt)
-        kinds = sorted(set(o["eng"] + o["w"][0].rstrip("0123456789") for o in ops))
-        kind = [kinds.index(o["eng"] + o["w"][0].rstrip("0123456789")) for o in ops]
+        sets = {}
+        for k, o in enumerate(ops):
+            sets.setdefault(o["eng"] + o["w"][0].rstrip("0123456789"), []).append(k)
+            sets.setdefault("#" + o["tag"], []).append(k)
+        sets = [sets[c] for c in sorted(sets)]
         x = SEED
         for it in range(ITER):
             q = list(pr)
             for _ in range(2):
                 x = (x * 1103515245 + 12345) % 2147483648
-                c = (x >> 8) % len(kinds)
+                c = (x >> 8) % len(sets)
                 x = (x * 1103515245 + 12345) % 2147483648
                 a = ((x >> 8) % 2001 - 1000) * AMP
-                for k in range(n):
-                    if kind[k] == c:
-                        q[k] += a
-            r = decode(ops, deps, schedule(ops, deps, succ, q))
+                for k in sets[c]:
+                    q[k] += a
+            r = decode(use, deps, schedule(ops, deps, succ, q))
+            if r is None:
+                continue
             v_ = replay(r, alt)
             if v_ <= val:
                 best, pr, val = r, q, v_
-        PLANS[n] = refine(ops, deps, best, alt)
+        PLANS[n] = refine(use, deps, best, alt)
     order, deps, slot = PLANS[n]
     for j, k in enumerate(order):
         ops[k]["t0"] = j
     for k, i in slot.items():
-        ops[k]["take"][0] = i
+        ops[k]["take"][1][0] = i
     return order, deps, 0.0
 
 

@@ -10,21 +10,25 @@ B = 4096.0
 BIG = 1.5 * 2.0 ** 23
 HOP = (1, 0, 2, 0)
 DVE_TILES = (2,)
-X_FIRST, V_FIRST = (8, 16, 24), ()
-HALF_PAIRS = ()
+X_FIRST, V_FIRST = (8, 9, 16, 17, 24, 25), ()
+HALF_PAIRS = (1, 3, 5, 7)
 Q_LAST = ()
 HALF_TILES = range(3, 32, 4)
-ACT_FLAGS = (0, 4, 22)
+ACT_FLAGS = ()
 EARLY = (0, 2, 4)
 SPLIT_SG = (0, 1)
-ON_ACT = ("FS", "JR", "TO", "QC", "YJ", "DS")
-MERGE = 2
-LW = 528
-PU_ACT = (0, 1, 3, 5, 7)
-NX, NAB, NFL = 8, 4, 8
-PARS = [(0.85, 1.56, 3.8, 90.0, 3300.0), (0.9, 1.15, 2.2, 150.0, 4000.0), (1.2, 1.9, 5.0, 100.0, 2800.0)]
-MEAN, FREE = 1.0, 3
-HOPNS, MIX, WIN, ITER, SEED, AMP, MOVES, TEMP = 100.0, 50.0, 100.0, 100, 5, 10.0, 50000, 500.0
+ON_ACT = ("FS", "JR", "TO", "QC", "YJ", "DS", "JF", "Y01")
+MERGE = 0
+LW = 432
+WHOLE = (0,)
+SHARED = ()
+PU_ACT = (1,)
+NX, NAB, NFL, LOADS = 8, 4, 8, 6
+PARS = [(0.83, 1.56, 3.8, 80.0, 1800.0, 35.0, 64, 60.0, 0.415, 1300.0, 270.0, 250.0),
+        (1.0, 1.2, 2.5, 120.0, 2600.0, 45.0, 48, 40.0, 0.5, 1000.0, 330.0, 800.0),
+        (1.2, 1.9, 5.0, 90.0, 1500.0, 35.0, 64, 60.0, 0.6, 1500.0, 230.0, 150.0)]
+MEAN, FREE, ROUNDS, SLACK = 1.0, 3, 16, 2500.0
+HOPNS, MIX, WIN, ITER, SEED, AMP, MOVES, TEMP = 100.0, 50.0, 100.0, 40, 4, 10.0, 4000, 500.0
 
 
 def _sb(d, **kw):
@@ -33,23 +37,22 @@ def _sb(d, **kw):
 
 SCRATCH = {}
 SCRATCH.update(_sb("bfloat16", D0=WX, D1=WX, D2=WX, D3=WX, D4=WX, V=1280, X=NX * 1024, AB=NAB * 1024, FL=NFL * 1024,
-                   AN=2048, EA=(8, 128), EB=(8, 128), EC=(8, 128), WR=1024, SG=512, DJ=256, ND=256, RL=512,
-                   ones=528, E=2048, ID=10 * 128, blk=384, C3=(8, 32), M=16 * 128, MN=9 * 128, Bs=256, BW2=144, BW4=144, R4=512,
-                   mk2=128, b8=8, bv=24, bw=24, bj=24))
-SCRATCH.update(_sb("float16", LN=10 * LW, LO=6 * LW, NF=2048, TB=512, LS=112, FS=64, Y0=256, VT=256, DS=512,
-                   cm=24, SP=32, d16=64))
-SCRATCH.update(_sb("int32", PT=WX, q0i=256, j0i=16, wai=2, aci=8, pi=4))
-SCRATCH.update(_sb("uint16", QU=1280, PU=1024, UL=1024, JU=64, FU=64, SO=64))
-SCRATCH.update(_sb("float32", waf=2, JF=64, sb=64, AC=8, U2=4, RS=4, S2=4, S0=512, SC=512, UF=256, TO=256, YJ=256, kk=32, rr=16,
-                   pf=12, r144=144, rg=128, rc=128, r4=512, m16=16, pw=48))
+                   AN=1024, EO=(16, 256), EC=(8, 128), WR=1024, SG=512, DJ=256, ND=256, RL=512,
+                   ones=128, E=1024, ID=10 * 128, blk=384, C3=(8, 32), M=16 * 128, MN=9 * 128, Bs=256, BW2=144, BW4=144, R4=512,
+                   mk2=256, JH=64, JL=64, S2=64, SU=520, b8=8, bv=32, bw=32, bj=32))
+SCRATCH.update(_sb("float16", LN=10 * LW, LO=6 * LW, JR=1024, NF=2048, TB=512, LS=112, XW=4096, Y0=256, VT=256, DS=512,
+                   cm=32, SP=32, d16=64))
+SCRATCH.update(_sb("int32", PT=WX, q0i=256, j0i=16, wai=2, pi=4))
+SCRATCH.update(_sb("uint16", QU=1280, PU=1024, UL=1024, JU=64, FU=64, SO=64, AU=8))
+SCRATCH.update(_sb("float32", waf=2, JF=64, sb=64, AC=8, U2=4, RS=64, ST=520, S0=512, SC=512, UF=256, TO=256, YJ=256, kk=64, rr=16,
+                   pf=12, r144=144, rg=128, rc=256, r4=512, m16=16, pw=48))
 SCRATCH.update({k: ("psum", [128, n], "float32") for k, n in (("DF0", 1024), ("DF1", 1024), ("ZP", 512), ("ZQ", 512), ("KT", 512), ("MI", 512))})
 SEMAPHORES = ["pe", "dve", "act", "pool", "sent"] + ["m%d" % k for k in range(30)] + ["a%d" % k for k in range(16)]
 
 
 def program(g, T, dests, par=None):
     ops = []
-    F, G, SCAT, _, XFER = par or PARS[0]
-    FPE = F / 2
+    F, G, SCAT, _, XFER, VOV, VMIN, POV, FPE, DMA0, RATE, CALL = par or PARS[0]
     nd = [0, 0]
     V_, S_, PE = g.vector, g.scalar, g.tensor
     tag = [""]
@@ -63,10 +66,10 @@ def program(g, T, dests, par=None):
         ops[-1]["give"] = len(ops) - 2
 
     def dve(n, fn, r, w, *banks):
-        add("dve", 55 + max(n, 16) * F, fn, r, w, banks)
+        add("dve", VOV + max(n, VMIN) * F, fn, r, w, banks)
 
     def act(n, fn, r, w, *banks):
-        add("act", 70 + max(n, 16) * F, fn, r, w, banks)
+        add("act", VOV + 15 + max(n, VMIN) * F, fn, r, w, banks)
 
     def pool(base, n, fn, r, w):
         add("pool", base + 2 * n * F, fn, r, w)
@@ -77,7 +80,7 @@ def program(g, T, dests, par=None):
             for (o, a, b, s0, s1, n) in lst:
                 ins = PE.matmul(o, a, b, s0, s1)
             return ins
-        add("pe", 60 + sum(x[5] for x in lst) * FPE, fn, r, w, banks)
+        add("pe", POV + sum(x[5] for x in lst) * FPE, fn, r, w, banks)
 
     def grp(out, terms, n):
         return [(out, a, b, k == 0, k == len(terms) - 1, n) for k, (a, b) in enumerate(terms)]
@@ -85,13 +88,14 @@ def program(g, T, dests, par=None):
     def dma(out, in_, nbytes, r, w):
         k = nd[0]
         nd[0] += 1
-        add("sp", 60.0, lambda: g.sync.dma_start(out, in_), r, w, (), "m%d" % k, 1900 + nbytes / 190.0, 16)
+        add("sp", 60.0, lambda: g.sync.dma_start(out, in_), r, w, (), "m%d" % k, DMA0 + nbytes / RATE, 16)
 
-    def send(t, out, in_, r, w):
+    def send(t, out, in_, r, w, nbytes=32768):
         k = nd[1]
         nd[1] += 1
         rid, pid, mask, ne = dests[t]
-        add("pool", 150.0, lambda: g.remote_dma(out, in_, T.sem["a%d" % k], T.sem.sent, pid, rid, mask), r, w, (), "a%d" % k, XFER, ne)
+        add("pool", CALL if k else CALL + 1400.0, lambda: g.remote_dma(out, in_, T.sem["a%d" % k], T.sem.sent, pid, rid, mask), r, w, (), "a%d" % k,
+            XFER + nbytes / 40.0, ne)
 
     def ts(out, in0, s1, op0, s2=None, op1=None):
         if op1 is None:
@@ -120,21 +124,23 @@ def program(g, T, dests, par=None):
             dve(n, ts(out, a, scale, A.mult, bias, A.add), r, w, *banks)
 
     D = [T.D0, T.D1, T.D2, T.D3, T.D4]
-    dma(T.q0i[:], T.q0[:], 131072, [], ["q0i"])
-    dma(T.D0[:, 0:W], T.d0[:], 917504, [], ["D0"])
     dma(T.j0i[:], T.j0[:], 8192, [], ["j0i"])
-    dma(T.V[:, 0:256], T.v0[:], 65536, [], ["V00", "V01"])
-    dma(T.wai[:], T.wa[:], 1024, [], ["wai"])
-    dma(T.PT[:, 0:W], T.p0[:], 3 * 917504, [], ["PT"])
+    dma(T.wai[:], T.wa[:], 10000, [], ["wai"])
+    dma(T.q0i[:], T.q0[:], 140000, [], ["q0i"])
+    dma(T.D0[:, 0:W], T.d0[:], 1060000, [], ["D0"])
+    dma(T.V[:, 0:256], T.v0[:], 1125000, [], ["V00", "V01"])
+    dma(T.PT[:, 0:W], T.p0[:], 2960000, [], ["PT"])
     dve(W / 2, cp(T.D1[:, 0:W], T.D0[:, 0:W]), ["D0"], ["D1"])
     add("pool", 150, lambda: g.iota(T.pi[:, 0:1], [[0, 1]], 0, 1), [], ["pi0"])
     pool(130, 144, iota(T.r144[:], [[1, 144]]), [], ["r144"])
     pool(130, 128, iota(T.rg[:], [[1, 8], [0, 16]]), [], ["rg"])
-    pool(130, 128, iota(T.rc[:], [[0, 8], [1, 16]]), [], ["rc"])
-    dve(264, ms(T.ones[:], 1.0), [], ["ones"])
+    pool(130, 256, iota(T.rc[:], [[0, 16], [1, 16]]), [], ["rc"])
+    dve(64, ms(T.ones[:], 1.0), [], ["ones"])
     dve(128, ms(T.Bs[:], B), [], ["Bs"])
-    dve(1024, ms(T.AN[:], 0.0), [], ["AN0", "AN1"])
-    pool(170, 2048, lambda: g.affine_select(T.E[:], T.AN[:], [[-1, 128], [0, 16]], A.not_equal, -1.0, 0, 1), ["AN0", "AN1"], ["E"])
+    pool(130, 1024, iota(T.AN[:], [[1, 64], [0, 16]]), [], ["AN"])
+    dve(1, ts(T.JH[:, 0:1], T.pi[:, 0:1], 63.5, A.is_gt, -64.0, A.mult), ["pi0"], ["JH00"])
+    dve(1, tt(T.JL[:, 0:1], T.pi[:, 0:1], T.JH[:, 0:1], A.add), ["pi0", "JH00"], ["JL00"])
+    dve(512, ts(T.E[:], T.AN[:], T.JL[:, 0:1], A.is_equal, -1.0, A.mult), ["AN", "JL00"], ["E"])
     pool(170, 256, lambda: g.affine_select(T.C3[:], T.Bs[:], [[-16, 8], [0, 2], [-1, 16]], A.is_equal, 0.0, 0, 1), ["Bs"], ["C3"])
     M = [T.M[:, 128 * k:128 * k + 128] for k in range(16)]
     MN = [T.MN[:, 128 * k:128 * k + 128] for k in range(9)]
@@ -145,9 +151,12 @@ def program(g, T, dests, par=None):
     pool(130, 512, iota(T.r4[:], [[1, 32], [0, 16]]), [], ["r4"])
     pool(130, WX - W, lambda: g.iota(T.PT[:, W:WX], [[0, WX - W]], 0, 0), [], ["PTx"])
     for t in range(5):
-        act(WX - W, ac(D[t][:, W:WX], T.ones[:, 0:WX - W], AF.Copy, scale=0.0), ["ones"], ["D%dx" % t])
+        pool(130, WX - W, iota(D[t][:, W:WX], [[0, WX - W]]), [], ["D%dx" % t])
     dve(512, ms(T.S0[:], 1.0e9), [], ["S00", "S01"])
-    dve(32, ms(T.kk[:], 0.0), [], ["kk0", "kk1"])
+    dve(64, ms(T.kk[:], -1.0e9), [], ["kk0", "kk1"])
+    dve(16, ms(T.kk[:, 1:64:4], 0.0), [], ["kk0", "kk1"])
+    for s in (0, 1, 4, 5):
+        act(32, ac(T.LO[:, LW * s + 384:LW * s + 416], T.ones[:, 0:32], AF.Copy), ["ones"], ["FSo%d%d" % divmod(s, 2)])
     dve(56, ts(T.LS[:], T.ones[:, 0:112], 0.0, A.mult), ["ones"], ["LS0", "LS1"])
     dve(1, ts(T.pi[:, 1:2], T.pi[:, 0:1], 15, A.bitwise_and), ["pi0"], ["pi1"])
     dve(1, ts(T.pi[:, 2:3], T.pi[:, 0:1], 4, A.arith_shift_right), ["pi0"], ["pi2"])
@@ -171,7 +180,7 @@ def program(g, T, dests, par=None):
     dve(32, tt(T.pw[:, 32:48], T.pw[:, 16:32], T.m16[:], A.mult), ["pw1", "m16"], ["pw2"])
     dve(16, lambda: V_.tensor_reduce(T.pf[:, 6:7], T.pw[:, 32:48], AxisListType.X, A.add), ["pw2"], ["pf6"])
     act(128, ac(blkW, blk, AF.Copy, scale=T.pf[:, 6:7]), ["blk", "pf6"], ["blkW"])
-    dve(128, ts(T.mk2[:], T.rc[:], pm, A.is_equal, -2.0, A.mult), ["pf", "rc"], ["mk2"])
+    dve(256, ts(T.mk2[:], T.rc[:], pm, A.is_equal, -2.0, A.mult), ["pf", "rc"], ["mk2"])
     dve(1, ts(T.pf[:, 7:8], pm, 0.0, A.is_equal, p_, A.mult), ["pf"], ["pf7"])
     dve(1, ts(T.pf[:, 8:9], pm, -200.0, A.mult, T.pf[:, 7:8], A.add), ["pf", "pf7"], ["pf8"])
     dve(144, ts(T.BW2[:, 15:144], T.r144[:, 0:129], T.pf[:, 8:9], A.is_equal, 2304.0, A.mult), ["pf8", "r144"], ["BW2"])
@@ -187,19 +196,28 @@ def program(g, T, dests, par=None):
     dve(8, ts(T.b8[:], r8, pg, A.is_equal), ["pf", "r144"], ["b8"])
     dve(2, cp(T.waf[:], T.wai[:]), ["wai"], ["waf"])
     for buf, nm in ((T.bv, "bv"), (T.bw, "bw"), (T.bj, "bj")):
-        dve(12, ms(buf[:], 0.0), [], [nm])
-    dve(8, ts(T.bv[:, 0:16:2], T.b8[:], T.waf[:, 0:1], A.mult), ["b8", "waf"], ["bv"])
-    dve(8, ts(T.bv[:, 16:24], T.b8[:], T.waf[:, 0:1], A.mult), ["b8", "waf"], ["bv"])
-    dve(8, ts(T.bw[:, 1:16:2], T.b8[:], -384.0, A.mult), ["b8"], ["bw"])
-    dve(8, ts(T.bj[:, 1:16:2], T.b8[:], 1 / 16.0, A.mult), ["b8"], ["bj"])
-    for k, (dst, m_, a_) in enumerate(((T.cm[:, 0:16:2], -128.0, 914.0), (T.cm[:, 1:16:2], -128.0, 912.0), (T.cm[:, 16:24], 0.0, -511.5 / 128))):
-        dve(8, ts(dst, r8, m_, A.mult, a_, A.add), ["r144"], ["cm%d" % k])
+        pool(130, 32, iota(buf[:], [[0, 32]]), [], [nm])
+    act(32, ac(T.cm[:], T.ones[:, 0:32], AF.Copy, scale=0.0), ["ones"], ["cm"])
+    for c in (0, 2):
+        act(8, ac(T.bv[:, c:32:4], T.b8[:], AF.Copy, scale=T.waf[:, 0:1]), ["b8", "waf"], ["bv"])
+    act(8, ac(T.bw[:, 1:32:4], T.b8[:], AF.Copy, scale=-384.0), ["b8"], ["bw"])
+    act(8, ac(T.bj[:, 1:32:4], T.b8[:], AF.Copy, scale=1 / 16.0), ["b8"], ["bj"])
+    for c, m_, a_ in ((0, -128.0, 914.0), (1, -128.0, 912.0), (2, 0.0, -511.5 / 128)):
+        act(8, ac(T.cm[:, c:32:4], r8, AF.Identity, scale=m_, bias=a_), ["r144"], ["cm"])
     dve(1, ts(T.pf[:, 3:4], T.waf[:, 1:2], 2.0, A.mult, -1.0, A.add), ["waf"], ["a2"])
+    dve(4, ts(T.U2[:], T.r144[:, 0:4], 2.0, A.mult, T.pf[:, 3:4], A.add), ["a2", "r144"], ["U2"])
+    dve(210, lambda: V_.reciprocal(T.RS[:, 0:4], T.U2[:]), ["U2"], ["RS0"])
+    dve(1, ts(T.S2[:, 0:1], T.pf[:, 3:4], 0.0, A.is_gt, BIG, A.mult), ["a2"], ["S20"])
+    pool(130, 520, iota(T.ST[:], [[0, 520]]), [], ["ST"])
+    for k in range(4):
+        act(65, ac(T.ST[:, 2 * k:520:8], T.ones[:, 0:65], AF.Copy, scale=T.RS[:, k:k + 1]), ["RS0"], ["ST"])
+    pool(130, 520, lambda: g.iota(T.SU[:], [[0, 520]], int(BIG), 0, allow_small_or_imprecise_dtypes=True), [], ["SU"])
+    dve(65, ts(T.SU[:, 0:520:8], T.ones[:, 0:65], T.S2[:, 0:1], A.mult), ["S20"], ["SU"])
     ones128 = T.ones[:, 0:128]
     zPA, US, RR = T.ZP[:, 0:256], T.ZP[:, 256:384], T.ZP[:, 384:512]
     vTp, xW = T.ZQ[:, 128:256], T.ZQ[:, 336:352]
     XU = T.KT[:, 256:384]
-    cw, penP, penQ = T.MI[:, 0:128], T.MI[:, 256:384], T.MI[:, 384:512]
+    penP, penQ = T.MI[:, 256:384], T.MI[:, 384:512]
     for h in range(2):
         n = "0%d" % h
         dve(128, cp(T.QU[:, 128 * h:128 * h + 128], T.q0i[:, 128 * h:128 * h + 128]), ["q0i"], ["QU" + n])
@@ -210,27 +228,23 @@ def program(g, T, dests, par=None):
         last = t == 3
         Dn, Dw = "D%d" % t, D[t][:, 0:W]
         tag[0] = "s%d" % t
-        u2, rs, s2, ds = T.U2[:, t:t + 1], T.RS[:, t:t + 1], T.S2[:, t:t + 1], T.DS[:, 128 * t:128 * t + 128]
-        if t == 0:
-            u2, un_ = T.pf[:, 3:4], "a2"
-        else:
-            un_, k = "U2%d" % t, 2 * (t - 1)
-            dve(1, tt(T.aci[:, k:k + 1], T.AC[:, k:k + 1], T.AC[:, k + 1:k + 2], A.add), ["AC%d0" % (t - 1), "AC%d1" % (t - 1)], ["aci%d" % k])
-            dve(1, ts(T.aci[:, k + 1:k + 2], T.aci[:, k:k + 1], 1, A.arith_shift_right, 3, A.bitwise_and), ["aci%d" % k], ["aci%d" % (k + 1)])
-            dve(1, ts(u2, T.aci[:, k + 1:k + 2], 2.0, A.mult, T.pf[:, 3:4], A.add), ["aci%d" % (k + 1), "a2"], [un_])
+        rs, s2, ds = T.RS[:, 16 * t:16 * t + 1], T.S2[:, 16 * t:16 * t + 1], T.DS[:, 128 * t:128 * t + 128]
+        if t:
+            k, au = 2 * t - 1, T.AU[:, 2 * t:2 * t + 1]
+            if t - 1 in WHOLE:
+                dve(1, ts(au, T.AC[:, k:k + 1], 256.0, A.add), ["AC%d1" % (t - 1)], ["AU%d" % t])
+            else:
+                dve(1, ts(au, T.AC[:, k:k + 1], T.AC[:, k - 1:k], A.add, 256.0, A.add), ["AC%d0" % (t - 1), "AC%d1" % (t - 1)], ["AU%d" % t])
+            act(16 * G, ac(T.RS[:, 16 * t:16 * t + 16], T.ST[:, 0:520].indirect(au), AF.Copy), ["AU%d" % t, "ST"], ["RS%d" % t])
+            act(16 * G, ac(T.S2[:, 16 * t:16 * t + 16], T.SU[:, 0:520].indirect(au), AF.Copy), ["AU%d" % t, "SU"], ["S2%d" % t])
             dma(D[t + 1][:, 0:W], D[t][:, 0:W], 917504, [Dn] + (["DV%d0" % t] if HOP[t - 1] else []), ["D%d" % (t + 1)])
-        dve(190, lambda rs=rs, u2=u2: V_.reciprocal(rs, u2), [un_], ["RS%d" % t])
-        if "DS" in ON_ACT:
-            act(128, ac(ds, I0, AF.Copy, scale=rs), ["I0", "RS%d" % t], ["DS%d" % t])
-        else:
-            dve(64, ts(ds, I0, rs, A.mult), ["I0", "RS%d" % t], ["DS%d" % t])
-        dve(1, ts(s2, u2, 0.0, A.is_gt, BIG, A.mult), [un_], ["S2%d" % t])
+        affine("DS", 128, ds, I0, rs, 0.0, ["I0", "RS%d" % t], ["DS%d" % t])
         for h in range(2):
             n, H, s, c0 = "%d%d" % (t, h), str(h), 2 * t + h, 256 * t + 128 * h
             hs = slice(128 * h, 128 * h + 128)
             v, pu, wr = [b[:, c0:c0 + 128] for b in (T.V, T.PU, T.WR)]
             pc, qc = T.LN[:, LW * s:LW * s + 128], T.LN[:, LW * s + 128:LW * s + 256]
-            jr, jw = T.LN[:, LW * s + 384:LW * s + 512], T.LN[:, LW * s + 512:LW * s + 520]
+            jr, jw = T.JR[:, c0:c0 + 128], T.LN[:, LW * s + 416:LW * s + 424]
             ju, jf = [b[:, 8 * s:8 * s + 8] for b in (T.JU, T.JF)]
             tag[0] = "e" + n
             if t == 0:
@@ -243,11 +257,16 @@ def program(g, T, dests, par=None):
                 dve(8, ts(ju, jf, OFF, A.add), ["JF" + n], ["JU" + n])
             if t == 0:
                 for b in range(8):
-                    dve(8, ts(T.Y0[:, 128 * h + 16 * b:128 * h + 16 * b + 16], T.m16[:], T.JF[:, 8 * h + b:8 * h + b + 1], A.mult),
-                        ["m16", "JF" + n], ["Y0%s%d" % (H, b)])
-                mm(grp(RR, [(blk, T.Y0[:, hs])], 128), ["blk"] + ["Y0%s%d" % (H, b) for b in range(8)], ["RR9" + H], "ZP")
-                affine("JR", 128, jr, RR, 1.0, 0.0, ["RR9" + H], ["JR" + n], "ZP")
-                lend("RR")
+                    affine("Y0%d" % h, 16, T.Y0[:, 128 * h + 16 * b:128 * h + 16 * b + 16], T.m16[:], T.JF[:, 8 * h + b:8 * h + b + 1], 0.0,
+                           ["m16", "JF" + n], ["Y0%s%d" % (H, b)])
+                mm(grp(RR, [(blk, T.Y0[:, hs])], 128), ["blk"] + ["Y0%s%d" % (H, b) for b in range(8)], ["RE" + n], "ZP")
+            else:
+                mm([(T.ZP[:, 384 + a:512:4], T.R4[0:32, 128 * a:128 * a + 128], T.LN[0:32, LW * s + 384:LW * s + 416], True, True, 64)
+                    for a in range(4)], ["FS" + n, "R4"], ["RE" + n], "ZP")
+            affine("JR", 128, jr, RR, 1.0, 0.0, ["RE" + n], ["JR" + n], "ZP")
+            lend("RR")
+            if t and HOP[t - 1] and s - 2 not in EARLY:
+                dve(64, ts(T.QU[:, c0:c0 + 128], qc, OFF, A.add), ["QC" + n], ["QU" + n])
             dv, dvn = (v, "V" + n) if t == 0 else (T.LN[:, LW * s + 256:LW * s + 384], "DV" + n)
             if t:
                 act(128, ac(v, dv, AF.Abs), [dvn], ["V" + n])
@@ -272,30 +291,41 @@ def program(g, T, dests, par=None):
                    ["I0", "I1", "PC" + n, "QC" + n, "JR" + n], ["pen" + n], "MI")
                 act(256, ac(T.SG[:, 256 * h:256 * h + 256], T.MI[:, 256:512], AF.Sign, bias=-0.5), ["pen" + n], ["SG%s0" % H, "SG%s1" % H], "MI")
                 lend("pen")
-            tag[0] = "w" + n
-            EO, en = (T.EA, "EA") if h == 0 else (T.EB, "EB")
-            terms, rd = [(cw, blkW, T.mk2[:], True, False, 128)], ["blkC", "blkW", "mk2"]
-            if h == 1:
-                for b in range(8):
-                    dve(64, ts(T.EC[:, b, :], jr, T.JF[:, 16 * t + b:16 * t + b + 1], A.is_equal), ["JR" + n, "JF%d0" % t], ["EC%d" % b])
-                    terms.append((cw, blkC, T.EC[:, b, :], False, False, 128))
-                    rd.append("EC%d" % b)
-            for b in range(8):
-                m = 128 - 16 * b
-                dve(m / 2, ts(EO[:, b, 0:m], T.LN[:, LW * s + 384 + 16 * b:LW * s + 512], T.JF[:, 8 * s + b:8 * s + b + 1], A.is_equal),
-                    ["JR" + n, "JF" + n], [en + str(b)])
-                if b < 7:
-                    terms.append((T.MI[:, 16 * b + 16:128], blkC, EO[:, b, 16:m], False, False, max(64, m - 16)))
-            terms.append((cw, blkW, EO[:, :, 0:16], False, True, 128))
-            mm(terms, rd + [en + str(b) for b in range(8)], ["cw" + n], "MI")
-            act(128, ac(wr, cw, AF.Sign, bias=0.5, accum_out=T.AC[:, s:s + 1]), ["cw" + n], ["WR" + n, "AC" + n], "MI")
-            lend("cw")
-            tag[0] = "y" + n
-            y0 = 128 + 24 * h
-            mm(grp(T.MI[:, y0:y0 + 24], [(ones128, T.cm[:]), (v, T.bv[:]), (jr, T.bj[:]), (wr, T.bw[:])], 64),
-               ["WR" + n, "JR" + n, "V" + n, "ones", "bv", "bw", "bj", "cm0", "cm1", "cm2"], ["y" + H], "MI")
-            dve(8, ts(T.kk[:, 16 * h:16 * h + 16:2], T.MI[:, y0 + 16:y0 + 24], 1024 * BIG, A.add, 1024 * BIG, A.subtract), ["y" + H], ["kk" + H], "MI")
-            dve(16, tt(T.S0[:, 256 * h:256 * h + 256:16], T.MI[:, y0:y0 + 16], T.kk[:, 16 * h:16 * h + 16], A.subtract), ["y" + H, "kk" + H], ["S0" + H], "MI")
+            for lo in ([0] if h else []) if t in WHOLE else [h]:
+                tag[0] = "w" + n
+                hv = range(lo, h + 1)
+                nm = lambda x, hv=hv: ["%s%d%d" % (x, t, y) for y in hv]
+                a, z, j0 = 128 * lo, 128 * h + 128, 256 * t
+                c8 = slice(16 * t + 8 * lo, 8 * s + 8)
+                jx, jxn = (jw, nm("JW")) if t and HOP[t - 1] and lo == h else (T.JF[:, c8], nm("JF"))
+                dve(16, ts(T.JH[:, c8], jx, 16 * BIG, A.add, 16 * BIG, A.subtract), jxn, nm("JH"))
+                dve(32, tt(T.JL[:, c8], jx, T.JH[:, c8], A.subtract), jxn + nm("JH"), nm("JL"))
+                cw = T.MI[:, a:z]
+                terms, rd = [(cw, blkW, T.mk2[:, 0:z - a], True, False, z - a)], ["blkC", "blkW", "mk2"]
+                for b in range(8 * h + 8):
+                    c, m = 16 * t + b, z - max(a, 16 * b)
+                    e_, en = (T.EC[:, b, :], "EC%d" % b) if 16 * b < a else (T.EO[:, b, 0:m], "EO%d" % b)
+                    dve(m / 2, ts(e_, T.JR[:, j0 + z - m:j0 + z], T.JH[:, c:c + 1], A.subtract, T.JL[:, c:c + 1], A.is_equal),
+                        nm("JR") + ["JL%d%d" % (t, b // 8)], [en])
+                    rd.append(en)
+                    if 16 * b < a:
+                        terms.append((cw, blkC, e_, False, False, m))
+                    elif m > 16:
+                        terms.append((T.MI[:, 16 * b + 16:z], blkC, T.EO[:, b, 16:m], False, False, max(64, m - 16)))
+                terms.append((cw, blkW, T.EO[:, 8 * lo:8 * h + 8, 0:16], False, True, z - a))
+                mm(terms, rd, ["cw" + n], "MI")
+                act(z - a, ac(T.WR[:, j0 + a:j0 + z], cw, AF.Sign, bias=0.5, accum_out=T.AC[:, s:s + 1]), ["cw" + n], nm("WR") + ["AC" + n], "MI")
+                lend("cw")
+                tag[0] = "y" + n
+                lst = []
+                for y in hv:
+                    c = slice(j0 + 128 * y, j0 + 128 * y + 128)
+                    lst += grp(T.KT[:, 384 + 32 * y:416 + 32 * y], [(ones128, T.cm[:]), (T.V[:, c], T.bv[:]), (T.JR[:, c], T.bj[:]), (T.WR[:, c], T.bw[:])], 64)
+                yn, c, e_ = ["y%d" % y for y in hv], 32 * lo, 32 * h + 32
+                mm(lst, nm("WR") + nm("JR") + nm("V") + ["ones", "bv", "bw", "bj", "cm"], yn, "KT")
+                dve(16, ts(T.kk[:, c:e_:4], T.KT[:, 384 + c + 2:384 + e_:4], 1024 * BIG, A.add, 1024 * BIG, A.subtract), yn, ["kk%d" % y for y in hv], "KT")
+                dve(64, tt(T.S0[:, 8 * c:8 * e_:8], T.KT[:, 384 + c:384 + e_], T.kk[:, c:e_], A.subtract),
+                    yn + ["kk%d" % y for y in hv], ["S0%d" % y for y in hv], "KT")
             if h == 1:
                 tag[0] = "d%d" % t
                 t16, tn = slice(16 * t, 16 * t + 16), str(t)
@@ -326,6 +356,30 @@ def program(g, T, dests, par=None):
                     k = 4 * s + 2 * kind + u
                     x0, xn = 1024 * (k % NX), ["Xa%d" % (k % NX), "Xb%d" % (k % NX)]
                     parts = 2 if k in HALF_TILES else 1
+                    if 2 * s + u in SHARED:
+                        xq = [T.XW[:, 1024 * (2 * h + q):1024 * (2 * h + q + 1)] for q in range(2)]
+                        xn = ["XW%s%d" % (H, q) for q in range(2)]
+                        act(1024 * G, ac(xq[kind], Dw.indirect(offs[:, c0 + 64 * u:c0 + 64 * u + 64]), AF.Copy, scale=rs), [Dn, on, "RS%d" % t], [xn[kind]])
+                        if kind == kinds[0]:
+                            continue
+                        slot, first = [0], len(ops)
+
+                        def vterm(slot=slot, u=u, hs=hs):
+                            for b in range(2):
+                                ins = PE.matmul(DFS[slot[0]][:, 512 * b:512 * b + 512], T.VT[64 * u:64 * u + 64, hs],
+                                                T.E[64 * u:64 * u + 64, 512 * b:512 * b + 512], True, True)
+                            return ins
+                        add("pe", POV + 1024 * FPE, vterm, [xn[kinds[0]], "VT" + H, "E"], ["df%d" % k])
+                        ops[first]["take"] = ("DF", slot)
+                        for q in kinds:
+                            dve(1024, lambda slot=slot, x=xq[q]: V_.tensor_tensor(x, DFS[slot[0]][:], x, A.add),
+                                ["df%d" % k, xn[kinds[0]]], [xn[q]])
+                        ops[-1]["give"] = first
+                        for q in kinds:
+                            kq = (4 * s + 2 * q + u) % NFL
+                            dve(512, ts(T.FL[:, 1024 * kq:1024 * kq + 1024], xq[q], BIG, A.add, s2, A.is_equal),
+                                [xn[q], "S2%d" % t], ["FLa%d" % kq, "FLb%d" % kq])
+                        continue
                     for b in range(parts):
                         m = 64 // parts
                         src = Dw.indirect(offs[:, c0 + 64 * u + m * b:c0 + 64 * u + m * b + m])
@@ -344,13 +398,13 @@ def program(g, T, dests, par=None):
                     def diff(terms, slot=slot, x0=x0, u=u, hs=hs, ds=ds):
                         def fn():
                             for b, side, s0 in terms:
-                                a_, b_ = (T.VT[:, hs], T.E[:, 1024 * u + 512 * b:1024 * u + 512 * b + 512]) if side == "v" else \
+                                a_, b_ = (T.VT[64 * u:64 * u + 64, hs], T.E[64 * u:64 * u + 64, 512 * b:512 * b + 512]) if side == "v" else \
                                     (ds, T.X[:, x0 + 512 * b:x0 + 512 * b + 512])
                                 ins = PE.matmul(DFS[slot[0]][:, 512 * b:512 * b + 512], a_, b_, s0, not s0)
                             return ins
                         rd = [xn[b] for b, side, _ in terms if side == "x"] + ["DS%d" % t] + ["dfa%d" % k] * terms[0][0]
                         rd += ["VT" + H, "E"] if any(side == "v" for _, side, _ in terms) else []
-                        add("pe", 60 + 512 * len(terms) * FPE, fn, rd, ["df%s%d" % ("ab"[b], k) for b in sorted(set(x[0] for x in terms))])
+                        add("pe", POV + 512 * len(terms) * FPE, fn, rd, ["df%s%d" % ("ab"[b], k) for b in sorted(set(x[0] for x in terms))])
                     first = len(ops)
                     s1_, s2_ = "xv" if k in X_FIRST else "vx"
                     if k in X_FIRST or k in V_FIRST:
@@ -416,7 +470,7 @@ def program(g, T, dests, par=None):
                         PE.matmul(DFS[slot[0]][:, 128 * k - 128:128 * k], M[k], tp, True, False)
                         ins = PE.matmul(DFS[slot[0]][:, 128 * k - 128:128 * k], MN[k], tb, False, True)
                     return ins
-                add("pe", 60 + 256 * m * FPE, pairs, ["TB" + H] + ["dp0" + n] * b + [x + str(k) for x in ("M", "MN") for k in range(1, 9)], ["dp%d%s" % (b, n)])
+                add("pe", POV + 256 * m * FPE, pairs, ["TB" + H] + ["dp0" + n] * b + [x + str(k) for x in ("M", "MN") for k in range(1, 9)], ["dp%d%s" % (b, n)])
             ops[first]["take"] = ("DF", slot)
             for b in range(parts):
                 a = 128 * m * b
@@ -431,10 +485,8 @@ def program(g, T, dests, par=None):
             lend("XU")
             if not last:
                 dve(128 * SCAT, cp(T.PT[:, 0:WX].indirect(T.SO[:, 8 * s:8 * s + 8]), uf), ["UF" + H, "SO%d" % t, "PTx"], ["PT"])
-                if not early:
+                if not early and not mv:
                     dve(128, cp(ul, uf), ["UF" + H], [uln])
-                    if mv:
-                        send(t, T.QU[:, c1:c1 + 128], ul, [uln], ["QU" + n1])
                 affine("QC", 128, LB[:, o1 + 128:o1 + 256], uf, 1.0, -OFF, ["UF" + H], ["QC" + on1])
                 if mv and MERGE < 2:
                     send(t, T.LN[:, l1 + 128:l1 + 256], LB[:, o1 + 128:o1 + 256], ["QC" + on1], ["QC" + n1])
@@ -450,29 +502,25 @@ def program(g, T, dests, par=None):
             sc, l0 = T.SC[:, 256 * h + 31:256 * h + 256:32], 56 * h
             dve(8, ts(T.rr[:, 8 * h:8 * h + 8], sc, B * BIG, A.add, B * BIG, A.subtract), ["SC" + H], ["rr" + H])
             dve(16, tt(T.LS[:, l0 + 24:l0 + 32], sc, T.rr[:, 8 * h:8 * h + 8], A.subtract), ["SC" + H, "rr" + H], ["LS" + H])
-            fs = T.FS[0:32, 32 * h:32 * h + 32]
+            fs, fsn = LB[0:32, o1 + 384:o1 + 416], "FS" + on1
             f32, Wr = T.ZQ[0:32, 256 + 32 * h:288 + 32 * h], T.ZQ[:, 320 + 8 * h:328 + 8 * h]
             mm(grp(f32, [(T.LS[:, l0 + 24 - 8 * a:l0 + 56 - 8 * a], T.ID[:, a:128:4]) for a in range(4)], 32), ["LS" + H, "I0"], ["F32" + H], "ZQ")
-            affine("FS", 32, fs, f32, 1.0, 0.0, ["F32" + H], ["FS" + H], "ZQ")
-            mm(grp(Wr, [(I0, d16)] + [(T.BW4[0:32, 12 - 4 * a:140 - 4 * a], T.FS[0:32, 32 * h + a:32 * h + 32:4]) for a in range(4)], 64),
-               ["FS" + H, "BW4", "I0", "d16%d" % t], ["Wr" + H], "ZQ")
+            affine("FS", 32, fs, f32, 1.0, 0.0, ["F32" + H], [fsn], "ZQ")
+            mm(grp(Wr, [(I0, d16)] + [(T.BW4[0:32, 12 - 4 * a:140 - 4 * a], LB[0:32, o1 + 384 + a:o1 + 416:4]) for a in range(4)], 64),
+               [fsn, "BW4", "I0", "d16%d" % t], ["Wr" + H], "ZQ")
             dve(8, ts(fu, Wr, OFF, A.add), ["Wr" + H], ["FU" + n], "ZQ")
             dve(128 * G, tt(vo, D[t][:, 0:WX].indirect(fu), v, A.subtract), [Dn, Dn + "x", "FU" + n, "V" + n], [vn])
             if not last:
                 if mv:
-                    dve(8, tt(LB[:, o1 + 512:o1 + 520], Wr, d16, A.subtract), ["Wr" + H, "d16%d" % t], ["JW" + on1], "ZQ")
+                    dve(8, tt(LB[:, o1 + 416:o1 + 424], Wr, d16, A.subtract), ["Wr" + H, "d16%d" % t], ["JW" + on1], "ZQ")
+                    parts = ((256, 384, ["DV"]), (384, 424, ["FS", "JW"])) if MERGE == 0 else \
+                        ((384 - 128 * MERGE, 424, ["QC", "DV", "FS", "JW"][2 - MERGE:]),)
+                    for a, b, names in parts:
+                        send(t, T.LN[:, l1 + a:l1 + b], LB[:, o1 + a:o1 + b], [x + on1 for x in names], [x + n1 for x in names], 256 * (b - a))
                 else:
                     dve(8, tt(T.JF[:, 8 * s1:8 * s1 + 8], Wr, d16, A.subtract), ["Wr" + H, "d16%d" % t], ["JF" + n1], "ZQ")
-                mm([(T.ZP[:, 384 + a:512:4], T.R4[0:32, 128 * a:128 * a + 128], fs, True, True, 64) for a in range(4)], ["FS" + H, "R4"], ["RR" + n], "ZP")
-                affine("JR", 128, LB[:, o1 + 384:o1 + 512], RR, 1.0, 0.0, ["RR" + n], ["JR" + on1], "ZP")
-                lend("RR")
-                if mv:
-                    parts = ((256, 384, ["DV"]), (384, 520, ["JR", "JW"])) if MERGE == 0 else \
-                        ((384 - 128 * MERGE, 520, ["QC", "DV", "JR", "JW"][2 - MERGE:]),)
-                    for a, b, names in parts:
-                        send(t, T.LN[:, l1 + a:l1 + b], LB[:, o1 + a:o1 + b], [x + on1 for x in names], [x + n1 for x in names])
             else:
-                mm([(T.ZP[0:8, 384 + a:512:4], T.ID[0:32, 8 * a:8 * a + 8], fs, True, True, 32) for a in range(4)], ["FS" + H, "I0"], ["RR" + n], "ZP")
+                mm([(T.ZP[0:8, 384 + a:512:4], T.ID[0:32, 8 * a:8 * a + 8], fs, True, True, 32) for a in range(4)], [fsn, "I0"], ["RR" + n], "ZP")
                 affine("YJ", 128, T.YJ[0:8, hs], T.ZP[0:8, 384:512], 1.0, OFF, ["RR" + n], ["YJ" + H], "ZP")
                 lend("RR")
                 dma(T.yj[:, hs], T.YJ[0:8, hs], 4096, ["YJ" + H], ["yj" + H])
@@ -485,7 +533,7 @@ def slots(what):
     return 2 if what == "DF" else 1
 
 
-def schedule(ops, deps0, succ, pr):
+def schedule(ops, deps0, succ, pr, WIN=WIN):
     n = len(ops)
     left = [len(d) for d in deps0]
     ready = {k: 0.0 for k in range(n) if left[k] == 0}
@@ -583,7 +631,7 @@ def queued(r, a, done, deps0):
     return out, prev
 
 
-def refine(ops, deps0, cur, alt):
+def refine(ops, deps0, cur, alt, MOVES, TEMP, SEED):
     n, eng = len(ops), [o[0] for o in alt[0][0]]
     dones = [ends(cur, a, [0.0] * n, 0, 1e18) for a in alt]
     vals = [max(d) / a[2] for d, a in zip(dones, alt)]
@@ -732,7 +780,18 @@ def plan(ops, others=()):
             v_ = replay(r, alt)
             if v_ <= val:
                 best, pr, val = r, q, v_
-        PLANS[n] = refine(use, deps, best, alt)
+        for rnd in range(ROUNDS):
+            best = refine(use, deps, best, alt, MOVES, TEMP * (1 - rnd / ROUNDS), SEED + rnd)
+            kept = min(kept, best, key=lambda r: replay(r, alt)) if rnd else best
+            done = ends(best, alt[0], [0.0] * n, 0, 1e18)
+            start = [ops[k]["dur"] + ops[k]["lat"] - done[k] for k in range(n)]
+            for win in (0.0, 200.0, 500.0, 1000.0):
+                r = decode(use, deps, schedule(ops, deps, succ, start, win))
+                if r is not None and replay(r, alt) < replay(best, alt) + (SLACK if rnd < ROUNDS - 1 else 0.0):
+                    best = r
+                    break
+        order, deps, slot = min(kept, best, key=lambda r: replay(r, alt))
+        PLANS[n] = (list(range(LOADS)) + [k for k in order if k >= LOADS], deps, slot)
     order, deps, slot = PLANS[n]
     for j, k in enumerate(order):
         ops[k]["t0"] = j

from concourse.mybir import AluOpType, ActivationFunctionType, AxisListType

A = AluOpType
AF = ActivationFunctionType
W = 3584
WX = 4112
ZONE = 260
OFF = 1792.0
B = 4096.0
BIG = 1.5 * 2.0 ** 23
HOP = (1, 0, 2, 0)
DVE_TILES = (2,)
X_FIRST, V_FIRST = (8, 9, 16, 17, 24, 25), ()
HALF_PAIRS = (1, 3, 5, 7)
Q_LAST = ()
HALF_TILES = range(3, 32, 4)
ACT_FLAGS = ()
EARLY = (0, 2, 4)
SPLIT_SG = (0, 1)
ON_ACT = ("FS", "JR", "TO", "QC", "YJ", "DS", "JF", "Y01")
MERGE = 0
LW = 432
WHOLE = (0,)
SHARED = ()
PU_ACT = (1,)
NX, NAB, NFL, LOADS = 8, 4, 8, 6
PARS = [(0.83, 1.56, 3.8, 80.0, 1800.0, 35.0, 64, 60.0, 0.415, 1300.0, 270.0, 250.0),
        (1.0, 1.2, 2.5, 120.0, 2600.0, 45.0, 48, 40.0, 0.5, 1000.0, 330.0, 800.0),
        (1.2, 1.9, 5.0, 90.0, 1500.0, 35.0, 64, 60.0, 0.6, 1500.0, 230.0, 150.0)]
MEAN, FREE, ROUNDS, SLACK = 1.0, 3, 16, 2500.0
HOPNS, MIX, WIN, ITER, SEED, AMP, MOVES, TEMP = 100.0, 50.0, 100.0, 40, 4, 10.0, 4000, 500.0


def _sb(d, **kw):
    return {k: ("sbuf", [128] + (list(v) if isinstance(v, tuple) else [v]), d) for k, v in kw.items()}


SCRATCH = {}
SCRATCH.update(_sb("bfloat16", D0=WX, D1=WX, D2=WX, D3=WX, D4=WX, V=1280, X=NX * 1024, AB=NAB * 1024, FL=NFL * 1024,
                   AN=1024, EO=(16, 256), EC=(8, 128), WR=1024, SG=512, DJ=256, ND=256, RL=512,
                   ones=128, E=1024, ID=10 * 128, blk=384, C3=(8, 32), M=16 * 128, MN=9 * 128, Bs=256, BW2=144, BW4=144, R4=512,
                   mk2=256, JH=64, JL=64, S2=64, SU=520, b8=8, bv=32, bw=32, bj=32))
SCRATCH.update(_sb("float16", LN=10 * LW, LO=6 * LW, JR=1024, NF=2048, TB=512, LS=112, XW=4096, Y0=256, VT=256, DS=512,
                   cm=32, SP=32, d16=64))
SCRATCH.update(_sb("int32", PT=WX, q0i=256, j0i=16, wai=2, pi=4))
SCRATCH.update(_sb("uint16", QU=1280, PU=1024, UL=1024, JU=64, FU=64, SO=64, AU=8))
SCRATCH.update(_sb("float32", waf=2, JF=64, sb=64, AC=8, U2=4, RS=64, ST=520, S0=512, SC=512, UF=256, TO=256, YJ=256, kk=64, rr=16,
                   pf=12, r144=144, rg=128, rc=256, r4=512, m16=16, pw=48))
SCRATCH.update({k: ("psum", [128, n], "float32") for k, n in (("DF0", 1024), ("DF1", 1024), ("ZP", 512), ("ZQ", 512), ("KT", 512), ("MI", 512))})
SEMAPHORES = ["pe", "dve", "act", "pool", "sent"] + ["m%d" % k for k in range(30)] + ["a%d" % k for k in range(16)]


def program(g, T, dests, par=None):
    ops = []
    F, G, SCAT, _, XFER, VOV, VMIN, POV, FPE, DMA0, RATE, CALL = par or PARS[0]
    nd = [0, 0]
    V_, S_, PE = g.vector, g.scalar, g.tensor
    tag = [""]

    def add(eng, dur, fn, r, w, banks=(), sem=None, lat=0.0, cnt=0):
        ops.append({"eng": eng, "dur": dur, "fn": fn, "r": list(r), "w": list(w), "banks": banks, "sem": sem, "lat": lat, "cnt": cnt,
                    "tag": tag[0]})

    def lend(what, slot=None):
        ops[-2]["take"] = (what, slot or [0])
        ops[-1]["give"] = len(ops) - 2

    def dve(n, fn, r, w, *banks):
        add("dve", VOV + max(n, VMIN) * F, fn, r, w, banks)

    def act(n, fn, r, w, *banks):
        add("act", VOV + 15 + max(n, VMIN) * F, fn, r, w, banks)

    def pool(base, n, fn, r, w):
        add("pool", base + 2 * n * F, fn, r, w)

    def mm(lst, r, w, *banks):
        def fn():
            ins = None
            for (o, a, b, s0, s1, n) in lst:
                ins = PE.matmul(o, a, b, s0, s1)
            return ins
        add("pe", POV + sum(x[5] for x in lst) * FPE, fn, r, w, banks)

    def grp(out, terms, n):
        return [(out, a, b, k == 0, k == len(terms) - 1, n) for k, (a, b) in enumerate(terms)]

    def dma(out, in_, nbytes, r, w):
        k = nd[0]
        nd[0] += 1
        add("sp", 60.0, lambda: g.sync.dma_start(out, in_), r, w, (), "m%d" % k, DMA0 + nbytes / RATE, 16)

    def send(t, out, in_, r, w, nbytes=32768):
        k = nd[1]
        nd[1] += 1
        rid, pid, mask, ne = dests[t]
        add("pool", CALL if k else CALL + 1400.0, lambda: g.remote_dma(out, in_, T.sem["a%d" % k], T.sem.sent, pid, rid, mask), r, w, (), "a%d" % k,
            XFER + nbytes / 40.0, ne)

    def ts(out, in0, s1, op0, s2=None, op1=None):
        if op1 is None:
            return lambda: V_.tensor_scalar(out, in0, s1, None, op0)
        return lambda: V_.tensor_scalar(out, in0, s1, s2, op0, op1)

    def tt(out, a, b, op):
        return lambda: V_.tensor_tensor(out, a, b, op)

    def cp(out, a):
        return lambda: V_.tensor_copy(out, a)

    def ms(out, c):
        return lambda: V_.memset(out, c)

    def ac(out, a, f, **kw):
        return lambda: S_.activation(out, a, f, **kw)

    def iota(out, pat):
        return lambda: g.iota(out, pat, 0, 0, allow_small_or_imprecise_dtypes=True)

    def affine(what, n, out, a, scale, bias, r, w, *banks):
        if what in ON_ACT:
            act(n, ac(out, a, AF.Identity, bias=bias, scale=scale) if bias else ac(out, a, AF.Copy, scale=scale), r, w, *banks)
        else:
            dve(n, ts(out, a, scale, A.mult, bias, A.add), r, w, *banks)

    D = [T.D0, T.D1, T.D2, T.D3, T.D4]
    dma(T.j0i[:], T.j0[:], 8192, [], ["j0i"])
    dma(T.wai[:], T.wa[:], 10000, [], ["wai"])
    dma(T.q0i[:], T.q0[:], 140000, [], ["q0i"])
    dma(T.D0[:, 0:W], T.d0[:], 1060000, [], ["D0"])
    dma(T.V[:, 0:256], T.v0[:], 1125000, [], ["V00", "V01"])
    dma(T.PT[:, 0:W], T.p0[:], 2960000, [], ["PT"])
    dve(W / 2, cp(T.D1[:, 0:W], T.D0[:, 0:W]), ["D0"], ["D1"])
    add("pool", 150, lambda: g.iota(T.pi[:, 0:1], [[0, 1]], 0, 1), [], ["pi0"])
    pool(130, 144, iota(T.r144[:], [[1, 144]]), [], ["r144"])
    pool(130, 128, iota(T.rg[:], [[1, 8], [0, 16]]), [], ["rg"])
    pool(130, 256, iota(T.rc[:], [[0, 16], [1, 16]]), [], ["rc"])
    dve(64, ms(T.ones[:], 1.0), [], ["ones"])
    dve(128, ms(T.Bs[:], B), [], ["Bs"])
    pool(130, 1024, iota(T.AN[:], [[1, 64], [0, 16]]), [], ["AN"])
    dve(1, ts(T.JH[:, 0:1], T.pi[:, 0:1], 63.5, A.is_gt, -64.0, A.mult), ["pi0"], ["JH00"])
    dve(1, tt(T.JL[:, 0:1], T.pi[:, 0:1], T.JH[:, 0:1], A.add), ["pi0", "JH00"], ["JL00"])
    dve(512, ts(T.E[:], T.AN[:], T.JL[:, 0:1], A.is_equal, -1.0, A.mult), ["AN", "JL00"], ["E"])
    pool(170, 256, lambda: g.affine_select(T.C3[:], T.Bs[:], [[-16, 8], [0, 2], [-1, 16]], A.is_equal, 0.0, 0, 1), ["Bs"], ["C3"])
    M = [T.M[:, 128 * k:128 * k + 128] for k in range(16)]
    MN = [T.MN[:, 128 * k:128 * k + 128] for k in range(9)]
    for k in range(1, 16):
        pool(170, 128, lambda k=k: g.affine_select(M[k], T.C3[:, :, k:k + 16], [[-1, 128]], A.not_equal, B, 0, 1), ["C3"], ["M%d" % k])
        if k <= 8:
            act(128, ac(MN[k], M[k], AF.Copy, scale=-1.0), ["M%d" % k], ["MN%d" % k])
    pool(130, 512, iota(T.r4[:], [[1, 32], [0, 16]]), [], ["r4"])
    pool(130, WX - W, lambda: g.iota(T.PT[:, W:WX], [[0, WX - W]], 0, 0), [], ["PTx"])
    for t in range(5):
        pool(130, WX - W, iota(D[t][:, W:WX], [[0, WX - W]]), [], ["D%dx" % t])
    dve(512, ms(T.S0[:], 1.0e9), [], ["S00", "S01"])
    dve(64, ms(T.kk[:], -1.0e9), [], ["kk0", "kk1"])
    dve(16, ms(T.kk[:, 1:64:4], 0.0), [], ["kk0", "kk1"])
    for s in (0, 1, 4, 5):
        act(32, ac(T.LO[:, LW * s + 384:LW * s + 416], T.ones[:, 0:32], AF.Copy), ["ones"], ["FSo%d%d" % divmod(s, 2)])
    dve(56, ts(T.LS[:], T.ones[:, 0:112], 0.0, A.mult), ["ones"], ["LS0", "LS1"])
    dve(1, ts(T.pi[:, 1:2], T.pi[:, 0:1], 15, A.bitwise_and), ["pi0"], ["pi1"])
    dve(1, ts(T.pi[:, 2:3], T.pi[:, 0:1], 4, A.arith_shift_right), ["pi0"], ["pi2"])
    dve(1, cp(T.pf[:, 0:3], T.pi[:, 0:3]), ["pi0", "pi1", "pi2"], ["pf"])
    p_, pm, pg = T.pf[:, 0:1], T.pf[:, 1:2], T.pf[:, 2:3]
    r8 = T.r144[:, 0:8]
    I0, In, I16, Iwp, Iwn, Io, Ip, Ih, Inh, Ib = [T.ID[:, 128 * k:128 * k + 128] for k in range(10)]
    dve(128, ts(I0, T.r144[:, 0:128], p_, A.is_equal), ["pf", "r144"], ["I0"])
    for k, val in ((1, -1.0), (2, -16.0), (3, 1024.0), (4, -1024.0), (5, -OFF), (6, OFF), (7, B), (8, -B), (9, -B / 2)):
        act(128, ac(T.ID[:, 128 * k:128 * k + 128], I0, AF.Copy, scale=val), ["I0"], ["I%d" % k])
    IRp, IRq = M[0], MN[0]
    for k, (dst, c) in enumerate(((IRp, B), (IRq, 2 * B))):
        dve(1, ts(T.pf[:, 4 + k:5 + k], pg, -4 * B, A.mult, 28 * B + c, A.add), ["pf"], ["pf%d" % (4 + k)])
        act(128, ac(dst, I0, AF.Copy, scale=T.pf[:, 4 + k:5 + k]), ["I0", "pf%d" % (4 + k)], ["IR%d" % k])
    blk, blkC, blkW = T.blk[:, 0:128], T.blk[:, 128:256], T.blk[:, 256:384]
    dve(128, ts(blk, T.rg[:], pg, A.is_equal), ["pf", "rg"], ["blk"])
    act(128, ac(blkC, blk, AF.Copy, scale=131072.0), ["blk"], ["blkC"])
    dve(16, ts(T.m16[:], T.r144[:, 0:16], pm, A.is_equal), ["pf", "r144"], ["m16"])
    dve(16, ms(T.pw[:, 0:16], 0.5), [], ["pw0"])
    dve(16, lambda: V_.tensor_tensor_scan(T.pw[:, 16:32], T.pw[:, 0:16], T.ones[:, 0:16], 65536.0, A.mult, A.mult), ["pw0", "ones"], ["pw1"])
    dve(32, tt(T.pw[:, 32:48], T.pw[:, 16:32], T.m16[:], A.mult), ["pw1", "m16"], ["pw2"])
    dve(16, lambda: V_.tensor_reduce(T.pf[:, 6:7], T.pw[:, 32:48], AxisListType.X, A.add), ["pw2"], ["pf6"])
    act(128, ac(blkW, blk, AF.Copy, scale=T.pf[:, 6:7]), ["blk", "pf6"], ["blkW"])
    dve(256, ts(T.mk2[:], T.rc[:], pm, A.is_equal, -2.0, A.mult), ["pf", "rc"], ["mk2"])
    dve(1, ts(T.pf[:, 7:8], pm, 0.0, A.is_equal, p_, A.mult), ["pf"], ["pf7"])
    dve(1, ts(T.pf[:, 8:9], pm, -200.0, A.mult, T.pf[:, 7:8], A.add), ["pf", "pf7"], ["pf8"])
    dve(144, ts(T.BW2[:, 15:144], T.r144[:, 0:129], T.pf[:, 8:9], A.is_equal, 2304.0, A.mult), ["pf8", "r144"], ["BW2"])
    dve(8, ms(T.BW2[:, 0:15], 0.0), [], ["BW2a"])
    dve(1, ts(T.pi[:, 3:4], T.pi[:, 0:1], 3, A.arith_shift_right), ["pi0"], ["pi3"])
    dve(1, ts(T.pf[:, 9:10], T.pi[:, 3:4], -127.0, A.mult, 12.0, A.add), ["pi3"], ["pf9"])
    dve(1, ts(T.pf[:, 10:11], p_, 16.0, A.mult, T.pf[:, 9:10], A.add), ["pf", "pf9"], ["pf10"])
    dve(144, ts(T.BW4[:], T.r144[:], T.pf[:, 10:11], A.is_equal), ["pf10", "r144"], ["BW4"])
    dve(512, ts(T.R4[:], T.r4[:], p_, A.is_equal), ["pf", "r4"], ["R4"])
    for z in range(2):
        dve(1, ts(T.pf[:, 11:12], pm, W + ZONE * z + 2.0 - OFF - 2304.0, A.add), ["pf"], ["pf11"])
        dve(16, ts(T.SP[:, 16 * z:16 * z + 16], T.r144[:, 0:16], 16.0, A.mult, T.pf[:, 11:12], A.add), ["r144", "pf11"], ["SP%d" % z])
    dve(8, ts(T.b8[:], r8, pg, A.is_equal), ["pf", "r144"], ["b8"])
    dve(2, cp(T.waf[:], T.wai[:]), ["wai"], ["waf"])
    for buf, nm in ((T.bv, "bv"), (T.bw, "bw"), (T.bj, "bj")):
        pool(130, 32, iota(buf[:], [[0, 32]]), [], [nm])
    act(32, ac(T.cm[:], T.ones[:, 0:32], AF.Copy, scale=0.0), ["ones"], ["cm"])
    for c in (0, 2):
        act(8, ac(T.bv[:, c:32:4], T.b8[:], AF.Copy, scale=T.waf[:, 0:1]), ["b8", "waf"], ["bv"])
    act(8, ac(T.bw[:, 1:32:4], T.b8[:], AF.Copy, scale=-384.0), ["b8"], ["bw"])
    act(8, ac(T.bj[:, 1:32:4], T.b8[:], AF.Copy, scale=1 / 16.0), ["b8"], ["bj"])
    for c, m_, a_ in ((0, -128.0, 914.0), (1, -128.0, 912.0), (2, 0.0, -511.5 / 128)):
        act(8, ac(T.cm[:, c:32:4], r8, AF.Identity, scale=m_, bias=a_), ["r144"], ["cm"])
    dve(1, ts(T.pf[:, 3:4], T.waf[:, 1:2], 2.0, A.mult, -1.0, A.add), ["waf"], ["a2"])
    dve(4, ts(T.U2[:], T.r144[:, 0:4], 2.0, A.mult, T.pf[:, 3:4], A.add), ["a2", "r144"], ["U2"])
    dve(210, lambda: V_.reciprocal(T.RS[:, 0:4], T.U2[:]), ["U2"], ["RS0"])
    dve(1, ts(T.S2[:, 0:1], T.pf[:, 3:4], 0.0, A.is_gt, BIG, A.mult), ["a2"], ["S20"])
    pool(130, 520, iota(T.ST[:], [[0, 520]]), [], ["ST"])
    for k in range(4):
        act(65, ac(T.ST[:, 2 * k:520:8], T.ones[:, 0:65], AF.Copy, scale=T.RS[:, k:k + 1]), ["RS0"], ["ST"])
    pool(130, 520, lambda: g.iota(T.SU[:], [[0, 520]], int(BIG), 0, allow_small_or_imprecise_dtypes=True), [], ["SU"])
    dve(65, ts(T.SU[:, 0:520:8], T.ones[:, 0:65], T.S2[:, 0:1], A.mult), ["S20"], ["SU"])
    ones128 = T.ones[:, 0:128]
    zPA, US, RR = T.ZP[:, 0:256], T.ZP[:, 256:384], T.ZP[:, 384:512]
    vTp, xW = T.ZQ[:, 128:256], T.ZQ[:, 336:352]
    XU = T.KT[:, 256:384]
    penP, penQ = T.MI[:, 256:384], T.MI[:, 384:512]
    for h in range(2):
        n = "0%d" % h
        dve(128, cp(T.QU[:, 128 * h:128 * h + 128], T.q0i[:, 128 * h:128 * h + 128]), ["q0i"], ["QU" + n])
        dve(128, ts(T.LN[:, LW * h + 128:LW * h + 256], T.q0i[:, 128 * h:128 * h + 128], -OFF, A.add), ["q0i"], ["QC" + n])

    DFS = [T.DF0, T.DF1]
    for t in range(4):
        last = t == 3
        Dn, Dw = "D%d" % t, D[t][:, 0:W]
        tag[0] = "s%d" % t
        rs, s2, ds = T.RS[:, 16 * t:16 * t + 1], T.S2[:, 16 * t:16 * t + 1], T.DS[:, 128 * t:128 * t + 128]
        if t:
            k, au = 2 * t - 1, T.AU[:, 2 * t:2 * t + 1]
            if t - 1 in WHOLE:
                dve(1, ts(au, T.AC[:, k:k + 1], 256.0, A.add), ["AC%d1" % (t - 1)], ["AU%d" % t])
            else:
                dve(1, ts(au, T.AC[:, k:k + 1], T.AC[:, k - 1:k], A.add, 256.0, A.add), ["AC%d0" % (t - 1), "AC%d1" % (t - 1)], ["AU%d" % t])
            act(16 * G, ac(T.RS[:, 16 * t:16 * t + 16], T.ST[:, 0:520].indirect(au), AF.Copy), ["AU%d" % t, "ST"], ["RS%d" % t])
            act(16 * G, ac(T.S2[:, 16 * t:16 * t + 16], T.SU[:, 0:520].indirect(au), AF.Copy), ["AU%d" % t, "SU"], ["S2%d" % t])
            dma(D[t + 1][:, 0:W], D[t][:, 0:W], 917504, [Dn] + (["DV%d0" % t] if HOP[t - 1] else []), ["D%d" % (t + 1)])
        affine("DS", 128, ds, I0, rs, 0.0, ["I0", "RS%d" % t], ["DS%d" % t])
        for h in range(2):
            n, H, s, c0 = "%d%d" % (t, h), str(h), 2 * t + h, 256 * t + 128 * h
            hs = slice(128 * h, 128 * h + 128)
            v, pu, wr = [b[:, c0:c0 + 128] for b in (T.V, T.PU, T.WR)]
            pc, qc = T.LN[:, LW * s:LW * s + 128], T.LN[:, LW * s + 128:LW * s + 256]
            jr, jw = T.JR[:, c0:c0 + 128], T.LN[:, LW * s + 416:LW * s + 424]
            ju, jf = [b[:, 8 * s:8 * s + 8] for b in (T.JU, T.JF)]
            tag[0] = "e" + n
            if t == 0:
                dve(8, cp(ju, T.j0i[:, 8 * h:8 * h + 8]), ["j0i"], ["JU" + n])
                dve(8, ts(jf, T.j0i[:, 8 * h:8 * h + 8], -OFF, A.add), ["j0i"], ["JF" + n])
            elif HOP[t - 1]:
                dve(8, ts(ju, jw, OFF, A.add), ["JW" + n], ["JU" + n])
                affine("JF", 8, jf, jw, 1.0, 0.0, ["JW" + n], ["JF" + n])
            else:
                dve(8, ts(ju, jf, OFF, A.add), ["JF" + n], ["JU" + n])
            if t == 0:
                for b in range(8):
                    affine("Y0%d" % h, 16, T.Y0[:, 128 * h + 16 * b:128 * h + 16 * b + 16], T.m16[:], T.JF[:, 8 * h + b:8 * h + b + 1], 0.0,
                           ["m16", "JF" + n], ["Y0%s%d" % (H, b)])
                mm(grp(RR, [(blk, T.Y0[:, hs])], 128), ["blk"] + ["Y0%s%d" % (H, b) for b in range(8)], ["RE" + n], "ZP")
            else:
                mm([(T.ZP[:, 384 + a:512:4], T.R4[0:32, 128 * a:128 * a + 128], T.LN[0:32, LW * s + 384:LW * s + 416], True, True, 64)
                    for a in range(4)], ["FS" + n, "R4"], ["RE" + n], "ZP")
            affine("JR", 128, jr, RR, 1.0, 0.0, ["RE" + n], ["JR" + n], "ZP")
            lend("RR")
            if t and HOP[t - 1] and s - 2 not in EARLY:
                dve(64, ts(T.QU[:, c0:c0 + 128], qc, OFF, A.add), ["QC" + n], ["QU" + n])
            dv, dvn = (v, "V" + n) if t == 0 else (T.LN[:, LW * s + 256:LW * s + 384], "DV" + n)
            if t:
                act(128, ac(v, dv, AF.Abs), [dvn], ["V" + n])
            mm(grp(vTp, [(dv, ds)], 128), [dvn, "DS%d" % t], ["vTp" + n], "ZQ")
            act(128, ac(T.VT[:, hs], vTp, AF.Abs), ["vTp" + n], ["VT" + H], "ZQ")
            lend("vT")
            tag[0] = "p" + n
            if s in PU_ACT:
                act(128 * G, ac(pc, T.PT[:, 0:W].indirect(ju), AF.Identity, bias=-OFF), ["PT", "JU" + n], ["PC" + n])
                dve(64, ts(pu, pc, OFF, A.add), ["PC" + n], ["PU" + n])
            else:
                dve(128 * G, cp(pu, T.PT[:, 0:W].indirect(ju)), ["PT", "JU" + n], ["PU" + n])
                dve(64, ts(pc, pu, -OFF, A.add), ["PU" + n], ["PC" + n])
            if s in SPLIT_SG:
                for kind, (pen, e_, en_) in enumerate(((penQ, qc, "QC"), (penP, pc, "PC"))):
                    g0 = 256 * h + 128 * (1 - kind)
                    mm(grp(pen, [(I0, e_), (In, jr)], 128), ["I0", "I1", en_ + n, "JR" + n], ["pen%s%d" % (n, kind)], "MI")
                    act(128, ac(T.SG[:, g0:g0 + 128], pen, AF.Sign, bias=-0.5), ["pen%s%d" % (n, kind)], ["SG%s%d" % (H, kind)], "MI")
                    lend("pen")
            else:
                mm(grp(penP, [(I0, pc), (In, jr)], 128) + grp(penQ, [(I0, qc), (In, jr)], 128),
                   ["I0", "I1", "PC" + n, "QC" + n, "JR" + n], ["pen" + n], "MI")
                act(256, ac(T.SG[:, 256 * h:256 * h + 256], T.MI[:, 256:512], AF.Sign, bias=-0.5), ["pen" + n], ["SG%s0" % H, "SG%s1" % H], "MI")
                lend("pen")
            for lo in ([0] if h else []) if t in WHOLE else [h]:
                tag[0] = "w" + n
                hv = range(lo, h + 1)
                nm = lambda x, hv=hv: ["%s%d%d" % (x, t, y) for y in hv]
                a, z, j0 = 128 * lo, 128 * h + 128, 256 * t
                c8 = slice(16 * t + 8 * lo, 8 * s + 8)
                jx, jxn = (jw, nm("JW")) if t and HOP[t - 1] and lo == h else (T.JF[:, c8], nm("JF"))
                dve(16, ts(T.JH[:, c8], jx, 16 * BIG, A.add, 16 * BIG, A.subtract), jxn, nm("JH"))
                dve(32, tt(T.JL[:, c8], jx, T.JH[:, c8], A.subtract), jxn + nm("JH"), nm("JL"))
                cw = T.MI[:, a:z]
                terms, rd = [(cw, blkW, T.mk2[:, 0:z - a], True, False, z - a)], ["blkC", "blkW", "mk2"]
                for b in range(8 * h + 8):
                    c, m = 16 * t + b, z - max(a, 16 * b)
                    e_, en = (T.EC[:, b, :], "EC%d" % b) if 16 * b < a else (T.EO[:, b, 0:m], "EO%d" % b)
                    dve(m / 2, ts(e_, T.JR[:, j0 + z - m:j0 + z], T.JH[:, c:c + 1], A.subtract, T.JL[:, c:c + 1], A.is_equal),
                        nm("JR") + ["JL%d%d" % (t, b // 8)], [en])
                    rd.append(en)
                    if 16 * b < a:
                        terms.append((cw, blkC, e_, False, False, m))
                    elif m > 16:
                        terms.append((T.MI[:, 16 * b + 16:z], blkC, T.EO[:, b, 16:m], False, False, max(64, m - 16)))
                terms.append((cw, blkW, T.EO[:, 8 * lo:8 * h + 8, 0:16], False, True, z - a))
                mm(terms, rd, ["cw" + n], "MI")
                act(z - a, ac(T.WR[:, j0 + a:j0 + z], cw, AF.Sign, bias=0.5, accum_out=T.AC[:, s:s + 1]), ["cw" + n], nm("WR") + ["AC" + n], "MI")
                lend("cw")
                tag[0] = "y" + n
                lst = []
                for y in hv:
                    c = slice(j0 + 128 * y, j0 + 128 * y + 128)
                    lst += grp(T.KT[:, 384 + 32 * y:416 + 32 * y], [(ones128, T.cm[:]), (T.V[:, c], T.bv[:]), (T.JR[:, c], T.bj[:]), (T.WR[:, c], T.bw[:])], 64)
                yn, c, e_ = ["y%d" % y for y in hv], 32 * lo, 32 * h + 32
                mm(lst, nm("WR") + nm("JR") + nm("V") + ["ones", "bv", "bw", "bj", "cm"], yn, "KT")
                dve(16, ts(T.kk[:, c:e_:4], T.KT[:, 384 + c + 2:384 + e_:4], 1024 * BIG, A.add, 1024 * BIG, A.subtract), yn, ["kk%d" % y for y in hv], "KT")
                dve(64, tt(T.S0[:, 8 * c:8 * e_:8], T.KT[:, 384 + c:384 + e_], T.kk[:, c:e_], A.subtract),
                    yn + ["kk%d" % y for y in hv], ["S0%d" % y for y in hv], "KT")
            if h == 1:
                tag[0] = "d%d" % t
                t16, tn = slice(16 * t, 16 * t + 16), str(t)
                mm(grp(xW, [(I0, T.SP[:, 16 * (t % 2):16 * (t % 2) + 16])]
                       + [(T.BW2[:, 15 - a:143 - a], T.WR[:, 256 * t + a:256 * t + 256:16]) for a in range(16)], 64),
                   ["I0", "SP0", "SP1", "BW2", "BW2a", "WR%d0" % t, "WR" + n], ["xW"], "ZQ")
                dve(16, tt(T.sb[:, t16], xW, T.JF[:, t16], A.max), ["xW", "JF%d0" % t, "JF" + n], ["sb" + tn], "ZQ")
                dve(16, ts(T.SO[:, t16], T.sb[:, t16], OFF, A.add), ["sb" + tn], ["SO" + tn])
                dve(32, tt(T.d16[:, t16], T.sb[:, t16], T.JF[:, t16], A.subtract), ["sb" + tn, "JF%d0" % t, "JF" + n], ["d16" + tn])
                dve(256 * G, tt(T.DJ[:], Dw.indirect(T.JU[:, t16]), T.V[:, 256 * t:256 * t + 256], A.subtract),
                    [Dn, "JU%d0" % t, "JU" + n, "V%d0" % t, "V" + n], ["DJ"])
                act(256, ac(T.ND[:], T.DJ[:], AF.Abs), ["DJ"], ["ND"])
                dve(256 * SCAT, cp(D[t + 1][:, 0:WX].indirect(T.SO[:, t16]), T.ND[:]), ["ND", "SO" + tn],
                    ["D%d" % (t + 1), "D%dx" % (t + 1)])
                if last:
                    dma(T.yd[:], T.D4[:, 0:W], 917504, ["D4"], ["yd"])
        for h in range(2):
            n, H, s, c0 = "%d%d" % (t, h), str(h), 2 * t + h, 256 * t + 128 * h
            hs = slice(128 * h, 128 * h + 128)
            v, pu, wr = [b[:, c0:c0 + 128] for b in (T.V, T.PU, T.WR)]
            pc, qc = T.LN[:, LW * s:LW * s + 128], T.LN[:, LW * s + 128:LW * s + 256]
            fu, d16 = [b[:, 8 * s:8 * s + 8] for b in (T.FU, T.d16)]
            kinds = (1, 0) if 4 * s in Q_LAST or 4 * s + 1 in Q_LAST else (0, 1)
            for kind in kinds:
                tag[0] = "g%s%d" % (n, kind)
                offs, on = (T.QU, "QU" + n) if kind == 0 else (T.PU, "PU" + n)
                for u in range(2):
                    k = 4 * s + 2 * kind + u
                    x0, xn = 1024 * (k % NX), ["Xa%d" % (k % NX), "Xb%d" % (k % NX)]
                    parts = 2 if k in HALF_TILES else 1
                    if 2 * s + u in SHARED:
                        xq = [T.XW[:, 1024 * (2 * h + q):1024 * (2 * h + q + 1)] for q in range(2)]
                        xn = ["XW%s%d" % (H, q) for q in range(2)]
                        act(1024 * G, ac(xq[kind], Dw.indirect(offs[:, c0 + 64 * u:c0 + 64 * u + 64]), AF.Copy, scale=rs), [Dn, on, "RS%d" % t], [xn[kind]])
                        if kind == kinds[0]:
                            continue
                        slot, first = [0], len(ops)

                        def vterm(slot=slot, u=u, hs=hs):
                            for b in range(2):
                                ins = PE.matmul(DFS[slot[0]][:, 512 * b:512 * b + 512], T.VT[64 * u:64 * u + 64, hs],
                                                T.E[64 * u:64 * u + 64, 512 * b:512 * b + 512], True, True)
                            return ins
                        add("pe", POV + 1024 * FPE, vterm, [xn[kinds[0]], "VT" + H, "E"], ["df%d" % k])
                        ops[first]["take"] = ("DF", slot)
                        for q in kinds:
                            dve(1024, lambda slot=slot, x=xq[q]: V_.tensor_tensor(x, DFS[slot[0]][:], x, A.add),
                                ["df%d" % k, xn[kinds[0]]], [xn[q]])
                        ops[-1]["give"] = first
                        for q in kinds:
                            kq = (4 * s + 2 * q + u) % NFL
                            dve(512, ts(T.FL[:, 1024 * kq:1024 * kq + 1024], xq[q], BIG, A.add, s2, A.is_equal),
                                [xn[q], "S2%d" % t], ["FLa%d" % kq, "FLb%d" % kq])
                        continue
                    for b in range(parts):
                        m = 64 // parts
                        src = Dw.indirect(offs[:, c0 + 64 * u + m * b:c0 + 64 * u + m * b + m])
                        dst, dn = T.X[:, x0 + 16 * m * b:x0 + 16 * m * (b + 1)], xn[b::parts]
                        rd, wt = [Dn, on], dn
                        if kind == 0 and k in Q_LAST:
                            rd = rd + ["go" + n]
                        if kind == 1 and kinds[0]:
                            wt = wt + ["go" + n]
                        if k in DVE_TILES:
                            dve(16 * m * G, cp(dst, src), rd, wt)
                        else:
                            act(16 * m * G, ac(dst, src, AF.Copy), rd, wt)
                    slot = [0]

                    def diff(terms, slot=slot, x0=x0, u=u, hs=hs, ds=ds):
                        def fn():
                            for b, side, s0 in terms:
                                a_, b_ = (T.VT[64 * u:64 * u + 64, hs], T.E[64 * u:64 * u + 64, 512 * b:512 * b + 512]) if side == "v" else \
                                    (ds, T.X[:, x0 + 512 * b:x0 + 512 * b + 512])
                                ins = PE.matmul(DFS[slot[0]][:, 512 * b:512 * b + 512], a_, b_, s0, not s0)
                            return ins
                        rd = [xn[b] for b, side, _ in terms if side == "x"] + ["DS%d" % t] + ["dfa%d" % k] * terms[0][0]
                        rd += ["VT" + H, "E"] if any(side == "v" for _, side, _ in terms) else []
                        add("pe", POV + 512 * len(terms) * FPE, fn, rd, ["df%s%d" % ("ab"[b], k) for b in sorted(set(x[0] for x in terms))])
                    first = len(ops)
                    s1_, s2_ = "xv" if k in X_FIRST else "vx"
                    if k in X_FIRST or k in V_FIRST:
                        diff([(0, s1_, True), (1, s1_, True)])
                        rest = [[(b, s2_, False)] for b in range(2)]
                    else:
                        rest = [[(b, s1_, True), (b, s2_, False)] for b in range(2)]
                    for terms in (rest if parts == 2 else [rest[0] + rest[1]]):
                        diff(terms)
                    ops[first]["take"] = ("DF", slot)
                    f0, fn_, dn = 1024 * (k % NFL), ["FLa%d" % (k % NFL), "FLb%d" % (k % NFL)], ["dfa%d" % k, "dfb%d" % k]
                    m = 1024 // parts
                    if k in ACT_FLAGS:
                        ab, an = T.AB[:, 1024 * (k % NAB):1024 * (k % NAB) + 1024], "AB%d" % (k % NAB)
                        act(1024, lambda slot=slot, ab=ab: S_.activation(ab, DFS[slot[0]][:], AF.Identity, bias=192.0), dn, [an])
                        ops[-1]["give"] = first
                        dve(512, ts(T.FL[:, f0:f0 + 1024], ab, BIG - 192.0, A.add, s2, A.is_equal), [an, "S2%d" % t], fn_)
                    else:
                        for b in range(parts):
                            dve(m, lambda slot=slot, fl=T.FL[:, f0 + m * b:f0 + m * b + m], s2=s2, a=m * b, m=m:
                                V_.tensor_scalar(fl, DFS[slot[0]][:, a:a + m], BIG, s2, A.add, A.is_equal),
                                dn[b::parts] + ["S2%d" % t] + fn_[:b], fn_[b::parts])
                        ops[-1]["give"] = first
            for kind in range(2):
                tag[0] = "g%s%d" % (n, kind)
                k = 4 * s + 1 + 2 * kind
                f0, g0, z0 = 1024 * ((k - 1) % NFL), 256 * h + 128 * (1 - kind), 384 * kind
                zT, zn = T.ZQ[:, z0:z0 + 128], "zT%s%d" % (n, kind)
                lst = [(zT, T.SG[:, g0:g0 + 128], I16, True, False, 128), (zT, wr, Iwp if kind else Iwn, False, False, 128)]
                lst += [(T.ZQ[:, z0 + i:z0 + 128:16], T.FL[:, f0 + i:f0 + 2048:16], T.b8[:], False, i == 15, 64) for i in range(16)]
                mm(lst, ["b8", "I2", "I3", "I4", "WR" + n, "SG%s%d" % (H, kind)] + ["FL%s%d" % (a, b % NFL) for a in "ab" for b in (k - 1, k)], [zn], "ZQ")
                rl = T.RL[:, 256 * h + 128 * kind:256 * h + 128 * kind + 128]
                act(128, ac(rl, zT, AF.Sign, bias=7.5 + (1024.0 if kind else -1024.0)), [zn], ["RL%s%d" % (H, kind)], "ZQ")
                lend("zT%d" % kind)
            tag[0] = "u" + n
            mv = HOP[t] != 0
            n1, s1, c1 = "%d%d" % (t + 1, h), s + 2, c0 + 256
            l1 = LW * s1
            LB, o1, on1 = (T.LO, LW * s, "o" + n) if mv else (T.LN, l1, n1)
            vo, vn = LB[:, o1 + 256:o1 + 384], "DV" + on1
            ul, uln = (T.UL[:, c0:c0 + 128], "UL" + n) if mv else (T.QU[:, c1:c1 + 128], "QU" + n1)
            rq, rp, rqn, rpn = T.RL[:, 256 * h:256 * h + 128], T.RL[:, 256 * h + 128:256 * h + 256], "RL%s0" % H, "RL%s1" % H
            tp, tb = T.TB[:, 256 * h:256 * h + 128], T.TB[:, 256 * h + 128:256 * h + 256]
            mm(grp(T.ZP[:, 0:128], [(rp, Io)], 128) + grp(T.ZP[:, 128:256], [(rp, Ip)], 128), ["I5", "I6", rpn], ["zPA" + n], "ZP")
            dve(256, tt(T.TB[:, 256 * h:256 * h + 256], zPA, T.LN[:, LW * s:LW * s + 256], A.min), ["zPA" + n, "PC" + n, "QC" + n], ["TB" + H], "ZP")
            lend("zP")
            affine("TO", 128, T.TO[:, hs], tp, 1.0, OFF, ["TB" + H], ["TO" + H])
            early = s in EARLY and not last
            if early:
                mm(grp(US, [(I0, tp), (I0, tb)], 128), ["I0", "TB" + H], ["US" + n], "ZP")
                dve(128, ts(ul, US, 2 * OFF, A.add), ["US" + n], [uln], "ZP")
                lend("US")
                if mv:
                    send(t, T.QU[:, c1:c1 + 128], ul, [uln], ["QU" + n1])
            tag[0] = "r" + n
            slot = [0]

            parts, first = 2 if s in HALF_PAIRS else 1, len(ops)
            m = 8 // parts
            for b in range(parts):
                def pairs(slot=slot, tp=tp, tb=tb, ks=range(1 + m * b, 1 + m * b + m)):
                    for k in ks:
                        PE.matmul(DFS[slot[0]][:, 128 * k - 128:128 * k], M[k], tp, True, False)
                        ins = PE.matmul(DFS[slot[0]][:, 128 * k - 128:128 * k], MN[k], tb, False, True)
                    return ins
                add("pe", POV + 256 * m * FPE, pairs, ["TB" + H] + ["dp0" + n] * b + [x + str(k) for x in ("M", "MN") for k in range(1, 9)], ["dp%d%s" % (b, n)])
            ops[first]["take"] = ("DF", slot)
            for b in range(parts):
                a = 128 * m * b
                dve(128 * m, lambda slot=slot, nf=T.NF[:, 1024 * h + a:1024 * h + a + 128 * m], a=a, m=m:
                    V_.tensor_scalar(nf, DFS[slot[0]][:, a:a + 128 * m], 0.0, 257.0 / 256, A.not_equal, A.subtract),
                    ["dp%d%s" % (b, n)] + ["NF0" + H] * b, ["NF0" + H, "NF1" + H][b::parts])
            ops[-1]["give"] = first
            mm(grp(XU, [(M[16 - k], T.NF[:, 1024 * h + 128 * k - 128:1024 * h + 128 * k]) for k in range(1, 9)] + [(I0, tb), (rq, Ib)], 128),
               ["NF0" + H, "NF1" + H, "TB" + H, rqn, "I0", "I9"] + ["M%d" % k for k in range(8, 16)], ["XU" + n], "KT")
            uf = T.UF[:, hs]
            dve(128, tt(uf, XU, T.TO[:, hs], A.max), ["XU" + n, "TO" + H], ["UF" + H], "KT")
            lend("XU")
            if not last:
                dve(128 * SCAT, cp(T.PT[:, 0:WX].indirect(T.SO[:, 8 * s:8 * s + 8]), uf), ["UF" + H, "SO%d" % t, "PTx"], ["PT"])
                if not early and not mv:
                    dve(128, cp(ul, uf), ["UF" + H], [uln])
                affine("QC", 128, LB[:, o1 + 128:o1 + 256], uf, 1.0, -OFF, ["UF" + H], ["QC" + on1])
                if mv and MERGE < 2:
                    send(t, T.LN[:, l1 + 128:l1 + 256], LB[:, o1 + 128:o1 + 256], ["QC" + on1], ["QC" + n1])
            else:
                dma(T.yq[:, hs], uf, 65536, ["UF" + H], ["yq" + H])
            tag[0] = "f" + n
            mm(grp(T.KT[:, 1:256:2], [(ones128, IRq), (qc, I0), (Ih, rq), (Inh, rp)], 128)
               + grp(T.KT[:, 0:256:2], [(ones128, IRp), (pc, I0), (Ih, rp)], 128),
               ["ones", "IR0", "IR1", "I0", "I7", "I8", "QC" + n, "PC" + n, rqn, rpn], ["KT" + n], "KT")
            dve(256, lambda h=h: V_.tensor_tensor_scan(T.SC[:, 256 * h:256 * h + 256], T.S0[:, 256 * h:256 * h + 256], T.KT[:, 0:256], 1.0e9, A.min, A.min),
                ["KT" + n, "S0" + H], ["SC" + H], "KT")
            lend("KT")
            sc, l0 = T.SC[:, 256 * h + 31:256 * h + 256:32], 56 * h
            dve(8, ts(T.rr[:, 8 * h:8 * h + 8], sc, B * BIG, A.add, B * BIG, A.subtract), ["SC" + H], ["rr" + H])
            dve(16, tt(T.LS[:, l0 + 24:l0 + 32], sc, T.rr[:, 8 * h:8 * h + 8], A.subtract), ["SC" + H, "rr" + H], ["LS" + H])
            fs, fsn = LB[0:32, o1 + 384:o1 + 416], "FS" + on1
            f32, Wr = T.ZQ[0:32, 256 + 32 * h:288 + 32 * h], T.ZQ[:, 320 + 8 * h:328 + 8 * h]
            mm(grp(f32, [(T.LS[:, l0 + 24 - 8 * a:l0 + 56 - 8 * a], T.ID[:, a:128:4]) for a in range(4)], 32), ["LS" + H, "I0"], ["F32" + H], "ZQ")
            affine("FS", 32, fs, f32, 1.0, 0.0, ["F32" + H], [fsn], "ZQ")
            mm(grp(Wr, [(I0, d16)] + [(T.BW4[0:32, 12 - 4 * a:140 - 4 * a], LB[0:32, o1 + 384 + a:o1 + 416:4]) for a in range(4)], 64),
               [fsn, "BW4", "I0", "d16%d" % t], ["Wr" + H], "ZQ")
            dve(8, ts(fu, Wr, OFF, A.add), ["Wr" + H], ["FU" + n], "ZQ")
            dve(128 * G, tt(vo, D[t][:, 0:WX].indirect(fu), v, A.subtract), [Dn, Dn + "x", "FU" + n, "V" + n], [vn])
            if not last:
                if mv:
                    dve(8, tt(LB[:, o1 + 416:o1 + 424], Wr, d16, A.subtract), ["Wr" + H, "d16%d" % t], ["JW" + on1], "ZQ")
                    parts = ((256, 384, ["DV"]), (384, 424, ["FS", "JW"])) if MERGE == 0 else \
                        ((384 - 128 * MERGE, 424, ["QC", "DV", "FS", "JW"][2 - MERGE:]),)
                    for a, b, names in parts:
                        send(t, T.LN[:, l1 + a:l1 + b], LB[:, o1 + a:o1 + b], [x + on1 for x in names], [x + n1 for x in names], 256 * (b - a))
                else:
                    dve(8, tt(T.JF[:, 8 * s1:8 * s1 + 8], Wr, d16, A.subtract), ["Wr" + H, "d16%d" % t], ["JF" + n1], "ZQ")
            else:
                mm([(T.ZP[0:8, 384 + a:512:4], T.ID[0:32, 8 * a:8 * a + 8], fs, True, True, 32) for a in range(4)], [fsn, "I0"], ["RR" + n], "ZP")
                affine("YJ", 128, T.YJ[0:8, hs], T.ZP[0:8, 384:512], 1.0, OFF, ["RR" + n], ["YJ" + H], "ZP")
                lend("RR")
                dma(T.yj[:, hs], T.YJ[0:8, hs], 4096, ["YJ" + H], ["yj" + H])
                act(128, ac(T.V[:, c1:c1 + 128], vo, AF.Abs), [vn], ["V" + n1])
                dma(T.yv[:, hs], T.V[:, c1:c1 + 128], 32768, ["V" + n1], ["yv" + H])
    return ops


def slots(what):
    return 2 if what == "DF" else 1


def schedule(ops, deps0, succ, pr, WIN=WIN):
    n = len(ops)
    left = [len(d) for d in deps0]
    ready = {k: 0.0 for k in range(n) if left[k] == 0}
    free, done, bank, order = {}, [0.0] * n, {}, []
    held, slot = {}, {}
    while ready:
        st = {}
        for k, s in ready.items():
            o = ops[k]
            if "take" in o:
                c = [x for x in held.setdefault(o["take"][0], [0.0] * slots(o["take"][0])) if x is not None]
                if not c:
                    continue
                s = max(s, min(c))
            s = max(s, free.get(o["eng"], 0.0))
            for b in o["banks"]:
                for e, d in bank.get(b, {}).items():
                    if e != o["eng"]:
                        s = max(s, done[d] + HOPNS)
            st[k] = s
        if not st:
            return None
        k0 = min(st, key=lambda k: (st[k], -pr[k]))
        e0 = ops[k0]["eng"]
        k = max([x for x in st if ops[x]["eng"] == e0 and st[x] <= st[k0] + WIN], key=lambda x: (pr[x], -x))
        o = ops[k]
        for b in o["banks"]:
            bank.setdefault(b, {})[e0] = k
        free[e0] = st[k] + o["dur"]
        done[k] = st[k] + o["dur"] + o["lat"]
        if "take" in o:
            c = held[o["take"][0]]
            slot[k] = min([i for i, x in enumerate(c) if x is not None], key=lambda i: c[i])
            c[slot[k]] = None
        if "give" in o:
            held[ops[o["give"]]["take"][0]][slot[o["give"]]] = done[k] + HOPNS
        order.append(k)
        del ready[k]
        for x in succ[k]:
            left[x] -= 1
            if left[x] == 0:
                ready[x] = max(done[d] for d in deps0[x]) + HOPNS
    return order


def replay(r, alt):
    return sum(max(ends(r, a, [0.0] * len(a[0]), 0, 1e18)) / a[2] for a in alt)


def decode(ops, deps0, order):
    if order is None:
        return None
    deps, bank, free, slot = list(deps0), {}, {}, {}
    for k in order:
        u = ops[k]
        if u is None:
            continue
        eng, b, take, give, cls = u
        if b:
            e1, k1, k2 = bank.get(b, (eng, None, None))
            if e1 != eng:
                k2 = k1
            bank[b] = (eng, k, k2)
            if k2 is not None:
                deps[k] = deps[k] + [k2]
        if take:
            c = free.get(take)
            if c is None:
                c = free[take] = [(i, None) for i in range(slots(take))]
            if not c:
                return None
            slot[k], d = c.pop(0)
            if d is not None:
                deps[k] = deps[k] + [d]
        if give is not None:
            free[cls].append((slot[give], k))
    return order, deps, slot


def queued(r, a, done, deps0):
    o2, hop = a[:2]
    last, prev = {}, {}
    for k in r[0]:
        e = o2[k][0]
        prev[k], last[e] = last.get(e), k
    k, out = done.index(max(done)), []
    while k is not None:
        s, w = done[k] - o2[k][1] - o2[k][2] - hop - 0.01, prev[k]
        for d in r[1][k]:
            if done[d] > s:
                w = d
        if w is not None and w not in deps0[k]:
            out.append((w, k))
        k = w
    return out, prev


def refine(ops, deps0, cur, alt, MOVES, TEMP, SEED):
    n, eng = len(ops), [o[0] for o in alt[0][0]]
    dones = [ends(cur, a, [0.0] * n, 0, 1e18) for a in alt]
    vals = [max(d) / a[2] for d, a in zip(dones, alt)]
    val = sum(vals) + MEAN * sum(dones[0]) / n
    best, bval, x, edges = cur, sum(vals), SEED, None
    for it in range(MOVES):
        order = cur[0]
        if edges is None:
            edges, prev = queued(cur, alt[it % len(alt)], dones[it % len(alt)], deps0)
            pos = {k: j for j, k in enumerate(order)}
        x = (x * 1103515245 + 12345) % 2147483648
        if (x >> 24) % 8 < FREE:
            k = (x >> 8) % n
            p = prev[k]
            if p is None:
                continue
        else:
            p, k = edges[(x >> 8) % len(edges)]
        x = (x * 1103515245 + 12345) % 2147483648
        i, j, e = pos[p], pos[k], eng[k]
        hops = (x >> 10) % 4 - 1
        if (x >> 20) % 2:
            while hops > 0 and i > 0:
                i -= 1
                hops -= eng[order[i]] == e
            need, seg = {k}, order[i:j + 1]
            for y in reversed(seg):
                if y in need:
                    need.update(deps0[y])
            if order[i] in need:
                continue
            seg = [y for y in seg if y in need] + [y for y in seg if y not in need]
        else:
            while hops > 0 and j < len(order) - 1:
                j += 1
                hops -= eng[order[j]] == e
            late, seg = {p}, order[i:j + 1]
            for y in seg:
                if not late.isdisjoint(deps0[y]):
                    late.add(y)
            if order[j] in late:
                continue
            seg = [y for y in seg if y not in late] + [y for y in seg if y in late]
        r = decode(ops, deps0, order[:i] + seg + order[j + 1:])
        if r is None:
            continue
        room, new = TEMP * (1 - it / MOVES) * ((x >> 14) % 64) / 64.0, []
        for a, d, v_ in zip(alt, dones, vals):
            d = ends(r, a, d, i, (v_ + room + 400.0) * a[2])
            if d is None:
                break
            new.append(d)
        else:
            nv = [max(d) / a[2] for d, a in zip(new, alt)]
            v_ = sum(nv) + MEAN * sum(new[0]) / n
            if v_ <= val + room:
                cur, dones, vals, val, edges = r, new, nv, v_, None
                if sum(nv) < bval:
                    best, bval = r, sum(nv)
    return best


def ends(r, a, done, i, limit):
    order, deps = r[0], r[1]
    o2, hop, _, tail = a
    done, free = list(done), {}
    for j in range(i - 1, max(-1, i - 120), -1):
        k = order[j]
        if o2[k][0] not in free:
            free[o2[k][0]] = done[k] - o2[k][2]
    for j in range(i, len(order)):
        k = order[j]
        eng, dur, lat = o2[k]
        s = free.get(eng, 0.0) - hop
        for d in deps[k]:
            if done[d] > s:
                s = done[d]
        s += hop + dur
        free[eng] = s
        done[k] = s + lat
        if s + tail[k] > limit:
            return None
    return done


PLANS = {}


def plan(ops, others=()):
    n = len(ops)
    if n not in PLANS:
        wr, rd, deps = {}, {}, []
        for k, o in enumerate(ops):
            d = set(wr[x] for x in o["r"] + o["w"] if x in wr)
            for x in o["w"]:
                d.update(rd.get(x, ()))
            for x in o["r"]:
                rd.setdefault(x, []).append(k)
            for x in o["w"]:
                wr[x] = k
                rd[x] = []
            deps.append(sorted(d))
        anc = [0] * n
        for k in range(n):
            via = 0
            for d in deps[k]:
                via |= anc[d]
            anc[k] = via | sum(1 << d for d in deps[k])
            deps[k] = [d for d in deps[k] if not via >> d & 1]
        use = [(o["eng"], o["banks"] and o["banks"][0], o.get("take", [None])[0], o.get("give"), ops[o.get("give", k)].get("take", [None])[0])
               if o["banks"] or "take" in o or "give" in o else None for k, o in enumerate(ops)]
        succ = [[] for _ in range(n)]
        for k in range(n):
            for d in deps[k]:
                succ[d].append(k)
        pr = [0.0] * n
        for k in range(n - 1, -1, -1):
            pr[k] = ops[k]["dur"] + ops[k]["lat"] + max([pr[x] + HOPNS for x in succ[k]] + [0.0])
        pr = [pr[k] - k * MIX for k in range(n)]
        best = decode(use, deps, schedule(ops, deps, succ, pr))
        alt = []
        for o2, p in zip([ops] + list(others), PARS):
            tail = [0.0] * n
            for k in range(n - 1, -1, -1):
                tail[k] = o2[k]["lat"] + max([tail[x] + o2[x]["dur"] + p[3] for x in succ[k]] + [0.0])
            alt.append(([(o["eng"], o["dur"], o["lat"]) for o in o2], p[3], p[0] * (1 + p[1] / 4), tail))
        val = replay(best, alt)
        sets = {}
        for k, o in enumerate(ops):
            sets.setdefault(o["eng"] + o["w"][0].rstrip("0123456789"), []).append(k)
            sets.setdefault("#" + o["tag"], []).append(k)
        sets = [sets[c] for c in sorted(sets)]
        x = SEED
        for it in range(ITER):
            q = list(pr)
            for _ in range(2):
                x = (x * 1103515245 + 12345) % 2147483648
                c = (x >> 8) % len(sets)
                x = (x * 1103515245 + 12345) % 2147483648
                a = ((x >> 8) % 2001 - 1000) * AMP
                for k in sets[c]:
                    q[k] += a
            r = decode(use, deps, schedule(ops, deps, succ, q))
            if r is None:
                continue
            v_ = replay(r, alt)
            if v_ <= val:
                best, pr, val = r, q, v_
        for rnd in range(ROUNDS):
            best = refine(use, deps, best, alt, MOVES, TEMP * (1 - rnd / ROUNDS), SEED + rnd)
            kept = min(kept, best, key=lambda r: replay(r, alt)) if rnd else best
            done = ends(best, alt[0], [0.0] * n, 0, 1e18)
            start = [ops[k]["dur"] + ops[k]["lat"] - done[k] for k in range(n)]
            for win in (0.0, 200.0, 500.0, 1000.0):
                r = decode(use, deps, schedule(ops, deps, succ, start, win))
                if r is not None and replay(r, alt) < replay(best, alt) + (SLACK if rnd < ROUNDS - 1 else 0.0):
                    best = r
                    break
        order, deps, slot = min(kept, best, key=lambda r: replay(r, alt))
        PLANS[n] = (list(range(LOADS)) + [k for k in order if k >= LOADS], deps, slot)
    order, deps, slot = PLANS[n]
    for j, k in enumerate(order):
        ops[k]["t0"] = j
    for k, i in slot.items():
        ops[k]["take"][1][0] = i
    return order, deps, 0.0


def rank_program(g, core, T, topo):
    rank = T.rank_of(core)
    if rank is None:
        return
    dests = {}
    for t, hop in enumerate(HOP):
        if hop:
            dst = T.cores[(rank + hop) % len(T.cores)]
            rid, pid, _ = topo.addr(dst)
            dests[t] = (rid, pid, topo.mask(core, dst), len(topo.engines(core, dst)))
    ops = program(g, T, dests)
    order, deps, _ = plan(ops, [program(g, T, dests, p) for p in PARS[1:]])
    queue = {"pe": g.tensor, "dve": g.vector, "act": g.scalar, "pool": g, "sp": g.sync}
    count, mark, known, place, waited, sent = {}, {}, {}, {}, {}, 0
    seen = {e: {} for e in queue}
    for k in order:
        o = ops[k]
        e = o["eng"]
        for d in sorted(set(deps[k]), key=lambda d: -ops[d]["t0"]):
            sem, val = mark[d]
            if not (sem == "pe" and e == "pe") and seen[e].get(sem, 0) < val:
                queue[e].wait_ge(T.sem[sem], val)
                seen[e][sem] = val
                waited[sem] = max(waited.get(sem, 0), val)
                for s_, v_ in known[d].items():
                    if seen[e].get(s_, 0) < v_:
                        seen[e][s_] = v_
        known[k] = dict(seen[e]) if o["sem"] is None or o["sem"][0] == "m" else {}
        ins = o["fn"]()
        if o["sem"] is None:
            count[e] = count.get(e, 0) + 1
            ins.then_inc(T.sem[e], 1)
            mark[k] = (e, count[e])
        else:
            if o["sem"][0] == "m":
                ins.then_inc(T.sem[o["sem"]], 16)
            else:
                sent += o["cnt"]
            count[o["sem"]] = o["cnt"]
            mark[k] = (o["sem"], o["cnt"])
        place[mark[k][0]] = o["t0"]
    g.wait_ge(T.sem.sent, sent)
    for sem in sorted(count, key=lambda s_: place[s_]):
        if waited.get(sem, 0) < count[sem]:
            g.wait_ge(T.sem[sem], count[sem])
